import numpy as np, ml_dtypes
CORES = [13,21,141,149]
N = 4
BF = ml_dtypes.bfloat16
def gentries(a):
    return np.ascontiguousarray(a.reshape(8, 16, -1).transpose(0, 2, 1)).reshape(8, -1)
def gtable(e):
    e = np.asarray(e); return np.ascontiguousarray(e.reshape(8, -1, 16).transpose(0, 2, 1)).reshape(128, -1).astype(np.int32)
V, S, L, M, C, A, B = 1328, 1024, 3, 4, 64, 8, 12
W = V + C * M
def parts(rng):
    c = rng.integers(0, 16, (N, 8, 12, V)); o = np.argsort(rng.random((N, 8, 1, V)), axis=-1)
    i = np.minimum((V * rng.random((N, 8, 2, V)) ** 1.5).astype(np.int64), V - 1)
    t = np.take_along_axis(np.broadcast_to(o, (N, 8, 2, V)), i, 3)
    t = np.where(rng.random(t.shape) < 0.04, np.arange(V), t)
    n = np.exp2(9 * rng.random((N, 8, 2, V))).astype(np.int64) - 1
    s = rng.integers(0, V, (N, 8, S)); x = rng.integers(0, 16, (N, 8, 12, S))
    e = np.where(np.argsort(rng.random((N, 8, 12)), axis=-1) % 2 == 1, 1, -1)
    return c, t, n, s, x, e
def pack(c, t, n, s, x, e):
    return {"recs": np.concatenate([c, t, n], axis=2).reshape(N, 128, V).astype(np.int32), "st0": np.stack([gtable(a) for a in s]),
            "cx0": np.concatenate([x, np.zeros((N, 8, 4, S), np.int64)], axis=2).reshape(N, 128, S).astype(np.float32).astype(BF),
            "sg": np.concatenate([e, np.zeros((N, 8, 4), np.int64)], axis=2).reshape(N, 128, 1).astype(np.int32)}
def setup_inputs(rng):
    return pack(*parts(rng))
def setup_inputs_full(rng):
    c, t, n, s, x, e = parts(rng); n = rng.integers(400, 501, n.shape); h = V // M
    for g in range(8):
        base = rng.permutation(V)
        for r in range(N):
            for m in range(M):
                blk = rng.permutation(base[m * h:(m + 1) * h])
                t[r, g][:, blk] = np.roll(blk, -1)
                s[r, g, m * C:(m + 1) * C] = blk[:C] if g % 2 == 0 else rng.permutation(blk)[:C]
    return pack(c, t, n, s, x, e)
def setup_inputs_meet(rng):
    c, t, n, s, x, e = parts(rng); n = n // 4 + 60
    hub = np.stack([rng.permutation(V)[:24] for g in range(8)])
    t = np.where(rng.random(t.shape) < 0.85, hub[np.arange(8)[None, :, None, None], rng.integers(0, 24, t.shape)], t)
    for r in range(N):
        for g in range(8): t[r, g][:, hub[g, :6]] = hub[g, :6]
    s[:, 0] = s[:, 0, :1].copy(); x[:, 0] = x[:, 0, :, :1].copy(); t[:, 1] = np.arange(V)
    for r in range(N):
        o = rng.permutation(V); h = o[L * C]
        t[r, 4][:, o[:(L - 1) * C]] = o[C:L * C]; t[r, 4][:, o[(L - 1) * C:L * C]] = h
        n[r, 4][:, h] = rng.integers(400, 501, 2); s[r, 4, :C] = rng.permutation(o[:C])
    return pack(c, t, n, s, x, e)
def setup_inputs_ties(rng):
    c, t, n, s, x, e = parts(rng); c[:, ::2] = c[:, ::2] & 1; x[:, ::2] = x[:, ::2] & 1
    a = A - 2 + rng.integers(0, 4, (N, 8, V)); b = A - 2 + rng.integers(0, 4, (N, 8, V))
    b = np.where(rng.random((N, 8, V)) < 0.6, A + B - a + rng.integers(-3, 4, (N, 8, V)), b)
    turn = rng.random((N, 8, V)) < 0.5
    n = np.stack([np.where(turn, b, a), np.where(turn, a, b)], axis=2)
    o = np.argsort(rng.random((N, 8, 1, V)), axis=-1)[..., :3 * C]
    t = np.take_along_axis(np.broadcast_to(o, (N, 8, 2, 3 * C)), rng.integers(0, 3 * C, t.shape), 3)
    return pack(c, t, n, s, x, e)
def setup_inputs_ahead(rng):
    c, t, n, s, x, e = parts(rng); n = rng.integers(300, 401, n.shape); n[1::2] = 0
    t[:, 2] = np.where(rng.random((N, 2, V)) < 0.5, (V - 1) * rng.integers(0, 2, (N, 2, V)), t[:, 2])
    s[:, 3] = (V - 1) * rng.integers(0, 2, (N, S))
    return pack(c, t, n, s, x, e)
def setup_inputs_spread(rng):
    c, t, n, s, x, e = parts(rng)
    c = np.minimum((np.exp2(4 * rng.random((N, 8, 1, V))) * rng.random((N, 8, 12, V))).astype(np.int64), 15); c[rng.random(c.shape) < 0.02] = 15
    x = np.minimum((np.exp2(4 * rng.random((N, 8, 1, S))) * rng.random((N, 8, 12, S))).astype(np.int64), 15)
    t = np.minimum((V * rng.random(t.shape) ** np.exp2(rng.integers(-1, 3, (N, 8, 1, 1)))).astype(np.int64), V - 1)
    n = np.minimum(np.exp2(12 * rng.random(n.shape)).astype(np.int64), 4095); n[rng.random(n.shape) < 0.1] = 0; n[rng.random(n.shape) < 0.01] = 4095
    e = np.where(rng.random(e.shape) < 0.5, 1, -1); e[:, 1] = 1; e[:, 6] = -1
    for g, a in ((2, 1), (5, -1)): e[:, g] = np.where(np.argsort(rng.random((N, 12)), axis=-1) < 10, a, -a)
    for g in (1, 2, 5, 6):
        c[:, g] = np.where(rng.random((N, 1, V)) < 0.5, rng.integers(14, 16, (N, 12, V)), c[:, g])
        x[:, g] = np.where(rng.random((N, 1, S)) < 0.5, rng.integers(14, 16, (N, 12, S)), x[:, g])
    n[:, 3] = rng.integers(4000, 4096, (N, 2, V))
    return pack(c, t, n, s, x, e)
def check_inputs(d):
    bad = []
    a = np.asarray(d["recs"]).reshape(-1, 8, 16, V)
    for k, i, j, hi in (("statistics", 0, 12, 15), ("transitions", 12, 14, V - 1), ("counts", 14, 16, 4095)):
        if np.min(a[:, :, i:j]) < 0 or np.max(a[:, :, i:j]) > hi: bad.append("range of the " + k)
    if np.min(d["st0"]) < 0 or np.max(d["st0"]) > V - 1: bad.append("range of st0")
    x = np.asarray(d["cx0"]).astype(np.float32).reshape(-1, 8, 16, S)
    if not np.all((x >= 0) & (x <= 15) & (x == np.floor(x))): bad.append("cx0 holds whole numbers from 0 to 15")
    if np.any(x[:, :, 12:] != 0): bad.append("rows of 0 of cx0")
    e = np.asarray(d["sg"]).reshape(-1, 8, 16)
    if not np.all(np.abs(e[:, :, :12]) == 1): bad.append("sg holds 1 and -1")
    if np.any(e[:, :, 12:] != 0): bad.append("rows of 0 of sg")
    return bad
def reference(recs, st0, cx0, sg):
    p = np.zeros((N, 8, 16, W), np.int64); p[..., :V] = recs.astype(np.int64).reshape(N, 8, 16, V)
    s = np.stack([gentries(a) for a in st0]).astype(np.int64)
    x = cx0.astype(np.float32).astype(np.int64).reshape(N, 8, 16, S)[:, :, :12].copy()
    e = sg.astype(np.int64).reshape(N, 8, 16, 1)[:, :, :12]
    free = np.full((N, 8), V, np.int64)
    for v in range(M):
        for q in range(N):
            r = (q - v) % N
            for step in range(L):
                rec = np.take_along_axis(p[q], s[r][:, None, :], 2)
                b = (np.sum(e[q] * rec[:, :12] * x[r], axis=1) > 0).astype(np.int64)
                x[r] = (x[r] + rec[:, :12]) >> 1
                old = s[r].copy(); s[r] = np.where(b == 1, rec[:, 13], rec[:, 12])
            lo = C * v
            for g in range(8):
                pg = p[q, g]; so = old[g, lo:lo + C]; bo = b[g, lo:lo + C]; sn = s[r, g, lo:lo + C].copy()
                w = np.sort(np.unique(so, return_index=True)[1])
                pg[14 + bo[w], so[w]] += 1
                w = w[np.sort(np.unique(sn[w], return_index=True)[1])]
                n = pg[14 + bo[w], so[w]]
                ok = (sn[w] != so[w]) & (n >= A) & (pg[14, sn[w]] + pg[15, sn[w]] - n >= B)
                w = w[ok]; k = len(w); new = free[q, g] + np.arange(k)
                t = pg[:, sn[w]]
                pg[:12, new] = (t[:12] + x[r, g][:, lo + w]) >> 1
                pg[12:14, new] = t[12:14]
                pg[14:16, new] = t[14:16] >> 1
                pg[14:16, sn[w]] = t[14:16] - (t[14:16] >> 1)
                pg[12 + bo[w], so[w]] = new
                s[r, g, lo + w] = new; free[q, g] += k
    yx = np.zeros((N, 8, 16, S), np.float32); yx[:, :, :12] = x
    return {"yp": p.reshape(N, 128, W).astype(np.float32), "ys": np.stack([gtable(a) for a in s]).astype(np.float32), "yx": yx.reshape(N, 128, S).astype(BF)}

@@ -1,0 +1,659 @@
+import math
+from concourse.bass import DstId, RemoteDMATransfer
+from concourse.mybir import AluOpType, ActivationFunctionType
+
+OP = AluOpType
+AF = ActivationFunctionType
+V0, W0, WD = 1328, 1584, 1712
+MAGIC = 12582912.0
+KV = 4096.0
+OPT = {"na": 320, "a": "AV", "c": "V", "b": "G", "gt": "v", "iters": 5000, "seed": 1}
+MODEL = {"cyc": 1.04, "pe": 0.62, "g": 1.56, "s": 3.5, "h": 130.0, "hs": 110.0, "hop": 5000.0, "fix": 30.0}
+MODELS = [MODEL, dict(MODEL, pe=0.52, h=60.0, hs=60.0, g=1.2, hop=4000.0),
+          dict(MODEL, pe=0.9, h=200.0, hs=200.0, g=1.9, hop=6500.0)]
+
+SCRATCH = {}
+
+
+def _buf(dtype, cols, names):
+    for n in names.split():
+        SCRATCH[n] = ("sbuf", [128, cols], dtype)
+
+
+_buf("int32", V0, "raw")
+_buf("int32", 64, "sti")
+_buf("int32", 8, "sgi coli")
+_buf("float32", WD, "mp0 mp1 mp2 mp3 mp4 cn")
+_buf("float32", 48, "soa soc sfa sfc")
+_buf("float32", 32, "col")
+_buf("float32", 64, "ihp ihn mof32 c0 zer bb zz nxm k1 k2 gsc gsm sel ns gt ht clo cl2 ncm d0 d1 cd ee vn")
+_buf("float32", 128, "i32 i32n wh wn wc cl k0 vc vv")
+_buf("float32", 384, "rra rrb rrc")
+_buf("bfloat16", 32, "w24")
+_buf("bfloat16", 64, "jm moff hh sgn")
+_buf("bfloat16", 128, "jd bd wv wt0 wdl we ib ibn wx ik")
+_buf("bfloat16", 256, "j64 ra ras tri1 tri2 hb yb xb0 xb1 xb2 xb3")
+_buf("bfloat16", 512, "zb selb lc")
+_buf("bfloat16", 640, "ha hc ya yc xa0 xa1 xa2 xa3 xa4 xc0 xc1 xc2 xc3 xc4")
+_buf("float16", 640, "pa pb pc")
+_buf("float16", 64, "ph sw tw ng")
+_buf("float16", 320, "eq eq2")
+_buf("uint16", 8, "l1 l2 l3 lsd ltd")
+_buf("uint16", 48, "sa0 sa1 sa2 sa3 sb0 sb1 sb2 sb3 sc0 sc1 sc2 sc3")
+for _b in range(8):
+    SCRATCH["ps%d" % _b] = ("psum", [128, 512], "float32")
+
+SEMAPHORES = ["cv", "ca", "cp", "cg", "sent"] + ["m%d" % i for i in range(24)] + ["d%d" % i for i in range(48)]
+BYTES = {"float32": 4, "int32": 4, "float16": 2, "bfloat16": 2, "uint16": 2}
+IO = ("recs", "st0", "cx0", "sg", "yp", "ys", "yx")
+
+
+def A(name, c0, c1, st=1, p0=0, p1=128):
+    return ("ap", name, p0, p1, 1, c0, c1, st)
+
+
+def C(k):
+    return A("col", k, k + 1)
+
+
+def IND(win, off):
+    return ("ind", win, off)
+
+
+def ncols(a):
+    if a[0] == "ind":
+        return 16 * ncols(a[2])
+    return len(range(a[5], a[6], a[7]))
+
+
+def isz(a):
+    if a[0] == "ind":
+        a = a[1]
+    return 4 if a[1] in IO else BYTES[SCRATCH[a[1]][2]]
+
+
+def inps(a):
+    return a[0] == "ap" and a[1].startswith("ps")
+
+
+def cost(op, m):
+    k, a = op["k"], op["a"]
+    if k == "mm":
+        t = 0.0
+        for (out, l, r, st, sp) in a:
+            t += max(min(64, ncols(l)), ncols(r)) * (4 if isz(l) == 4 else 1) * m["pe"] + 5
+        return t + m["fix"]
+    if k in ("iota", "sel"):
+        return 250 + 2 * ncols(a[0]) * m["cyc"]
+    if k == "dma":
+        return 60.0
+    if k == "send":
+        return 700.0
+    out, i0 = a[0], (a[1] if k != "ms" else a[0])
+    n = ncols(out)
+    if out[0] == "ind":
+        return 50 + n * m["s"] * m["cyc"]
+    if i0[0] == "ind":
+        return 60 + n * m["g"] * m["cyc"]
+    f = 1.0
+    if k == "tt":
+        f = 1.0 if (inps(a[1]) or inps(a[2])) else 2.0
+    elif k in ("ts", "cp", "ms") and isz(out) == 2 and isz(i0) == 2:
+        f = 0.5
+    return max(64, n * f) * m["cyc"] + m["fix"]
+
+
+def latency(op, m):
+    if op["k"] == "dma":
+        return 1800 + op["load"] / 180.0
+    if op["k"] == "send":
+        o = op["a"][0]
+        return m["hop"] + 128 * ncols(o) * isz(o) / 100.0
+    return 0.0
+
+
+def regions(op):
+    k, a = op["k"], op["a"]
+    rd, wr = [], []
+
+    def add(x, lst):
+        if isinstance(x, tuple) and len(x) > 0 and x[0] == "ind":
+            lst.append(x[1])
+            rd.append(x[2])
+        elif isinstance(x, tuple) and len(x) > 0 and x[0] == "ap":
+            lst.append(x)
+    if k == "mm":
+        for (out, l, r, st, sp) in a:
+            add(out, wr)
+            add(l, rd)
+            add(r, rd)
+    elif k == "send":
+        add(a[1], rd)
+        wr.append(A(a[0][1], 0, SCRATCH[a[0][1]][1][1]))
+    else:
+        add(a[0], wr)
+        for x in a[1:]:
+            add(x, rd)
+    return rd, wr
+
+
+def build():
+    ops = []
+    NA, NB = OPT["na"], 256
+    NC = 1024 - NA - NB
+
+    def put(q, k, *a):
+        ops.append({"q": q, "k": k, "a": a})
+    ts = lambda out, i, s1, s2, o0, o1=None: put("v", "ts", out, i, s1, s2, o0, o1)
+    tt = lambda out, i, j, o: put("v", "tt", out, i, j, o)
+    cp = lambda out, i: put("v", "cp", out, i)
+    scan = lambda out, d0, d1, init, o0, o1: put("v", "scan", out, d0, d1, init, o0, o1)
+    act = lambda out, i, f, bias, scale: put("a", "act", out, i, f, bias, scale)
+    lin = lambda out, i, scale, bias=0.0: act(out, i, AF.Identity, bias, scale)
+    mm = lambda lst: put("p", "mm", *lst)
+    full = lambda n: A(n, 0, SCRATCH[n][1][1])
+    half = lambda n, h, c=None: A(n, 0, c or SCRATCH[n][1][1], 1, 64 * h, 64 * h + 64)
+    pick = lambda out, pat, cmp, fill, base, cm: put("g", "sel", out, A("zb", 0, ncols(out), 1, out[2], out[3]), pat, cmp,
+                                                     fill, base, cm)
+    MP, CN, IB = [A("mp%d" % v, 0, W0) for v in range(5)], A("cn", 0, W0), full("ib")
+    load = [0]
+
+    def dma(q, out, i):
+        put(q, "dma", out, i)
+        load[0] += (out[3] - out[2]) * ncols(out) * (2 if out[1][0] == "x" or out[1] == "yx" else 4)
+        ops[-1]["load"] = load[0]
+
+    hv = V0 // 4
+    dma("s", A("sgi", 0, 1), A("sg", 0, 1))
+    dma("a", full("sti"), A("st0", 0, 64))
+    for k in range(4):
+        dma("sa"[k % 2], A("raw", hv * k, hv * k + hv), A("recs", hv * k, hv * k + hv))
+        if k == 1:
+            dma("s", A("xb0", 0, NB), A("cx0", 0, NB))
+    dma("a", A("xa0", 0, NA), A("cx0", NB + NC, 1024))
+    dma("s", A("xc0", 0, NC), A("cx0", NB, NB + NC))
+    put("v", "ms", full("zb"), 0.0)
+    put("g", "iota", A("coli", 0, 1), [[0, 1]], 0, 1)
+    put("g", "iota", full("jd"), [[1, 8], [0, 16]], 0, 0)
+    put("g", "iota", full("jm"), [[0, 4], [1, 16]], 0, 0)
+    pick(IB, [[-1, 128]], OP.not_equal, 1.0, 0, 1)
+    put("g", "iota", full("j64"), [[1, 4], [0, 64]], 0, 0)
+    for h in range(2):
+        pick(half("tri1", h), [[0, 4], [1, 64]], OP.is_gt, 4096.0, 0, -1)
+        pick(half("ra", h), [[-16, 4], [0, 64]], OP.not_equal, 1.0, 0, 1)
+        pick(half("lc", h), [[-1, 4], [1, 8], [0, 16]], OP.not_equal, 1.0, -4 * h, 0)
+    pick(full("selb"), [[-16, 4], [-64, 2], [0, 64]], OP.not_equal, -1.0, 0, 1)
+    ci = lambda k: A("coli", k, k + 1)
+    ts(ci(1), ci(0), 15, None, OP.bitwise_and)
+    ts(ci(2), ci(0), 4, None, OP.arith_shift_right)
+    ts(ci(3), ci(0), 1, None, OP.bitwise_and)
+    ts(ci(4), ci(0), 4, 3, OP.arith_shift_right, OP.bitwise_and)
+    cp(A("col", 0, 5), A("coli", 0, 5))
+    cp(C(5), A("sgi", 0, 1))
+    ts(A("col", 6, 8), A("jm", 12, 14), C(1), None, OP.is_equal)
+    ts(C(8), C(1), 12.0, None, OP.is_lt)
+    ts(C(9), C(1), 14.0, None, OP.is_ge)
+    ts(full("bd"), full("jd"), C(2), None, OP.is_equal)
+    ts(full("moff"), full("jm"), C(1), 4096.0, OP.not_equal, OP.mult)
+    ts(full("c0"), full("jm"), 0.0, 2000.0, OP.is_equal, OP.mult)
+    ts(full("ras"), full("j64"), C(4), 2048.0, OP.is_equal, OP.mult)
+    lin(C(10), C(6), 1.0, C(7))
+    lin(C(11), C(6), -1.0, C(7))
+    lin(C(12), C(5), KV)
+    lin(C(13), C(5), KV, C(11))
+    lin(C(14), C(8), 0.5)
+    lin(C(15), C(8), -0.25)
+    lin(C(16), C(8), -0.25, C(10))
+    lin(C(17), C(8), 0.5, C(10))
+    lin(C(18), C(10), 0.25, -0.25)
+    lin(C(19), C(10), -1.0)
+    lin(C(20), C(9), 0.5)
+    lin(C(21), C(9), -1.0)
+    lin(C(23), C(5), -1.0)
+    lin(C(24), C(3), -1.0, 0.5)
+    lin(C(25), C(8), -1.0e6, C(24))
+    lin(C(26), C(1), 1.0, float(W0))
+    lin(C(27), C(1), 0.0, float(V0 - 1))
+    lin(C(29), C(16), 1.0, 128.0)
+    bd8 = A("bd", 0, 128, 16)
+    for s, c in enumerate((19, 13, 12)):
+        lin(A("w24", 8 * s, 8 * s + 8), bd8, C(c))
+    for n, c in (("wv", 5), ("wt0", 6), ("wdl", 11), ("wc", 9)):
+        lin(full(n), full("bd"), C(c))
+    for n, c in (("wx", C(14)), ("i32", 1.0), ("ik", 16384.0), ("i32n", -1.0), ("ibn", -1.0), ("wh", C(20)), ("wn", C(21))):
+        lin(full(n), IB, c)
+    lin(full("ihp"), A("ib", 0, 64), 0.5)
+    lin(full("ihn"), A("ib", 0, 64), -0.5)
+    lin(full("mof32"), full("moff"), 1.0)
+    lin(full("tri2"), full("tri1"), 1.0, -30720.0)
+    lin(A("mp0", V0, W0), A("zb", 0, W0 - V0), 1.0)
+    for k in range(4):
+        lin(A("cn", 396 * k, 396 * k + 396), A("zb", 0, 396), 1.0)
+    lin(full("zer"), A("zb", 0, 64), 1.0)
+    lin(full("we"), A("zb", 0, 128), 1.0)
+    for k in range(12, 16):
+        lin(A("we", k, 128, 16), bd8, C(23 if k % 2 else 5))
+    lin(full("cl"), A("zb", 0, 128), 1.0)
+    lin(A("cl", 0, 128, 16), A("jd", 0, 128, 16), 16.0, C(26))
+    for k in range(4):
+        cp(A("mp0", hv * k, hv * k + hv), A("raw", hv * k, hv * k + hv))
+    load[0] = 0
+    for g in range(8):
+        dma("s", A("cn", 0, V0, 1, 16 * g + 14, 16 * g + 16), A("mp0", 0, V0, 1, 16 * g + 14, 16 * g + 16))
+    cp(A("sb0", 0, NB // 16), A("sti", 0, NB // 16))
+    cp(A("sc0", 0, NC // 16), A("sti", NB // 16, (NB + NC) // 16))
+    cp(A("sa0", 0, NA // 16), A("sti", (NB + NC) // 16, 64))
+    for (n, i, j) in (("xb0", 0, 64), ("xb0", 64, NB), ("xa0", 0, NA), ("xc0", 0, NC)):
+        lin(A(n, i, j), A(n, i, j), 1.0, C(10))
+
+    def xstep(win, X, XO, H, Y, off, n, bank, last, mode):
+        if mode == "G":
+            def both():
+                tt(A(H, 0, n), IND(win, off), X, OP.add)
+                lin(A(Y, 0, n), A(H, 0, n), C(14), C(29))
+                lin(XO, A(Y, 0, n), 1.0, -128.0)
+            return [], [], both
+        lin(A(H, 0, n), IND(win, off), C(14), C(15 if last else 16))
+        o = A(bank[0], bank[1], bank[1] + n)
+
+        def rnd():
+            if mode == "V":
+                ts(XO, o, MAGIC, MAGIC, OP.add, OP.subtract)
+            else:
+                lin(A(Y, 0, n), o, 1.0, 128.0)
+                ts(XO, A(Y, 0, n), -128.0, None, OP.add)
+        return [(o, full("wx"), X, True, False)], [(o, IB, A(H, 0, n), False, True)], rnd
+
+    def bulk_step(c, v, step):
+        n = {"a": NA + 64 * v, "b": NB - 64 - 64 * v, "c": NC}[c]
+        o = 64 if c == "b" else 0
+        m = n // 16
+        X = A("x%s%d" % (c, v), o, o + n)
+        S = A("s%s%d" % (c, v), o // 16, o // 16 + m)
+        last = v == 3 and step == 2
+        bs, bx = {"a": ("ps0", "ps2"), "c": ("ps1", "ps3"), "b": ("ps4", None)}[c]
+        P, R = "p" + c, "rr" + c
+        m1, m2, rnd = xstep(MP[v], X, X, "h" + c, "y" + c, S, n, (bx, 0), last, OPT[c])
+        if m1:
+            mm(m1)
+        tt(A(P, 0, n), IND(MP[v], S), X, OP.mult)
+        if not m1:
+            rnd()
+        mm([(A(bs, k, 384, 16, 0, m), A(P, k, n, 16), A("w24", 0, 24), True, True) for k in range(16)])
+        act(A(R, 0, 384, 1, 0, m), A(bs, 0, 384, 1, 0, m), AF.Abs, -2048.0, 1.0)
+        if m2:
+            mm(m2)
+        o3 = A(bs, 384, 384 + m)
+        mm([(o3, A(R, 128 * s, 128 * s + 128, 1, 0, m), A("ihn" if s == 2 else "ihp", 0, m, 1, 0, m), s == 0, s == 2)
+            for s in range(3)])
+        ts(A("so" + c, o // 16, o // 16 + m) if last else S, o3, -1024.0, None, OP.add)
+        if m1:
+            rnd()
+
+    def head_step(v, step):
+        X = A("xb%d" % v, 0, 64)
+        na = NA + 64 * v
+        XO = A("xa%d" % v, na, na + 64) if step == 2 else X
+        S = (A("sb%d" % v, 0, 4), A("l1", 0, 4), A("l2", 0, 4))[step]
+        m1, m2, rnd = xstep(MP[v], X, XO, "hh", None, S, 64, ("ps5", 256), v == 3 and step == 2, "V")
+        P = full("ph")
+        tt(P, IND(MP[v], S), X, OP.mult)
+        r = lambda k: A("ps5", 64 * k, 64 * k + 64)
+        lst = [(r(2), IB, full("moff"), True, False), (r(2), full("wt0"), P, False, True),
+               (r(0), full("wv"), P, True, True), (r(1), full("wdl"), P, True, True)]
+        if step > 0:
+            lst.append((r(3), full("wt0"), P, True, True))
+        mm(lst)
+        ts(full("bb"), r(0), 0.0, None, OP.is_gt)
+        tt(full("zz"), full("bb"), r(1), OP.mult)
+        tt(full("nxm"), full("zz"), r(2), OP.add)
+        if step > 0:
+            tt(full("sw" if step == 1 else "tw"), full("zz"), r(3), OP.add)
+        mm(m1 + m2)
+        scan(A("k0", 0, 64), full("c0"), full("nxm"), 0.0, OP.max, OP.min)
+        cp(A("l%d" % (step + 1), 0, 4), A("k0", 15, 64, 16))
+        rnd()
+
+    D, DF = A("ps6", 0, 256), A("ps6", 256, 320)
+
+    def pairs(w):
+        lst = [(half("ps6", h, 256), half(w, h), half("ra", h), False, False) for h in range(2)]
+        return lst + [(A("ps6", 64 * k, 64 * k + 64), A("selb", 128 * k, 128 * k + 128), full(w), False, k == 3)
+                      for k in range(4)]
+
+    def counts(out, e, start, stop):
+        return [(out, A("lc", 128 * k, 128 * k + 128), A(e, 64 * k, 64 * k + 64), start and k == 0, stop and k == 3)
+                for k in range(4)]
+
+    def stage1(v):
+        mm([(D, IB, full("tri1"), True, False)] + pairs("sw"))
+        ts(A("eq", 0, 256), D, 0.0, 4096.0, OP.is_equal, OP.mult)
+        sd = A("ps6", 320, 384)
+        mm([(sd, IB, full("moff"), True, False), (sd, IB, full("sw"), False, False)] + counts(sd, "eq", False, True))
+        ts(full("ng"), sd, 2000.0, None, OP.is_gt)
+        scan(full("k1"), A("cl", 0, 64), sd, 0.0, OP.max, OP.min)
+        cp(A("lsd", 0, 4), A("k1", 15, 64, 16))
+        mm([(D, IB, full("tri2"), True, False)]
+           + [(half("ps6", h, 256), half("ng", h), half("ras", h), False, False) for h in range(2)])
+        lin(full("gsc"), IND(CN, A("l2", 0, 4)), 1.0)
+        act(full("sgn"), full("gsc"), AF.Sign, -6.5, 1.0)
+        lin(full("gsm"), IND(MP[v], A("l2", 0, 4)), 1.0)
+        pg = A("ps7", 128, 192)
+        mm([(pg, full("i32n"), full("gsc"), True, False), (pg, full("ik"), full("sgn"), False, True)])
+
+    def train(v):
+        na = NA + 64 * v
+        e, q = A("ps7", 0, 64), A("ps7", 64, 128)
+        mm(counts(e, "eq", True, False) + [(e, full("we"), full("ph"), False, True)])
+        ts(full("sel"), e, C(25), None, OP.is_lt)
+        tt(IND(full("cn"), A("lsd", 0, 4)), full("gsc"), full("sel"), OP.add)
+        tt(full("ns"), full("sel"), A("ps7", 128, 192), OP.mult)
+        mm(pairs("tw") + [(DF, IB, full("tw"), True, False), (DF, full("ibn"), full("sw"), False, True)])
+        ts(full("eq2"), A("ps6", 0, 320), 0.0, -32768.0, OP.is_equal, OP.mult)
+        mm([(q, full("wc"), full("ns"), True, False)])
+        if OPT["gt"] == "v":
+            cp(full("gt"), IND(CN, A("l3", 0, 4)))
+        else:
+            lin(full("gt"), IND(CN, A("l3", 0, 4)), 1.0)
+        mm([(q, full("wt0"), A("eq2", 256, 320), False, False)] + counts(q, "eq2", False, False)
+           + [(q, full("wc"), full("gt"), False, True)])
+        lin(full("ht"), IND(MP[v], A("l3", 0, 4)), C(17), C(18))
+        ts(full("clo"), q, 16384.0 + 13, None, OP.is_ge)
+        ts(full("cl2"), q, 16384.0 + 13, 4096.0, OP.is_lt, OP.mult)
+        vt, vd = A("ps7", 192, 256), A("ps7", 256, 320)
+        mm([(vd, full("i32"), full("ht"), True, False), (vd, full("wx"), A("xa%d" % v, na, na + 64), False, False),
+            (vd, full("wh"), full("gt"), False, True),
+            (vt, full("wn"), full("ht"), True, False), (vt, full("wh"), full("gt"), False, True)])
+        dn = "d%d" % (v % 2)
+        scan(full(dn), full("clo"), full("zer"), C(27) if v == 0 else A("d%d" % (1 - v % 2), 63, 64), OP.add, OP.add)
+        tt(full("ncm"), full("cl2"), full("mof32"), OP.add)
+        tt(A("vv", 64, 128), full(dn), full("ncm"), OP.add)
+        tt(A("vv", 0, 64), full("nxm"), full("cl2"), OP.add)
+        tt(full("cd"), full("clo"), full(dn), OP.mult)
+        scan(full("k0"), full("cl"), full("vv"), 0.0, OP.max, OP.min)
+        tt(full("ee"), full("cd"), full("sel"), OP.mult)
+        cp(full("ltd"), A("k0", 15, 128, 16))
+        ts(full("vc"), A("ps7", 192, 320), MAGIC, MAGIC, OP.add, OP.subtract)
+        tt(full("vn"), full("nxm"), full("cd"), OP.max)
+        scan(full("k2"), full("c0"), full("vn"), 0.0, OP.max, OP.min)
+        cp(A("soa" if v == 3 else "sa%d" % v, na // 16, na // 16 + 4), A("k2", 15, 64, 16))
+        new = full("mp%d" % (v + 1))
+        tt(IND(new, A("lsd", 0, 4)), full("gsm"), full("ee"), OP.max)
+        cp(IND(new, A("ltd", 4, 8)), A("vc", 64, 128))
+        cp(IND(full("cn"), full("ltd")), full("vc"))
+
+    def send(c, v):
+        n = {"a": NA + 64 * v + 64, "b": NB - 64 - 64 * v, "c": NC}[c]
+        o = 64 if c == "b" else 0
+        k = 6 * v + 2 * "bca".index(c)
+        put("g", "send", A("x%s%d" % (c, v + 1), 0, n), A("x%s%d" % (c, v), o, o + n), k)
+        src, dst = ("so" + c, "sf" + c) if v == 3 else ("s%s%d" % (c, v), "s%s%d" % (c, v + 1))
+        put("g", "send", A(dst, 0, n // 16), A(src, o // 16, (o + n) // 16), k + 1)
+
+    for v in range(4):
+        load[0] = 0
+        dma("s", MP[v + 1], MP[v])
+        for step in range(3):
+            head_step(v, step)
+            if step == 1:
+                stage1(v)
+        train(v)
+        for c in ("bca" if v < 3 else "ca"):
+            for step in range(3):
+                bulk_step(c, v, step)
+            send(c, v)
+    load[0] = 0
+    for g in range(8):
+        dma("s", A("yp", 0, W0, 1, 16 * g, 16 * g + 14), A("mp4", 0, W0, 1, 16 * g, 16 * g + 14))
+    for g in range(8):
+        dma("s", A("yp", 0, W0, 1, 16 * g + 14, 16 * g + 16), A("cn", 0, W0, 1, 16 * g + 14, 16 * g + 16))
+    load[0] = 0
+    dma("s", A("yx", NB, NB + NC), A("xc4", 0, NC))
+    dma("s", A("ys", NB // 16, (NB + NC) // 16), A("sfc", 0, NC // 16))
+    load[0] = 0
+    dma("s", A("yx", NB + NC, 1024), A("xa4", 0, NA))
+    dma("a", A("yx", 0, 256), A("xa4", NA, NA + 256))
+    dma("s", A("ys", (NB + NC) // 16, 64), A("sfa", 0, NA // 16))
+    dma("a", A("ys", 0, 16), A("sfa", NA // 16, NA // 16 + 16))
+
+    hist = {}
+    for i, op in enumerate(ops):
+        rd, wr = regions(op)
+        dep = set()
+        for lst, w in ((rd, False), (wr, True)):
+            for r in lst:
+                if r[1] in IO:
+                    continue
+                for (j, r2, w2) in hist.get(r[1], []):
+                    if inps(r):
+                        if ops[j]["q"] != op["q"] or op["q"] == "p":
+                            dep.add(j)
+                    elif (w or w2) and r[5] < r2[6] and r2[5] < r[6] and r[2] < r2[3] and r2[2] < r[3]:
+                        dep.add(j)
+        for lst, w in ((rd, False), (wr, True)):
+            for r in lst:
+                hist.setdefault(r[1], []).append((i, r, w))
+        op["dep"] = sorted(dep)
+    return ops
+
+
+def gap(ops, j, i, m):
+    a, b = ops[j], ops[i]
+    if a["k"] in ("dma", "send"):
+        return latency(a, m) + m["h"]
+    if a["q"] == b["q"]:
+        return 0.0 if a["q"] == "p" else m["hs"]
+    return m["h"]
+
+
+def schedule(ops, ms, iters, seed):
+    n = len(ops)
+    near = []
+    for i in range(n):
+        far = set(k for j in ops[i]["dep"] for k in ops[j]["dep"] if ops[k]["k"] not in ("dma", "send"))
+        near.append([j for j in ops[i]["dep"] if j not in far])
+    tabs = []
+    for m in ms:
+        c = [cost(o, m) for o in ops]
+        tabs.append((c, [latency(o, m) for o in ops], [[(j, c[j] + gap(ops, j, i, m)) for j in near[i]] for i in range(n)]))
+    x = [seed]
+
+    def rnd():
+        x[0] = (x[0] * 1103515245 + 12345) % 2147483648
+        return x[0] / 2147483648
+
+    def order_of(bump):
+        c, lat, dep = tabs[0]
+        rank = [c[i] + lat[i] for i in range(n)]
+        for i in range(n - 1, -1, -1):
+            rank[i] += bump[i]
+            for (j, d) in dep[i]:
+                if d + rank[i] > rank[j]:
+                    rank[j] = d + rank[i]
+        busy = {q: [] for q in "vapgs"}
+        st = [0.0] * n
+        for i in sorted(range(n), key=lambda i: (-rank[i], i)):
+            t = 0.0
+            for (j, d) in dep[i]:
+                if st[j] + d > t:
+                    t = st[j] + d
+            b = busy[ops[i]["q"]]
+            k = len(b)
+            while k > 0 and b[k - 1][1] > t:
+                k -= 1
+            while k < len(b) and t + c[i] > b[k][0]:
+                t = max(t, b[k][1])
+                k += 1
+            st[i] = t
+            b.insert(k, (t, t + c[i]))
+        return sorted(range(n), key=lambda i: (st[i], i))
+
+    def value(order):
+        total = 0.0
+        for (c, lat, dep) in tabs:
+            free = {q: 0.0 for q in "vapgs"}
+            st = [0.0] * n
+            end = 0.0
+            for i in order:
+                t = free[ops[i]["q"]]
+                for (j, d) in dep[i]:
+                    if st[j] + d > t:
+                        t = st[j] + d
+                st[i] = t
+                free[ops[i]["q"]] = t + c[i]
+                end = max(end, t + c[i] + lat[i])
+            total += end
+        return total
+    bump = [0.0] * n
+    best = order_of(bump)
+    bv = value(best)
+    for it in range(iters):
+        nb = list(bump)
+        for r in range(1 + int(rnd() * 4)):
+            nb[int(rnd() * n)] = rnd() * 5000.0 if rnd() < 0.8 else 0.0
+        o = order_of(nb)
+        val = value(o)
+        if val <= bv:
+            bump, best, bv = nb, o, val
+    return best
+
+
+PLAN = {}
+
+
+def plan():
+    if not PLAN:
+        PLAN["ops"] = build()
+        PLAN["order"] = schedule(PLAN["ops"], MODELS, OPT["iters"], OPT["seed"])
+    return PLAN["ops"], PLAN["order"]
+
+
+def relays(T, topo, r):
+    src, dst = T.cores[r], T.cores[(r + 1) % len(T.cores)]
+    ok = [c for c in topo.cores_of(src) if c != src and topo.may_write(c, dst)]
+    ok.sort(key=lambda c: topo.die(c) != topo.die(src))
+    return ok[:3]
+
+
+def bits(engines):
+    return sum(1 << e for e in engines)
+
+
+def piece(a, h):
+    n = (a[6] - a[5]) // 2
+    return A(a[1], a[5] + h * n, a[5] + h * n + n)
+
+
+def rank_program(g, core, T, topo):
+    ops, order = plan()
+    rank = T.rank_of(core)
+
+    def ap(a):
+        if not (isinstance(a, tuple) and len(a) > 0 and a[0] in ("ap", "ind")):
+            return a
+        if a[0] == "ind":
+            return ap(a[1]).indirect(ap(a[2]))
+        return T[a[1]][slice(a[2], a[3]), slice(a[5], a[6], a[7] if a[7] != 1 else None)]
+
+    if rank is None:
+        for r in range(len(T.cores)):
+            rl = relays(T, topo, r)
+            if core in rl:
+                me = rl.index(core)
+                dst = T.cores[(r + 1) % len(T.cores)]
+                rid, pid = topo.addr(dst, core)
+                en = topo.engines(core, dst)
+                half = len(topo.engines(T.cores[r], core)) // 2
+                total = 0
+                for i in order:
+                    op = ops[i]
+                    if op["k"] == "send" and op["a"][2] % 2 == me // 2:
+                        sem = T.sem["m%d" % op["a"][2]]
+                        a = ap(op["a"][0] if me == 2 else piece(op["a"][0], me))
+                        g.wait_ge(sem, half)
+                        g.remote_dma(a, a, sem, T.sem.sent, pid, rid, bits(en))
+                        total += len(en)
+                g.wait_ge(T.sem.sent, total)
+        return
+
+    rl = relays(T, topo, rank)
+    arrive = len(topo.engines(relays(T, topo, (rank - 1) % len(T.cores))[0], core))
+    Q = {"v": g.vector, "a": g.scalar, "p": g.tensor, "g": g, "s": g.sync}
+    token, count, seen = {}, {}, {q: {} for q in Q}
+    nd = [0]
+
+    def wait(q, tok):
+        if seen[q].get(tok[0], 0) < tok[1]:
+            Q[q].wait_ge(T.sem[tok[0]], tok[1])
+            seen[q][tok[0]] = tok[1]
+
+    for i in order:
+        op = ops[i]
+        q, k, e = op["q"], op["k"], Q[op["q"]]
+        need = {}
+        for j in op["dep"]:
+            if q == "p" and ops[j]["q"] == "p":
+                continue
+            s, val = token[j]
+            need[s] = max(need.get(s, 0), val)
+        if k in ("iota", "sel") and "cg" in count:
+            need["cg"] = count["cg"]
+        for s in need:
+            wait(q, (s, need[s]))
+        a = [ap(x) for x in op["a"]] if k != "mm" else None
+        if k == "send":
+            en = topo.engines(core, rl[0])
+            half = len(en) // 2
+            s = "m%d" % a[2]
+            if a[2] % 2:
+                rid, pid = topo.addr(rl[2], core)
+                g.remote_dma(a[0], a[1], T.sem[s], T.sem.sent, pid, rid, bits(en[:half]))
+                ways = 1
+            else:
+                tr = []
+                for h in range(2):
+                    rid, pid = topo.addr(rl[h], core)
+                    tr.append(RemoteDMATransfer(dst_ids=[DstId(rid=rid, pnc=pid)], remote_sem=T.sem[s],
+                                                dma_engine_mask=bits(en[h * half:h * half + half]),
+                                                src=ap(piece(op["a"][1], h)), dst=ap(piece(op["a"][0], h))))
+                g.remote_dma_fused(tr, local_sem=T.sem.sent)
+                ways = 2
+            count["sent"] = count.get("sent", 0) + ways * half
+            count[s] = ways * arrive
+            token[i] = (s, count[s])
+            continue
+        if k == "dma":
+            s = "d%d" % nd[0]
+            nd[0] += 1
+            e.dma_start(a[0], a[1]).then_inc(T.sem[s], 16)
+            token[i] = (s, 16)
+            count[s] = 16
+            continue
+        if k == "mm":
+            for x in op["a"]:
+                ins = e.matmul(ap(x[0]), ap(x[1]), ap(x[2]), x[3], x[4])
+        elif k == "iota":
+            if SCRATCH[op["a"][0][1]][2] == "int32":
+                ins = e.iota(a[0], a[1], a[2], a[3])
+            else:
+                ins = e.iota(a[0], a[1], a[2], a[3], allow_small_or_imprecise_dtypes=True)
+        elif k == "sel":
+            ins = e.affine_select(*a)
+        elif k == "ts":
+            ins = e.tensor_scalar(*a[:5]) if a[5] is None else e.tensor_scalar(*a)
+        elif k == "tt":
+            ins = e.tensor_tensor(*a)
+        elif k == "cp":
+            ins = e.tensor_copy(*a)
+        elif k == "ms":
+            ins = e.memset(*a)
+        elif k == "scan":
+            ins = e.tensor_tensor_scan(*a)
+        else:
+            ins = e.activation(a[0], a[1], a[2], bias=a[3], scale=a[4])
+        s = "c" + q
+        count[s] = count.get(s, 0) + 1
+        ins.then_inc(T.sem[s], 1)
+        token[i] = (s, count[s])
+    for s in count:
+        wait("g", (s, count[s]))

@@ -1,16 +1,16 @@
-import math
 from concourse.bass import DstId, RemoteDMATransfer
 from concourse.mybir import AluOpType, ActivationFunctionType
 
 OP = AluOpType
 AF = ActivationFunctionType
 V0, W0, WD = 1328, 1584, 1712
+F = 8
 MAGIC = 12582912.0
 KV = 4096.0
-OPT = {"na": 320, "a": "AV", "c": "V", "b": "G", "gt": "v", "iters": 5000, "seed": 1}
-MODEL = {"cyc": 1.04, "pe": 0.62, "g": 1.56, "s": 3.5, "h": 130.0, "hs": 110.0, "hop": 5000.0, "fix": 30.0}
-MODELS = [MODEL, dict(MODEL, pe=0.52, h=60.0, hs=60.0, g=1.2, hop=4000.0),
-          dict(MODEL, pe=0.9, h=200.0, hs=200.0, g=1.9, hop=6500.0)]
+OPT = {"na": 320, "a": "V", "c": "V", "b": "G", "gt": "v", "iters": 6000, "seed": 1}
+MODEL = {"cyc": 0.95, "pe": 0.48, "g": 1.56, "s": 3.5, "h": 100.0, "hs": 100.0, "hop": 4500.0, "fix": 20.0, "bw": 60.0}
+MODELS = [MODEL, dict(MODEL, cyc=0.83, pe=0.42, h=80.0, hs=80.0, g=1.3, hop=4000.0, bw=80.0),
+          dict(MODEL, cyc=1.2, pe=0.6, h=130.0, hs=130.0, g=1.9, hop=6000.0, bw=45.0)]
 
 SCRATCH = {}
 
@@ -23,27 +23,27 @@ def _buf(dtype, cols, names):
 _buf("int32", V0, "raw")
 _buf("int32", 64, "sti")
 _buf("int32", 8, "sgi coli")
-_buf("float32", WD, "mp0 mp1 mp2 mp3 mp4 cn")
-_buf("float32", 48, "soa soc sfa sfc")
-_buf("float32", 32, "col")
+_buf("float32", F + WD, "mp0 mp1 rp1 rp2 rp3 cn")
+_buf("float32", 48, "soa soc col")
+_buf("float32", 8, "soh sfh")
 _buf("float32", 64, "ihp ihn mof32 c0 zer bb zz nxm k1 k2 gsc gsm sel ns gt ht clo cl2 ncm d0 d1 cd ee vn")
-_buf("float32", 128, "i32 i32n wh wn wc cl k0 vc vv")
-_buf("float32", 384, "rra rrb rrc")
-_buf("bfloat16", 32, "w24")
+_buf("float32", 128, "i32 i32n wh wn wc cl k0 vv")
+_buf("float32", 384, "rra rrb rrc dv")
+_buf("float32", 768, "vc")
 _buf("bfloat16", 64, "jm moff hh sgn")
-_buf("bfloat16", 128, "jd bd wv wt0 wdl we ib ibn wx ik")
-_buf("bfloat16", 256, "j64 ra ras tri1 tri2 hb yb xb0 xb1 xb2 xb3")
+_buf("bfloat16", 128, "jd bd wv wt0 wdl we ib ibn wx ik w24")
+_buf("bfloat16", 256, "j64 ra ras tri1 tri2 hb yb xb0 xb1 xb2 xb3 xo")
 _buf("bfloat16", 512, "zb selb lc")
-_buf("bfloat16", 640, "ha hc ya yc xa0 xa1 xa2 xa3 xa4 xc0 xc1 xc2 xc3 xc4")
+_buf("bfloat16", 640, "ha hc ya yc xa xc")
 _buf("float16", 640, "pa pb pc")
 _buf("float16", 64, "ph sw tw ng")
 _buf("float16", 320, "eq eq2")
-_buf("uint16", 8, "l1 l2 l3 lsd ltd")
-_buf("uint16", 48, "sa0 sa1 sa2 sa3 sb0 sb1 sb2 sb3 sc0 sc1 sc2 sc3")
+_buf("uint16", 8, "l1 l2 l3")
+_buf("uint16", 64, "sa sc sb0 sb1 sb2 sb3 ltd dl nl no")
 for _b in range(8):
     SCRATCH["ps%d" % _b] = ("psum", [128, 512], "float32")
 
-SEMAPHORES = ["cv", "ca", "cp", "cg", "sent"] + ["m%d" % i for i in range(24)] + ["d%d" % i for i in range(48)]
+SEMAPHORES = ["cv", "ca", "cp", "cg"] + [p + str(i) for p in "mt" for i in range(28)] + ["d%d" % i for i in range(48)]
 BYTES = {"float32": 4, "int32": 4, "float16": 2, "bfloat16": 2, "uint16": 2}
 IO = ("recs", "st0", "cx0", "sg", "yp", "ys", "yx")
 
@@ -108,7 +108,9 @@ def latency(op, m):
         return 1800 + op["load"] / 180.0
     if op["k"] == "send":
         o = op["a"][0]
-        return m["hop"] + 128 * ncols(o) * isz(o) / 100.0
+        if op["load"]:
+            return m["hop"] + op["load"] / m["bw"]
+        return m["hop"] * (1.0 if op["a"][4] else 0.55) + 128 * ncols(o) * isz(o) / 100.0
     return 0.0
 
 
@@ -127,9 +129,6 @@ def regions(op):
             add(out, wr)
             add(l, rd)
             add(r, rd)
-    elif k == "send":
-        add(a[1], rd)
-        wr.append(A(a[0][1], 0, SCRATCH[a[0][1]][1][1]))
     else:
         add(a[0], wr)
         for x in a[1:]:
@@ -143,7 +142,7 @@ def build():
     NC = 1024 - NA - NB
 
     def put(q, k, *a):
-        ops.append({"q": q, "k": k, "a": a})
+        ops.append({"q": q, "k": k, "a": a, "load": 0})
     ts = lambda out, i, s1, s2, o0, o1=None: put("v", "ts", out, i, s1, s2, o0, o1)
     tt = lambda out, i, j, o: put("v", "tt", out, i, j, o)
     cp = lambda out, i: put("v", "cp", out, i)
@@ -155,13 +154,20 @@ def build():
     half = lambda n, h, c=None: A(n, 0, c or SCRATCH[n][1][1], 1, 64 * h, 64 * h + 64)
     pick = lambda out, pat, cmp, fill, base, cm: put("g", "sel", out, A("zb", 0, ncols(out), 1, out[2], out[3]), pat, cmp,
                                                      fill, base, cm)
-    MP, CN, IB = [A("mp%d" % v, 0, W0) for v in range(5)], A("cn", 0, W0), full("ib")
-    load = [0]
+    win = lambda n, w=W0: A(n, F, F + w)
+    MP = [win("mp0")] + [win("mp1")] * 3
+    HOME = [win("mp0"), win("rp1"), win("rp2"), win("rp3")]
+    CN, IB = win("cn"), full("ib")
+    load, nsend = [0], [0]
 
     def dma(q, out, i):
         put(q, "dma", out, i)
         load[0] += (out[3] - out[2]) * ncols(out) * (2 if out[1][0] == "x" or out[1] == "yx" else 4)
         ops[-1]["load"] = load[0]
+
+    def send(dst, src, step, ways):
+        put("g", "send", dst, src, nsend[0], step % 4, [] if step % 4 == 2 and ways != [2, 3] else ways)
+        nsend[0] += 1
 
     hv = V0 // 4
     dma("s", A("sgi", 0, 1), A("sg", 0, 1))
@@ -170,8 +176,8 @@ def build():
         dma("sa"[k % 2], A("raw", hv * k, hv * k + hv), A("recs", hv * k, hv * k + hv))
         if k == 1:
             dma("s", A("xb0", 0, NB), A("cx0", 0, NB))
-    dma("a", A("xa0", 0, NA), A("cx0", NB + NC, 1024))
-    dma("s", A("xc0", 0, NC), A("cx0", NB, NB + NC))
+    dma("a", A("xa", 0, NA), A("cx0", NB + NC, 1024))
+    dma("s", A("xc", 0, NC), A("cx0", NB, NB + NC))
     put("v", "ms", full("zb"), 0.0)
     put("g", "iota", A("coli", 0, 1), [[0, 1]], 0, 1)
     put("g", "iota", full("jd"), [[1, 8], [0, 16]], 0, 0)
@@ -199,8 +205,6 @@ def build():
     ts(full("ras"), full("j64"), C(4), 2048.0, OP.is_equal, OP.mult)
     lin(C(10), C(6), 1.0, C(7))
     lin(C(11), C(6), -1.0, C(7))
-    lin(C(12), C(5), KV)
-    lin(C(13), C(5), KV, C(11))
     lin(C(14), C(8), 0.5)
     lin(C(15), C(8), -0.25)
     lin(C(16), C(8), -0.25, C(10))
@@ -216,8 +220,13 @@ def build():
     lin(C(27), C(1), 0.0, float(V0 - 1))
     lin(C(29), C(16), 1.0, 128.0)
     bd8 = A("bd", 0, 128, 16)
-    for s, c in enumerate((19, 13, 12)):
-        lin(A("w24", 8 * s, 8 * s + 8), bd8, C(c))
+
+    def weights(v, sign):
+        lin(C(32 + 2 * v), sign, KV, C(11))
+        lin(C(33 + 2 * v), sign, KV)
+        for s, c in enumerate((19, 32 + 2 * v, 33 + 2 * v)):
+            lin(A("w24", 32 * v + 8 * s, 32 * v + 8 * s + 8), bd8, C(c))
+    weights(0, C(5))
     for n, c in (("wv", 5), ("wt0", 6), ("wdl", 11), ("wc", 9)):
         lin(full(n), full("bd"), C(c))
     for n, c in (("wx", C(14)), ("i32", 1.0), ("ik", 16384.0), ("i32n", -1.0), ("ibn", -1.0), ("wh", C(20)), ("wn", C(21))):
@@ -226,9 +235,12 @@ def build():
     lin(full("ihn"), A("ib", 0, 64), -0.5)
     lin(full("mof32"), full("moff"), 1.0)
     lin(full("tri2"), full("tri1"), 1.0, -30720.0)
-    lin(A("mp0", V0, W0), A("zb", 0, W0 - V0), 1.0)
+    lin(A("mp0", 0, F), A("zb", 0, F), 1.0, C(5))
+    lin(A("mp0", F + V0, F + W0), A("zb", 0, W0 - V0), 1.0)
+    for v in range(1, 4):
+        lin(A("rp%d" % v, F + V0 + 64 * (v - 1), F + W0), A("zb", 0, W0 - V0 - 64 * (v - 1)), 1.0)
     for k in range(4):
-        lin(A("cn", 396 * k, 396 * k + 396), A("zb", 0, 396), 1.0)
+        lin(A("cn", F + 396 * k, F + 396 * k + 396), A("zb", 0, 396), 1.0)
     lin(full("zer"), A("zb", 0, 64), 1.0)
     lin(full("we"), A("zb", 0, 128), 1.0)
     for k in range(12, 16):
@@ -236,24 +248,24 @@ def build():
     lin(full("cl"), A("zb", 0, 128), 1.0)
     lin(A("cl", 0, 128, 16), A("jd", 0, 128, 16), 16.0, C(26))
     for k in range(4):
-        cp(A("mp0", hv * k, hv * k + hv), A("raw", hv * k, hv * k + hv))
+        cp(A("mp0", F + hv * k, F + hv * k + hv), A("raw", hv * k, hv * k + hv))
     load[0] = 0
     for g in range(8):
-        dma("s", A("cn", 0, V0, 1, 16 * g + 14, 16 * g + 16), A("mp0", 0, V0, 1, 16 * g + 14, 16 * g + 16))
+        dma("s", A("cn", F, F + V0, 1, 16 * g + 14, 16 * g + 16), A("mp0", F, F + V0, 1, 16 * g + 14, 16 * g + 16))
     cp(A("sb0", 0, NB // 16), A("sti", 0, NB // 16))
-    cp(A("sc0", 0, NC // 16), A("sti", NB // 16, (NB + NC) // 16))
-    cp(A("sa0", 0, NA // 16), A("sti", (NB + NC) // 16, 64))
-    for (n, i, j) in (("xb0", 0, 64), ("xb0", 64, NB), ("xa0", 0, NA), ("xc0", 0, NC)):
+    cp(A("sc", 0, NC // 16), A("sti", NB // 16, (NB + NC) // 16))
+    cp(A("sa", 0, NA // 16), A("sti", (NB + NC) // 16, 64))
+    for (n, i, j) in (("xb0", 0, 64), ("xb0", 64, NB), ("xa", 0, NA), ("xc", 0, NC)):
         lin(A(n, i, j), A(n, i, j), 1.0, C(10))
 
-    def xstep(win, X, XO, H, Y, off, n, bank, last, mode):
+    def xstep(w, X, XO, H, Y, off, n, bank, last, mode):
         if mode == "G":
             def both():
-                tt(A(H, 0, n), IND(win, off), X, OP.add)
+                tt(A(H, 0, n), IND(w, off), X, OP.add)
                 lin(A(Y, 0, n), A(H, 0, n), C(14), C(29))
                 lin(XO, A(Y, 0, n), 1.0, -128.0)
             return [], [], both
-        lin(A(H, 0, n), IND(win, off), C(14), C(15 if last else 16))
+        lin(A(H, 0, n), IND(w, off), C(14), C(15 if last else 16))
         o = A(bank[0], bank[1], bank[1] + n)
 
         def rnd():
@@ -268,34 +280,37 @@ def build():
         n = {"a": NA + 64 * v, "b": NB - 64 - 64 * v, "c": NC}[c]
         o = 64 if c == "b" else 0
         m = n // 16
-        X = A("x%s%d" % (c, v), o, o + n)
-        S = A("s%s%d" % (c, v), o // 16, o // 16 + m)
+        tag, w, wk = ("b%d" % v, MP[v], 0) if c == "b" else (c, HOME[v], 32 * v)
+        X = A("x" + tag, o, o + n)
+        S = A("s" + tag, o // 16, o // 16 + m)
         last = v == 3 and step == 2
         bs, bx = {"a": ("ps0", "ps2"), "c": ("ps1", "ps3"), "b": ("ps4", None)}[c]
         P, R = "p" + c, "rr" + c
-        m1, m2, rnd = xstep(MP[v], X, X, "h" + c, "y" + c, S, n, (bx, 0), last, OPT[c])
+        m1, m2, rnd = xstep(w, X, X, "h" + c, "y" + c, S, n, (bx, 0), last, OPT[c])
         if m1:
             mm(m1)
-        tt(A(P, 0, n), IND(MP[v], S), X, OP.mult)
+        tt(A(P, 0, n), IND(w, S), X, OP.mult)
         if not m1:
             rnd()
-        mm([(A(bs, k, 384, 16, 0, m), A(P, k, n, 16), A("w24", 0, 24), True, True) for k in range(16)])
+        mm([(A(bs, k, 384, 16, 0, m), A(P, k, n, 16), A("w24", wk, wk + 24), True, True) for k in range(16)])
         act(A(R, 0, 384, 1, 0, m), A(bs, 0, 384, 1, 0, m), AF.Abs, -2048.0, 1.0)
         if m2:
             mm(m2)
         o3 = A(bs, 384, 384 + m)
         mm([(o3, A(R, 128 * s, 128 * s + 128, 1, 0, m), A("ihn" if s == 2 else "ihp", 0, m, 1, 0, m), s == 0, s == 2)
             for s in range(3)])
-        ts(A("so" + c, o // 16, o // 16 + m) if last else S, o3, -1024.0, None, OP.add)
+        ts(A("so" + c, 0, m) if last else S, o3, -1024.0, None, OP.add)
         if m1:
             rnd()
 
+    def trained(v):
+        return A("xa", NA, NA + 64) if v == 0 else A("xo", 64 * v, 64 * v + 64)
+
     def head_step(v, step):
         X = A("xb%d" % v, 0, 64)
-        na = NA + 64 * v
-        XO = A("xa%d" % v, na, na + 64) if step == 2 else X
         S = (A("sb%d" % v, 0, 4), A("l1", 0, 4), A("l2", 0, 4))[step]
-        m1, m2, rnd = xstep(MP[v], X, XO, "hh", None, S, 64, ("ps5", 256), v == 3 and step == 2, "V")
+        m1, m2, rnd = xstep(MP[v], X, trained(v) if step == 2 else X, "hh", None, S, 64, ("ps5", 256),
+                            v == 3 and step == 2, "V")
         P = full("ph")
         tt(P, IND(MP[v], S), X, OP.mult)
         r = lambda k: A("ps5", 64 * k, 64 * k + 64)
@@ -325,6 +340,9 @@ def build():
         return [(out, A("lc", 128 * k, 128 * k + 128), A(e, 64 * k, 64 * k + 64), start and k == 0, stop and k == 3)
                 for k in range(4)]
 
+    LT = lambda v, i, j: A("ltd", 16 * v + i, 16 * v + j)
+    VC = lambda v, i, j: A("vc", 192 * v + i, 192 * v + j)
+
     def stage1(v):
         mm([(D, IB, full("tri1"), True, False)] + pairs("sw"))
         ts(A("eq", 0, 256), D, 0.0, 4096.0, OP.is_equal, OP.mult)
@@ -332,7 +350,7 @@ def build():
         mm([(sd, IB, full("moff"), True, False), (sd, IB, full("sw"), False, False)] + counts(sd, "eq", False, True))
         ts(full("ng"), sd, 2000.0, None, OP.is_gt)
         scan(full("k1"), A("cl", 0, 64), sd, 0.0, OP.max, OP.min)
-        cp(A("lsd", 0, 4), A("k1", 15, 64, 16))
+        cp(LT(v, 8, 12), A("k1", 15, 64, 16))
         mm([(D, IB, full("tri2"), True, False)]
            + [(half("ps6", h, 256), half("ng", h), half("ras", h), False, False) for h in range(2)])
         lin(full("gsc"), IND(CN, A("l2", 0, 4)), 1.0)
@@ -342,11 +360,10 @@ def build():
         mm([(pg, full("i32n"), full("gsc"), True, False), (pg, full("ik"), full("sgn"), False, True)])
 
     def train(v):
-        na = NA + 64 * v
         e, q = A("ps7", 0, 64), A("ps7", 64, 128)
         mm(counts(e, "eq", True, False) + [(e, full("we"), full("ph"), False, True)])
         ts(full("sel"), e, C(25), None, OP.is_lt)
-        tt(IND(full("cn"), A("lsd", 0, 4)), full("gsc"), full("sel"), OP.add)
+        tt(IND(win("cn", WD), LT(v, 8, 12)), full("gsc"), full("sel"), OP.add)
         tt(full("ns"), full("sel"), A("ps7", 128, 192), OP.mult)
         mm(pairs("tw") + [(DF, IB, full("tw"), True, False), (DF, full("ibn"), full("sw"), False, True)])
         ts(full("eq2"), A("ps6", 0, 320), 0.0, -32768.0, OP.is_equal, OP.mult)
@@ -361,7 +378,7 @@ def build():
         ts(full("clo"), q, 16384.0 + 13, None, OP.is_ge)
         ts(full("cl2"), q, 16384.0 + 13, 4096.0, OP.is_lt, OP.mult)
         vt, vd = A("ps7", 192, 256), A("ps7", 256, 320)
-        mm([(vd, full("i32"), full("ht"), True, False), (vd, full("wx"), A("xa%d" % v, na, na + 64), False, False),
+        mm([(vd, full("i32"), full("ht"), True, False), (vd, full("wx"), trained(v), False, False),
             (vd, full("wh"), full("gt"), False, True),
             (vt, full("wn"), full("ht"), True, False), (vt, full("wh"), full("gt"), False, True)])
         dn = "d%d" % (v % 2)
@@ -372,54 +389,74 @@ def build():
         tt(full("cd"), full("clo"), full(dn), OP.mult)
         scan(full("k0"), full("cl"), full("vv"), 0.0, OP.max, OP.min)
         tt(full("ee"), full("cd"), full("sel"), OP.mult)
-        cp(full("ltd"), A("k0", 15, 128, 16))
-        ts(full("vc"), A("ps7", 192, 320), MAGIC, MAGIC, OP.add, OP.subtract)
+        cp(LT(v, 0, 8), A("k0", 15, 128, 16))
+        ts(VC(v, 0, 128), A("ps7", 192, 320), MAGIC, MAGIC, OP.add, OP.subtract)
+        tt(VC(v, 128, 192), full("gsm"), full("ee"), OP.max)
+        cp(IND(win("mp1", WD), LT(v, 4, 12)), VC(v, 64, 192))
         tt(full("vn"), full("nxm"), full("cd"), OP.max)
         scan(full("k2"), full("c0"), full("vn"), 0.0, OP.max, OP.min)
-        cp(A("soa" if v == 3 else "sa%d" % v, na // 16, na // 16 + 4), A("k2", 15, 64, 16))
-        new = full("mp%d" % (v + 1))
-        tt(IND(new, A("lsd", 0, 4)), full("gsm"), full("ee"), OP.max)
-        cp(IND(new, A("ltd", 4, 8)), A("vc", 64, 128))
-        cp(IND(full("cn"), full("ltd")), full("vc"))
+        tail = A("sa", NA // 16 + 4 * v, NA // 16 + 4 * v + 4)
+        cp((tail, A("no", 8, 12), A("no", 16, 20), A("soh", 0, 4))[v], A("k2", 15, 64, 16))
+        cp(IND(win("cn", WD), LT(v, 0, 8)), VC(v, 0, 128))
+        if v < 3:
+            send(A("dv", 128 * v, 128 * v + 128), VC(v, 64, 192), -(v + 1), [0, 1])
+            send(A("dl", 8 * v, 8 * v + 8), LT(v, 4, 12), -(v + 1), [1])
+        if v > 0:
+            send(A("xa", NA + 64 * v, NA + 64 * v + 64), trained(v), -v, [0])
+        if v in (1, 2):
+            send(A("nl", 8 * v, 8 * v + 4), A("no", 8 * v, 8 * v + 4), -v, [1])
+            cp(tail, A("nl", 8 * v, 8 * v + 4))
+        if v == 3:
+            send(A("sfh", 0, 4), A("soh", 0, 4), -v, [1])
 
-    def send(c, v):
-        n = {"a": NA + 64 * v + 64, "b": NB - 64 - 64 * v, "c": NC}[c]
-        o = 64 if c == "b" else 0
-        k = 6 * v + 2 * "bca".index(c)
-        put("g", "send", A("x%s%d" % (c, v + 1), 0, n), A("x%s%d" % (c, v), o, o + n), k)
-        src, dst = ("so" + c, "sf" + c) if v == 3 else ("s%s%d" % (c, v), "s%s%d" % (c, v + 1))
-        put("g", "send", A(dst, 0, n // 16), A(src, o // 16, (o + n) // 16), k + 1)
+    def base(v):
+        n = (F + V0 + 64 * (v - 1)) // 2
+        for h in range(2):
+            send(A("rp%d" % v, n * h, n * h + n), A("mp0" if v == 1 else "mp1", n * h, n * h + n), -v, [2, 3])
+            ops[-1]["load"] = 512 * n * (h + 1)
+        weights(v, A("rp%d" % v, 0, 1))
 
+    base(1)
+    load[0] = 0
+    dma("s", A("mp1", 0, F + W0), A("mp0", 0, F + W0))
     for v in range(4):
-        load[0] = 0
-        dma("s", MP[v + 1], MP[v])
         for step in range(3):
             head_step(v, step)
             if step == 1:
                 stage1(v)
-        train(v)
-        for c in ("bca" if v < 3 else "ca"):
+        if v < 3:
+            for step in range(3):
+                bulk_step("b", v, step)
+            n = NB - 64 - 64 * v
+            send(A("xb%d" % (v + 1), 0, n), A("xb%d" % v, 64, 64 + n), 1, [0, 1])
+            send(A("sb%d" % (v + 1), 0, n // 16), A("sb%d" % v, 4, 4 + n // 16), 1, [1])
+        if v > 0:
+            cp(IND(win("rp%d" % v, WD), A("dl", 8 * v - 8, 8 * v)), A("dv", 128 * v - 128, 128 * v))
+        for c in "ca":
             for step in range(3):
                 bulk_step(c, v, step)
-            send(c, v)
+        train(v)
+        if v < 2:
+            base(v + 2)
     load[0] = 0
     for g in range(8):
-        dma("s", A("yp", 0, W0, 1, 16 * g, 16 * g + 14), A("mp4", 0, W0, 1, 16 * g, 16 * g + 14))
+        dma("s", A("yp", 0, W0, 1, 16 * g, 16 * g + 14), A("mp1", F, F + W0, 1, 16 * g, 16 * g + 14))
     for g in range(8):
-        dma("s", A("yp", 0, W0, 1, 16 * g + 14, 16 * g + 16), A("cn", 0, W0, 1, 16 * g + 14, 16 * g + 16))
+        dma("s", A("yp", 0, W0, 1, 16 * g + 14, 16 * g + 16), A("cn", F, F + W0, 1, 16 * g + 14, 16 * g + 16))
     load[0] = 0
-    dma("s", A("yx", NB, NB + NC), A("xc4", 0, NC))
-    dma("s", A("ys", NB // 16, (NB + NC) // 16), A("sfc", 0, NC // 16))
+    dma("s", A("yx", NB, NB + NC), A("xc", 0, NC))
+    dma("s", A("ys", NB // 16, (NB + NC) // 16), A("soc", 0, NC // 16))
     load[0] = 0
-    dma("s", A("yx", NB + NC, 1024), A("xa4", 0, NA))
-    dma("a", A("yx", 0, 256), A("xa4", NA, NA + 256))
-    dma("s", A("ys", (NB + NC) // 16, 64), A("sfa", 0, NA // 16))
-    dma("a", A("ys", 0, 16), A("sfa", NA // 16, NA // 16 + 16))
+    dma("s", A("yx", NB + NC, 1024), A("xa", 0, NA))
+    dma("a", A("yx", 0, 256), A("xa", NA, NA + 256))
+    dma("s", A("ys", (NB + NC) // 16, 64), A("soa", 0, NA // 16))
+    dma("a", A("ys", 0, 12), A("soa", NA // 16, NA // 16 + 12))
+    dma("a", A("ys", 12, 16), A("sfh", 0, 4))
 
     hist = {}
     for i, op in enumerate(ops):
         rd, wr = regions(op)
-        dep = set()
+        dep, land = set(), set()
         for lst, w in ((rd, False), (wr, True)):
             for r in lst:
                 if r[1] in IO:
@@ -430,15 +467,20 @@ def build():
                             dep.add(j)
                     elif (w or w2) and r[5] < r2[6] and r2[5] < r[6] and r[2] < r2[3] and r2[2] < r[3]:
                         dep.add(j)
+                        if w2:
+                            land.add(j)
         for lst, w in ((rd, False), (wr, True)):
             for r in lst:
                 hist.setdefault(r[1], []).append((i, r, w))
         op["dep"] = sorted(dep)
+        op["left"] = set(j for j in dep if ops[j]["k"] == "send" and j not in land)
     return ops
 
 
 def gap(ops, j, i, m):
     a, b = ops[j], ops[i]
+    if j in b["left"]:
+        return 2000 + a["load"] / 120.0
     if a["k"] in ("dma", "send"):
         return latency(a, m) + m["h"]
     if a["q"] == b["q"]:
@@ -529,24 +571,25 @@ def plan():
 
 
 def relays(T, topo, r):
-    src, dst = T.cores[r], T.cores[(r + 1) % len(T.cores)]
-    ok = [c for c in topo.cores_of(src) if c != src and topo.may_write(c, dst)]
+    src = T.cores[r]
+    ok = [c for c in topo.cores_of(src) if c != src and all(topo.may_write(c, d) for d in T.cores)]
     ok.sort(key=lambda c: topo.die(c) != topo.die(src))
-    return ok[:3]
+    return ok
 
 
 def bits(engines):
     return sum(1 << e for e in engines)
 
 
-def piece(a, h):
-    n = (a[6] - a[5]) // 2
+def piece(a, h, k):
+    n = (a[6] - a[5]) // k
     return A(a[1], a[5] + h * n, a[5] + h * n + n)
 
 
 def rank_program(g, core, T, topo):
     ops, order = plan()
     rank = T.rank_of(core)
+    nr = len(T.cores)
 
     def ap(a):
         if not (isinstance(a, tuple) and len(a) > 0 and a[0] in ("ap", "ind")):
@@ -556,30 +599,30 @@ def rank_program(g, core, T, topo):
         return T[a[1]][slice(a[2], a[3]), slice(a[5], a[6], a[7] if a[7] != 1 else None)]
 
     if rank is None:
-        for r in range(len(T.cores)):
+        for r in range(nr):
             rl = relays(T, topo, r)
             if core in rl:
                 me = rl.index(core)
-                dst = T.cores[(r + 1) % len(T.cores)]
-                rid, pid = topo.addr(dst, core)
-                en = topo.engines(core, dst)
                 half = len(topo.engines(T.cores[r], core)) // 2
                 total = 0
                 for i in order:
                     op = ops[i]
-                    if op["k"] == "send" and op["a"][2] % 2 == me // 2:
-                        sem = T.sem["m%d" % op["a"][2]]
-                        a = ap(op["a"][0] if me == 2 else piece(op["a"][0], me))
-                        g.wait_ge(sem, half)
-                        g.remote_dma(a, a, sem, T.sem.sent, pid, rid, bits(en))
+                    if op["k"] == "send" and me in op["a"][4]:
+                        (d, s, k, step, ways) = op["a"]
+                        dst = T.cores[(r + step) % nr]
+                        rid, pid = topo.addr(dst, core)
+                        en = topo.engines(core, dst)
+                        a = ap(piece(d, ways.index(me), len(ways)))
+                        g.wait_ge(T.sem["m%d" % k], half)
+                        g.remote_dma(a, a, T.sem["m%d" % k], T.sem.cg, pid, rid, bits(en))
                         total += len(en)
-                g.wait_ge(T.sem.sent, total)
+                g.wait_ge(T.sem.cg, total)
         return
 
     rl = relays(T, topo, rank)
-    arrive = len(topo.engines(relays(T, topo, (rank - 1) % len(T.cores))[0], core))
+    arrive = len(topo.engines(relays(T, topo, (rank - 1) % nr)[0], core))
     Q = {"v": g.vector, "a": g.scalar, "p": g.tensor, "g": g, "s": g.sync}
-    token, count, seen = {}, {}, {q: {} for q in Q}
+    token, gone, count, seen = {}, {}, {}, {q: {} for q in Q}
     nd = [0]
 
     def wait(q, tok):
@@ -594,33 +637,35 @@ def rank_program(g, core, T, topo):
         for j in op["dep"]:
             if q == "p" and ops[j]["q"] == "p":
                 continue
-            s, val = token[j]
+            s, val = gone[j] if j in op["left"] else token[j]
             need[s] = max(need.get(s, 0), val)
+        if k == "send":
+            need = {s: need[s] for s in need}
         if k in ("iota", "sel") and "cg" in count:
             need["cg"] = count["cg"]
         for s in need:
             wait(q, (s, need[s]))
         a = [ap(x) for x in op["a"]] if k != "mm" else None
         if k == "send":
+            (d, src, n, step, ways) = op["a"]
+            s, t = "m%d" % n, "t%d" % n
             en = topo.engines(core, rl[0])
             half = len(en) // 2
-            s = "m%d" % a[2]
-            if a[2] % 2:
-                rid, pid = topo.addr(rl[2], core)
-                g.remote_dma(a[0], a[1], T.sem[s], T.sem.sent, pid, rid, bits(en[:half]))
-                ways = 1
-            else:
+            if len(ways) == 2:
                 tr = []
                 for h in range(2):
-                    rid, pid = topo.addr(rl[h], core)
+                    rid, pid = topo.addr(rl[ways[h]], core)
                     tr.append(RemoteDMATransfer(dst_ids=[DstId(rid=rid, pnc=pid)], remote_sem=T.sem[s],
                                                 dma_engine_mask=bits(en[h * half:h * half + half]),
-                                                src=ap(piece(op["a"][1], h)), dst=ap(piece(op["a"][0], h))))
-                g.remote_dma_fused(tr, local_sem=T.sem.sent)
-                ways = 2
-            count["sent"] = count.get("sent", 0) + ways * half
-            count[s] = ways * arrive
-            token[i] = (s, count[s])
+                                                src=ap(piece(src, h, 2)), dst=ap(piece(d, h, 2))))
+                g.remote_dma_fused(tr, local_sem=T.sem[t])
+            else:
+                to = rl[ways[0]] if ways else T.cores[(rank + step) % nr]
+                rid, pid = topo.addr(to, core)
+                g.remote_dma(a[0], a[1], T.sem[s], T.sem[t], pid, rid, bits(topo.engines(core, to)[:half]))
+            count[t] = max(1, len(ways)) * half
+            count[s] = max(1, len(ways)) * arrive
+            token[i], gone[i] = (s, count[s]), (t, count[t])
             continue
         if k == "dma":
             s = "d%d" % nd[0]

@@ -5,51 +5,62 @@ OP = AluOpType
 AF = ActivationFunctionType
 V0, W0, WD = 1328, 1584, 1712
 F = 8
+E = 240.0
 MAGIC = 12582912.0
-KV = 4096.0
-OPT = {"na": 320, "a": "V", "c": "V", "b": "G", "gt": "v", "iters": 6000, "seed": 1}
-MODEL = {"cyc": 0.95, "pe": 0.48, "g": 1.56, "s": 3.5, "h": 100.0, "hs": 100.0, "hop": 4500.0, "fix": 20.0, "bw": 60.0}
-MODELS = [MODEL, dict(MODEL, cyc=0.83, pe=0.42, h=80.0, hs=80.0, g=1.3, hop=4000.0, bw=80.0),
-          dict(MODEL, cyc=1.2, pe=0.6, h=130.0, hs=130.0, g=1.9, hop=6000.0, bw=45.0)]
+NM, NB = 384, 256
+OPT = {"pieces": 8, "iters": 4000, "seed": 1}
+MODEL = {"cyc": 0.95, "pe": 0.48, "g": 1.56, "s": 3.5, "h": 100.0, "hs": 100.0, "hop": 3500.0, "fix": 20.0, "bw": 80.0}
+MODELS = [MODEL, dict(MODEL, cyc=0.83, pe=0.42, h=80.0, hs=80.0, g=1.3, hop=3000.0, bw=100.0),
+          dict(MODEL, cyc=1.2, pe=0.6, h=130.0, hs=130.0, g=1.9, hop=5500.0, bw=50.0)]
 
 SCRATCH = {}
 
 
-def _buf(dtype, cols, names):
+def _buf(dtype, shape, names, where="sbuf"):
     for n in names.split():
-        SCRATCH[n] = ("sbuf", [128, cols], dtype)
+        SCRATCH[n] = (where, [128] + (shape if isinstance(shape, list) else [shape]), dtype)
 
 
 _buf("int32", V0, "raw")
 _buf("int32", 64, "sti")
 _buf("int32", 8, "sgi coli")
+_buf("float32", V0, "tru")
+_buf("float16", V0, "hf")
 _buf("float32", F + WD, "mp0 mp1 rp1 rp2 rp3 cn")
-_buf("float32", 48, "soa soc col")
-_buf("float32", 8, "soh sfh")
-_buf("float32", 64, "ihp ihn mof32 c0 zer bb zz nxm k1 k2 gsc gsm sel ns gt ht clo cl2 ncm d0 d1 cd ee vn")
-_buf("float32", 128, "i32 i32n wh wn wc cl k0 vv")
-_buf("float32", 384, "rra rrb rrc dv")
-_buf("float32", 768, "vc")
-_buf("bfloat16", 64, "jm moff hh sgn")
-_buf("bfloat16", 128, "jd bd wv wt0 wdl we ib ibn wx ik w24")
-_buf("bfloat16", 256, "j64 ra ras tri1 tri2 hb yb xb0 xb1 xb2 xb3 xo")
-_buf("bfloat16", 512, "zb selb lc")
-_buf("bfloat16", 640, "ha hc ya yc xa xc")
-_buf("float16", 640, "pa pb pc")
-_buf("float16", 64, "ph sw tw ng")
-_buf("float16", 320, "eq eq2")
-_buf("uint16", 8, "l1 l2 l3")
-_buf("uint16", 64, "sa sc sb0 sb1 sb2 sb3 ltd dl nl no")
-for _b in range(8):
-    SCRATCH["ps%d" % _b] = ("psum", [128, 512], "float32")
+_buf("float32", 64, "so col gsc inc ns gt kd ks")
+_buf("float32", 96, "rca rcb rcc pat")
+_buf("float32", 128, "i32n wc wuz fn vcn")
+_buf("float32", 192, "kf")
+_buf("float32", 256, "cl yc zb")
+_buf("float32", 384, "dv")
+_buf("float32", 512, "vc za zc")
+_buf("float32", 224, "wz")
+_buf("bfloat16", 384, "wx")
+_buf("bfloat16", 64, "jm moff one sg7 ng cb xh")
+_buf("bfloat16", 128, "jd bd ib ibn ik ihp ihn i2p i2n wux wdt wtm wng wdf dge wav wst wtt ce")
+_buf("bfloat16", 192, "cf")
+_buf("bfloat16", 256, "j64 j256 ra ras tri1 xb0 xb1 xb2 xb3")
+_buf("bfloat16", 320, "tri2 eq eq2")
+_buf("bfloat16", 512, "zr xa xc")
+_buf("bfloat16", 1024, "xo")
+_buf("bfloat16", [4, 128], "selb lc")
+_buf("float16", 64, "rc1 gsm rct sg1 sg2 zz sw tw csg dd")
+_buf("float16", [35, 4], "r4a r4c")
+_buf("float16", [71, 2], "r2b")
+_buf("uint16", 64, "sa sc sb0 sb1 sb2 sb3 ltd dl no")
+_buf("float32", 512, "ps0 ps1 ps2 ps3 ps4 ps5 ps6 ps7", "psum")
 
 SEMAPHORES = ["cv", "ca", "cp", "cg"] + [p + str(i) for p in "mt" for i in range(28)] + ["d%d" % i for i in range(48)]
 BYTES = {"float32": 4, "int32": 4, "float16": 2, "bfloat16": 2, "uint16": 2}
 IO = ("recs", "st0", "cx0", "sg", "yp", "ys", "yx")
 
 
-def A(name, c0, c1, st=1, p0=0, p1=128):
-    return ("ap", name, p0, p1, 1, c0, c1, st)
+def A(name, c0, c1, st=1, p0=0, p1=128, ps=1):
+    return ("ap", name, (p0, p1, ps), (c0, c1, st))
+
+
+def A3(name, i, j, p1=128):
+    return ("ap", name, (0, p1, 1), i, j)
 
 
 def C(k):
@@ -63,13 +74,24 @@ def IND(win, off):
 def ncols(a):
     if a[0] == "ind":
         return 16 * ncols(a[2])
-    return len(range(a[5], a[6], a[7]))
+    n = 1
+    for d in a[3:]:
+        n *= len(range(*d)) if isinstance(d, tuple) else 1
+    return n
+
+
+def span(a):
+    ends = [(d[0], range(*d)[-1]) if isinstance(d, tuple) else (d, d) for d in a[3:]]
+    if len(ends) == 1:
+        return ends[0][0], ends[0][1] + 1
+    w = SCRATCH[a[1]][1][2]
+    return ends[0][0] * w + ends[1][0], ends[0][1] * w + ends[1][1] + 1
 
 
 def isz(a):
     if a[0] == "ind":
         a = a[1]
-    return 4 if a[1] in IO else BYTES[SCRATCH[a[1]][2]]
+    return (2 if a[1] in ("cx0", "yx") else 4) if a[1] in IO else BYTES[SCRATCH[a[1]][2]]
 
 
 def inps(a):
@@ -84,7 +106,7 @@ def cost(op, m):
             t += max(min(64, ncols(l)), ncols(r)) * (4 if isz(l) == 4 else 1) * m["pe"] + 5
         return t + m["fix"]
     if k in ("iota", "sel"):
-        return 250 + 2 * ncols(a[0]) * m["cyc"]
+        return 150 + 2 * ncols(a[0]) * m["cyc"]
     if k == "dma":
         return 60.0
     if k == "send":
@@ -138,11 +160,9 @@ def regions(op):
 
 def build():
     ops = []
-    NA, NB = OPT["na"], 256
-    NC = 1024 - NA - NB
 
     def put(q, k, *a):
-        ops.append({"q": q, "k": k, "a": a, "load": 0})
+        ops.append({"q": q, "k": k, "a": a, "load": 0, "after": []})
     ts = lambda out, i, s1, s2, o0, o1=None: put("v", "ts", out, i, s1, s2, o0, o1)
     tt = lambda out, i, j, o: put("v", "tt", out, i, j, o)
     cp = lambda out, i: put("v", "cp", out, i)
@@ -152,8 +172,7 @@ def build():
     mm = lambda lst: put("p", "mm", *lst)
     full = lambda n: A(n, 0, SCRATCH[n][1][1])
     half = lambda n, h, c=None: A(n, 0, c or SCRATCH[n][1][1], 1, 64 * h, 64 * h + 64)
-    pick = lambda out, pat, cmp, fill, base, cm: put("g", "sel", out, A("zb", 0, ncols(out), 1, out[2], out[3]), pat, cmp,
-                                                     fill, base, cm)
+    zero = lambda n: A("zr", 0, n)
     win = lambda n, w=W0: A(n, F, F + w)
     MP = [win("mp0")] + [win("mp1")] * 3
     HOME = [win("mp0"), win("rp1"), win("rp2"), win("rp3")]
@@ -162,252 +181,273 @@ def build():
 
     def dma(q, out, i):
         put(q, "dma", out, i)
-        load[0] += (out[3] - out[2]) * ncols(out) * (2 if out[1][0] == "x" or out[1] == "yx" else 4)
+        load[0] += len(range(*out[2])) * ncols(out) * isz(out)
         ops[-1]["load"] = load[0]
 
     def send(dst, src, step, ways):
         put("g", "send", dst, src, nsend[0], step % 4, [] if step % 4 == 2 and ways != [2, 3] else ways)
         nsend[0] += 1
 
-    hv = V0 // 4
+    np_ = OPT["pieces"]
+    hv = V0 // np_
     dma("s", A("sgi", 0, 1), A("sg", 0, 1))
     dma("a", full("sti"), A("st0", 0, 64))
-    for k in range(4):
+    for k in range(np_):
         dma("sa"[k % 2], A("raw", hv * k, hv * k + hv), A("recs", hv * k, hv * k + hv))
-        if k == 1:
+        if k == np_ // 2 - 1:
             dma("s", A("xb0", 0, NB), A("cx0", 0, NB))
-    dma("a", A("xa", 0, NA), A("cx0", NB + NC, 1024))
-    dma("s", A("xc", 0, NC), A("cx0", NB, NB + NC))
-    put("v", "ms", full("zb"), 0.0)
+    dma("a", A("xc", 0, NM), A("cx0", NB, NB + NM))
+    dma("s", A("xa", 64, 64 + NM), A("cx0", NB + NM, 1024))
+    put("v", "ms", full("zr"), 0.0)
     put("g", "iota", A("coli", 0, 1), [[0, 1]], 0, 1)
     put("g", "iota", full("jd"), [[1, 8], [0, 16]], 0, 0)
     put("g", "iota", full("jm"), [[0, 4], [1, 16]], 0, 0)
-    pick(IB, [[-1, 128]], OP.not_equal, 1.0, 0, 1)
+    put("g", "sel", IB, zero(128), [[-1, 128]], OP.not_equal, 1.0, 0, 1)
     put("g", "iota", full("j64"), [[1, 4], [0, 64]], 0, 0)
-    for h in range(2):
-        pick(half("tri1", h), [[0, 4], [1, 64]], OP.is_gt, 4096.0, 0, -1)
-        pick(half("ra", h), [[-16, 4], [0, 64]], OP.not_equal, 1.0, 0, 1)
-        pick(half("lc", h), [[-1, 4], [1, 8], [0, 16]], OP.not_equal, 1.0, -4 * h, 0)
-    pick(full("selb"), [[-16, 4], [-64, 2], [0, 64]], OP.not_equal, -1.0, 0, 1)
+    put("g", "iota", full("j256"), [[0, 4], [1, 64]], 0, 0)
     ci = lambda k: A("coli", k, k + 1)
     ts(ci(1), ci(0), 15, None, OP.bitwise_and)
     ts(ci(2), ci(0), 4, None, OP.arith_shift_right)
-    ts(ci(3), ci(0), 1, None, OP.bitwise_and)
+    ts(ci(3), ci(0), 63, None, OP.bitwise_and)
     ts(ci(4), ci(0), 4, 3, OP.arith_shift_right, OP.bitwise_and)
     cp(A("col", 0, 5), A("coli", 0, 5))
-    cp(C(5), A("sgi", 0, 1))
-    ts(A("col", 6, 8), A("jm", 12, 14), C(1), None, OP.is_equal)
-    ts(C(8), C(1), 12.0, None, OP.is_lt)
-    ts(C(9), C(1), 14.0, None, OP.is_ge)
+    SG, R12, R13, R14, R15, ST = C(5), C(6), C(7), C(8), C(9), C(10)
+    cp(SG, A("sgi", 0, 1))
+    ts(A("col", 6, 10), A("jm", 12, 16), C(1), None, OP.is_equal)
+    ts(ST, C(1), 12.0, None, OP.is_lt)
+    names = "xs xb xi c240 cm240 q25 lt14 rt rd rc ia r14e r12h cuz cux tneg tpos dgc cec spare d0 ck keep g4 h4".split()
+    K = {n: C(11 + i) for i, n in enumerate(names)}
+    lin(K["xs"], ST, 1.0 / 496)
+    lin(K["xb"], ST, 122.742, 1.0)
+    lin(K["xi"], ST, E - 1, 1.0)
+    lin(K["c240"], ST, E)
+    lin(K["cm240"], ST, -E)
+    lin(K["q25"], ST, -0.25)
+    lin(K["rt"], R12, 1.0, R13)
+    lin(K["lt14"], ST, 1.0, K["rt"])
+    lin(K["rd"], R12, -1.0, R13)
+    lin(K["rc"], R14, 1.0, R15)
+    lin(K["ia"], R14, -1.0, R15)
+    lin(K["r14e"], R14, E)
+    lin(K["r12h"], R12, 0.5)
+    lin(K["cec"], K["rt"], 4096.0, -8192.0)
+    lin(K["spare"], C(1), 1.0, float(W0))
+    lin(K["d0"], C(1), 0.0, 2.0 * (V0 - 1))
+    lin(K["g4"], C(2), 1.0, -4.0)
+    ts(K["h4"], C(2), C(4), None, OP.subtract)
+    ts(A("col", 40, 44), A("jm", 0, 4), K["h4"], None, OP.add)
+    for (n, s) in (("ia", 0.5), ("rc", 0.5)):
+        lin(C(44 if n == "ia" else 45), K[n], s)
     ts(full("bd"), full("jd"), C(2), None, OP.is_equal)
     ts(full("moff"), full("jm"), C(1), 4096.0, OP.not_equal, OP.mult)
-    ts(full("c0"), full("jm"), 0.0, 2000.0, OP.is_equal, OP.mult)
     ts(full("ras"), full("j64"), C(4), 2048.0, OP.is_equal, OP.mult)
-    lin(C(10), C(6), 1.0, C(7))
-    lin(C(11), C(6), -1.0, C(7))
-    lin(C(14), C(8), 0.5)
-    lin(C(15), C(8), -0.25)
-    lin(C(16), C(8), -0.25, C(10))
-    lin(C(17), C(8), 0.5, C(10))
-    lin(C(18), C(10), 0.25, -0.25)
-    lin(C(19), C(10), -1.0)
-    lin(C(20), C(9), 0.5)
-    lin(C(21), C(9), -1.0)
-    lin(C(23), C(5), -1.0)
-    lin(C(24), C(3), -1.0, 0.5)
-    lin(C(25), C(8), -1.0e6, C(24))
-    lin(C(26), C(1), 1.0, float(W0))
-    lin(C(27), C(1), 0.0, float(V0 - 1))
-    lin(C(29), C(16), 1.0, 128.0)
-    bd8 = A("bd", 0, 128, 16)
+    ts(full("ra"), full("j64"), C(4), 1.0 / 16, OP.is_equal, OP.mult)
+    for h in range(2):
+        ts(A3("selb", (0, 4, 1), (64 * h, 64 * h + 64, 1)), full("j64"), K["g4"] if h else C(2), -1.0 / 16,
+           OP.is_equal, OP.mult)
+    for k in range(4):
+        ts(A3("lc", k, (0, 128, 1)), full("jd"), C(40 + k), 32768.0, OP.is_equal, OP.mult)
+    ts(full("tri1"), full("j256"), C(3), 0.5, OP.is_le, OP.mult)
+    ts(A("tri2", 0, 256), full("tri1"), -57343.0, 28672.0, OP.mult, OP.add)
+    put("v", "ms", A("tri2", 256, 320), 0.0)
+    put("v", "ms", full("one"), 1.0)
+    put("v", "ms", full("pat"), -1.0)
+    put("v", "ms", A("pat", 0, 96, 3), 0.0)
+    put("v", "ms", full("cl"), 0.0)
+    put("v", "ms", A("cl", 128, 256, 32), 3000.0)
+    ts(A("cl", 0, 128, 16), A("jd", 0, 128, 16), 16.0, K["spare"], OP.mult, OP.add)
+    for n in ("r4a", "r4c", "r2b"):
+        lin(A3(n, (0, SCRATCH[n][1][1], 1), (0, SCRATCH[n][1][2], 1)), zero(SCRATCH[n][1][1] * SCRATCH[n][1][2]), 1.0)
+    for k in range(4):
+        put("v", "ms", A("cn", 430 * k, 430 * k + 430), 0.0)
+    bd8, BD = A("bd", 0, 128, 16), full("bd")
+    lin(K["tpos"], R13, 1.0 / 4096)
+    lin(K["tneg"], R12, -1.0 / 4096)
 
     def weights(v, sign):
-        lin(C(32 + 2 * v), sign, KV, C(11))
-        lin(C(33 + 2 * v), sign, KV)
-        for s, c in enumerate((19, 32 + 2 * v, 33 + 2 * v)):
-            lin(A("w24", 32 * v + 8 * s, 32 * v + 8 * s + 8), bd8, C(c))
-    weights(0, C(5))
-    for n, c in (("wv", 5), ("wt0", 6), ("wdl", 11), ("wc", 9)):
-        lin(full(n), full("bd"), C(c))
-    for n, c in (("wx", C(14)), ("i32", 1.0), ("ik", 16384.0), ("i32n", -1.0), ("ibn", -1.0), ("wh", C(20)), ("wn", C(21))):
+        lin(C(48 + 2 * v), sign, -1.0, K["r14e"])
+        lin(C(49 + 2 * v), sign, E, K["r12h"])
+        lin(A("wz", 56 * v + 4, 56 * v + 51, 6), bd8, C(48 + 2 * v))
+        lin(A("wx", 96 * v + 1, 96 * v + 48, 6), bd8, C(49 + 2 * v))
+    lin(full("wz"), zero(224), 1.0)
+    lin(full("wx"), zero(384), 1.0)
+    for v in range(4):
+        ts(A("wz", 56 * v + 3, 56 * v + 51, 6), bd8, K["tpos"], None, OP.mult)
+        ts(A("wz", 56 * v + 5, 56 * v + 51, 6), bd8, K["tneg"], None, OP.mult)
+    weights(0, SG)
+    lin(full("wst"), IB, K["lt14"])
+    lin(A("wst", 14, 128, 16), bd8, SG)
+    lin(K["cuz"], C(48), -1.0)
+    lin(K["cux"], C(49), -1.0)
+    lin(K["dgc"], K["rd"], 2048.0)
+    lin(C(46), K["rd"], 0.5)
+    lin(C(47), K["rt"], 0.5)
+    lin(C(56), K["rc"], -1.0)
+    lin(C(57), ST, 0.5)
+    for n, c in (("wuz", K["cuz"]), ("wux", K["cux"]), ("wdt", C(46)), ("wtm", C(47)), ("wc", C(56)), ("wng", 8192.0),
+                 ("wdf", 2048.0)):
+        lin(full(n), BD, c)
+    for n, c in (("i32n", -1.0), ("ibn", -1.0), ("ik", 16384.0), ("ihp", 0.5), ("ihn", -0.5), ("i2p", 2048.0),
+                 ("i2n", -2048.0), ("dge", K["dgc"]), ("wav", C(57)), ("wtt", K["rt"])):
         lin(full(n), IB, c)
-    lin(full("ihp"), A("ib", 0, 64), 0.5)
-    lin(full("ihn"), A("ib", 0, 64), -0.5)
-    lin(full("mof32"), full("moff"), 1.0)
-    lin(full("tri2"), full("tri1"), 1.0, -30720.0)
-    lin(A("mp0", 0, F), A("zb", 0, F), 1.0, C(5))
-    lin(A("mp0", F + V0, F + W0), A("zb", 0, W0 - V0), 1.0)
+    lin(A("ce", 0, 64), full("moff"), 1.0, 2048.0)
+    lin(A("ce", 64, 128), zero(64), 1.0, K["cec"])
+    lin(A("cf", 0, 64), full("moff"), 1.0, 2048.0)
+    lin(A("cf", 64, 192, 2), full("moff"), 1.0, 2048.0)
+    lin(A("cf", 65, 192, 2), full("moff"), 1.0, 4096.0)
+    lin(full("cb"), zero(64), 1.0, K["c240"])
+    mm([(A("ps3", 0, 8), full("wst"), A("cb", 0, 8), True, True)])
+    lin(C(58), R14, -1.0)
+    lin(K["ck"], A("ps3", 0, 1), C(58))
+    lin(A("mp0", 0, F), zero(F), 1.0, SG)
+    lin(A("mp0", F + V0, F + W0), zero(W0 - V0), 1.0, K["c240"])
     for v in range(1, 4):
-        lin(A("rp%d" % v, F + V0 + 64 * (v - 1), F + W0), A("zb", 0, W0 - V0 - 64 * (v - 1)), 1.0)
+        lin(A("rp%d" % v, F + V0 + 64 * (v - 1), F + W0), zero(W0 - V0 - 64 * (v - 1)), 1.0, K["c240"])
+    for k in range(np_):
+        c0, c1 = hv * k, hv * k + hv
+        o = A("ps%d" % (4 + k % 4), hv * (k // 4), hv * (k // 4) + hv)
+        cp(A("hf", c0, c1), A("raw", c0, c1))
+        mm([(o, full("wst"), A("hf", c0, c1), True, True)])
+        lin(A("mp0", F + c0, F + c1), o, 1.0, K["c240"])
     for k in range(4):
-        lin(A("cn", F + 396 * k, F + 396 * k + 396), A("zb", 0, 396), 1.0)
-    lin(full("zer"), A("zb", 0, 64), 1.0)
-    lin(full("we"), A("zb", 0, 128), 1.0)
-    for k in range(12, 16):
-        lin(A("we", k, 128, 16), bd8, C(23 if k % 2 else 5))
-    lin(full("cl"), A("zb", 0, 128), 1.0)
-    lin(A("cl", 0, 128, 16), A("jd", 0, 128, 16), 16.0, C(26))
-    for k in range(4):
-        cp(A("mp0", F + hv * k, F + hv * k + hv), A("raw", hv * k, hv * k + hv))
+        cp(A("tru", 332 * k, 332 * k + 332), A("raw", 332 * k, 332 * k + 332))
     load[0] = 0
-    for g in range(8):
-        dma("s", A("cn", F, F + V0, 1, 16 * g + 14, 16 * g + 16), A("mp0", F, F + V0, 1, 16 * g + 14, 16 * g + 16))
-    cp(A("sb0", 0, NB // 16), A("sti", 0, NB // 16))
-    cp(A("sc", 0, NC // 16), A("sti", NB // 16, (NB + NC) // 16))
-    cp(A("sa", 0, NA // 16), A("sti", (NB + NC) // 16, 64))
-    for (n, i, j) in (("xb0", 0, 64), ("xb0", 64, NB), ("xa", 0, NA), ("xc", 0, NC)):
-        lin(A(n, i, j), A(n, i, j), 1.0, C(10))
+    for r in (14, 15):
+        dma("s", A("cn", F, F + V0, 1, r, 128, 16), A("tru", 0, V0, 1, r, 128, 16))
+    cp(A("sb0", 0, 16), A("sti", 0, 16))
+    cp(A("sc", 0, 24), A("sti", 16, 40))
+    cp(A("sa", 4 + 4, 32), A("sti", 40, 64))
+    for (n, i, j) in (("xb0", 0, NB), ("xc", 0, NM), ("xa", 64, 64 + NM)):
+        lin(A(n, i, j), A(n, i, j), 1.0, K["xi"])
 
-    def xstep(w, X, XO, H, Y, off, n, bank, last, mode):
-        if mode == "G":
-            def both():
-                tt(A(H, 0, n), IND(w, off), X, OP.add)
-                lin(A(Y, 0, n), A(H, 0, n), C(14), C(29))
-                lin(XO, A(Y, 0, n), 1.0, -128.0)
-            return [], [], both
-        lin(A(H, 0, n), IND(w, off), C(14), C(15 if last else 16))
-        o = A(bank[0], bank[1], bank[1] + n)
+    P3 = lambda k: A("ps3", 64 * k, 64 * k + 64)
 
-        def rnd():
-            if mode == "V":
-                ts(XO, o, MAGIC, MAGIC, OP.add, OP.subtract)
-            else:
-                lin(A(Y, 0, n), o, 1.0, 128.0)
-                ts(XO, A(Y, 0, n), -128.0, None, OP.add)
-        return [(o, full("wx"), X, True, False)], [(o, IB, A(H, 0, n), False, True)], rnd
+    def step(c, w, wk, X, S, outs, side=None):
+        n = ncols(X)
+        kk = 2 if n <= 256 else 4
+        aa, mp, m = 16 // kk, n // kk, n // 16
+        bank, z, rc, r = "ps" + str("acb".index(c)), "z" + c, "rc" + c, "r%d%s" % (kk, c)
+        x0 = X[3][0]
+        xk = lambda k: A(X[1], x0 + k, x0 + n, kk)
+        if side:
+            rec, sgn, res = side
+            lin(full(rec), IND(w, A(S[1], S[3][0], S[3][0] + 4)), 1.0)
+            mm([(P3(0), full("wdt"), full(rec), True, True), (P3(1), full("wtm"), full(rec), True, True),
+                (P3(2), full("wux"), A(X[1], x0, x0 + 64), True, False)])
+        at = lambda k: 48 * (k // 2) + 3 * (k % 2) + 1
+        mm([(A(bank, 0, 24 * kk, 1, 0, mp), xk(0), A("wx", 96 * wk, 96 * wk + 24 * kk), True, False)]
+           + [(A(bank, at(k), at(k) + 43, 6, 0, mp), xk(k), A("wx", 96 * wk + 1, 96 * wk + 48, 6), False, False)
+              for k in range(1, kk)])
+        tt(A(z, 0, n), IND(w, S), X, OP.mult)
+        if side:
+            mm([(P3(2), full("wuz"), A(z, 0, 64), False, True)])
+            act(full(sgn), P3(2), AF.Sign, 0.0, 1.0)
+        mm([(A(bank, 48 * (k // 2), 48 * (k // 2) + 48, 1, 0, mp), A(z, k, n, kk),
+             A("wz", 56 * wk + 3 - 3 * (k % 2), 56 * wk + 51 - 3 * (k % 2)), False, k == kk - 1) for k in range(kk)])
+        lin(X, A(z, 0, n), K["xs"], K["xb"])
+        if side:
+            tt(full("zz"), P3(0), full(sgn), OP.mult)
+            tt(full(res), P3(1), full("zz"), OP.add)
+        scan(A(rc, 0, 24 * kk, 1, 0, mp), A("pat", 0, 24 * kk, 1, 0, mp), A(bank, 0, 24 * kk, 1, 0, mp), 0.0,
+             OP.mult, OP.max)
+        for h in range(kk // 2):
+            act(A3(r, (aa - 1, aa - 1 + 8 * aa, aa), (2 * h, 2 * h + 2, 1), mp), A(rc, 48 * h + 2, 48 * h + 48, 3, 0, mp),
+                AF.Abs, 0.0, 4096.0)
+        mm([(A(bank, 128, 128 + m), A3(r, (aa - 1 - a, aa - 1 - a + 128 // kk, 1), (0, kk, 1), mp),
+             A("ib", a, mp, aa, 0, mp), a == 0, a == aa - 1) for a in range(aa)])
+        for (out, i, j) in outs:
+            (cp if isz(out) == 2 else lambda o, p: lin(o, p, 1.0))(out, A(bank, 128 + i, 128 + j))
 
-    def bulk_step(c, v, step):
-        n = {"a": NA + 64 * v, "b": NB - 64 - 64 * v, "c": NC}[c]
-        o = 64 if c == "b" else 0
-        m = n // 16
-        tag, w, wk = ("b%d" % v, MP[v], 0) if c == "b" else (c, HOME[v], 32 * v)
-        X = A("x" + tag, o, o + n)
-        S = A("s" + tag, o // 16, o // 16 + m)
-        last = v == 3 and step == 2
-        bs, bx = {"a": ("ps0", "ps2"), "c": ("ps1", "ps3"), "b": ("ps4", None)}[c]
-        P, R = "p" + c, "rr" + c
-        m1, m2, rnd = xstep(w, X, X, "h" + c, "y" + c, S, n, (bx, 0), last, OPT[c])
-        if m1:
-            mm(m1)
-        tt(A(P, 0, n), IND(w, S), X, OP.mult)
-        if not m1:
-            rnd()
-        mm([(A(bs, k, 384, 16, 0, m), A(P, k, n, 16), A("w24", wk, wk + 24), True, True) for k in range(16)])
-        act(A(R, 0, 384, 1, 0, m), A(bs, 0, 384, 1, 0, m), AF.Abs, -2048.0, 1.0)
-        if m2:
-            mm(m2)
-        o3 = A(bs, 384, 384 + m)
-        mm([(o3, A(R, 128 * s, 128 * s + 128, 1, 0, m), A("ihn" if s == 2 else "ihp", 0, m, 1, 0, m), s == 0, s == 2)
-            for s in range(3)])
-        ts(A("so" + c, 0, m) if last else S, o3, -1024.0, None, OP.add)
-        if m1:
-            rnd()
+    def home(c, v):
+        lo, hi = {"a": (64 if v == 0 else 0, 448 + (64 if v == 3 else 0)), "c": (0, NM + (64 if v > 1 else 0))}[c]
+        o = 4 if c == "a" else 0
+        S = A("s" + c, o + lo // 16, o + hi // 16)
+        for s in range(3):
+            outs = [(S, 0, (hi - lo) // 16)]
+            if v == 3 and s == 2:
+                outs = {"a": [(A("so", 0, 4), 0, 4), (A("so", 40, 64), 4, 28), (A("so", 8, 12), 28, 32)],
+                        "c": [(A("so", 16, 40), 0, 24), (A("so", 4, 8), 24, 28)]}[c]
+            step(c, HOME[v], v, A("x" + c, lo, hi), S, outs)
 
-    def trained(v):
-        return A("xa", NA, NA + 64) if v == 0 else A("xo", 64 * v, 64 * v + 64)
+    D, DF = A("ps4", 0, 256), A("ps4", 256, 320)
+    Q, PG, SD = A("ps5", 0, 64), A("ps5", 64, 128), A("ps5", 128, 192)
 
-    def head_step(v, step):
-        X = A("xb%d" % v, 0, 64)
-        S = (A("sb%d" % v, 0, 4), A("l1", 0, 4), A("l2", 0, 4))[step]
-        m1, m2, rnd = xstep(MP[v], X, trained(v) if step == 2 else X, "hh", None, S, 64, ("ps5", 256),
-                            v == 3 and step == 2, "V")
-        P = full("ph")
-        tt(P, IND(MP[v], S), X, OP.mult)
-        r = lambda k: A("ps5", 64 * k, 64 * k + 64)
-        lst = [(r(2), IB, full("moff"), True, False), (r(2), full("wt0"), P, False, True),
-               (r(0), full("wv"), P, True, True), (r(1), full("wdl"), P, True, True)]
-        if step > 0:
-            lst.append((r(3), full("wt0"), P, True, True))
-        mm(lst)
-        ts(full("bb"), r(0), 0.0, None, OP.is_gt)
-        tt(full("zz"), full("bb"), r(1), OP.mult)
-        tt(full("nxm"), full("zz"), r(2), OP.add)
-        if step > 0:
-            tt(full("sw" if step == 1 else "tw"), full("zz"), r(3), OP.add)
-        mm(m1 + m2)
-        scan(A("k0", 0, 64), full("c0"), full("nxm"), 0.0, OP.max, OP.min)
-        cp(A("l%d" % (step + 1), 0, 4), A("k0", 15, 64, 16))
-        rnd()
+    def pairs(w, start):
+        lst = [(DF, full("ibn"), full(w), True, False)] if start else []
+        lst += [(half("ps4", h, 256), half(w, h), half("ra", h), False, False) for h in range(2)]
+        return lst + [(A("ps4", 64 * k, 64 * k + 64), A3("selb", k, (0, 128, 1)), full(w), False, k == 3) for k in range(4)]
 
-    D, DF = A("ps6", 0, 256), A("ps6", 256, 320)
-
-    def pairs(w):
-        lst = [(half("ps6", h, 256), half(w, h), half("ra", h), False, False) for h in range(2)]
-        return lst + [(A("ps6", 64 * k, 64 * k + 64), A("selb", 128 * k, 128 * k + 128), full(w), False, k == 3)
-                      for k in range(4)]
-
-    def counts(out, e, start, stop):
-        return [(out, A("lc", 128 * k, 128 * k + 128), A(e, 64 * k, 64 * k + 64), start and k == 0, stop and k == 3)
-                for k in range(4)]
+    def counts(out, e, stop):
+        return [(out, A3("lc", k, (0, 128, 1)), A(e, 64 * k, 64 * k + 64), False, stop and k == 3) for k in range(4)]
 
     LT = lambda v, i, j: A("ltd", 16 * v + i, 16 * v + j)
-    VC = lambda v, i, j: A("vc", 192 * v + i, 192 * v + j)
+    VC = lambda v, i, j: A("vc", 128 * v + i, 128 * v + j)
+    L = lambda v, s: A("sb%d" % v, 16 * s, 16 * s + 4)
 
     def stage1(v):
-        mm([(D, IB, full("tri1"), True, False)] + pairs("sw"))
-        ts(A("eq", 0, 256), D, 0.0, 4096.0, OP.is_equal, OP.mult)
-        sd = A("ps6", 320, 384)
-        mm([(sd, IB, full("moff"), True, False), (sd, IB, full("sw"), False, False)] + counts(sd, "eq", False, True))
-        ts(full("ng"), sd, 2000.0, None, OP.is_gt)
-        scan(full("k1"), A("cl", 0, 64), sd, 0.0, OP.max, OP.min)
-        cp(LT(v, 8, 12), A("k1", 15, 64, 16))
-        mm([(D, IB, full("tri2"), True, False)]
-           + [(half("ps6", h, 256), half("ng", h), half("ras", h), False, False) for h in range(2)])
-        lin(full("gsc"), IND(CN, A("l2", 0, 4)), 1.0)
-        act(full("sgn"), full("gsc"), AF.Sign, -6.5, 1.0)
-        lin(full("gsm"), IND(MP[v], A("l2", 0, 4)), 1.0)
-        pg = A("ps7", 128, 192)
-        mm([(pg, full("i32n"), full("gsc"), True, False), (pg, full("ik"), full("sgn"), False, True)])
+        mm(pairs("sw", True))
+        tt(A("eq", 0, 256), D, full("tri1"), OP.is_equal)
+        mm([(SD, IB, full("moff"), True, False), (SD, IB, full("sw"), False, False)] + counts(SD, "eq", True))
+        act(full("ng"), SD, AF.Sign, -2000.0, 1.0)
+        mm([(DF, full("ibn"), full("sw"), True, False)]
+           + [(half("ps4", h, 256), half("ng", h), half("ras", h), False, False) for h in range(2)])
+        scan(full("ks"), A("cl", 64, 128), SD, 0.0, OP.max, OP.min)
+        cp(LT(v, 8, 12), A("ks", 15, 64, 16))
+        lin(full("gsc"), IND(CN, L(v, 2)), 1.0)
+        act(full("sg7"), full("gsc"), AF.Sign, -6.5, 1.0)
+        mm([(PG, full("i32n"), full("gsc"), True, False), (PG, full("ik"), full("sg7"), False, True)])
 
     def train(v):
-        e, q = A("ps7", 0, 64), A("ps7", 64, 128)
-        mm(counts(e, "eq", True, False) + [(e, full("we"), full("ph"), False, True)])
-        ts(full("sel"), e, C(25), None, OP.is_lt)
-        tt(IND(win("cn", WD), LT(v, 8, 12)), full("gsc"), full("sel"), OP.add)
-        tt(full("ns"), full("sel"), A("ps7", 128, 192), OP.mult)
-        mm(pairs("tw") + [(DF, IB, full("tw"), True, False), (DF, full("ibn"), full("sw"), False, True)])
-        ts(full("eq2"), A("ps6", 0, 320), 0.0, -32768.0, OP.is_equal, OP.mult)
-        mm([(q, full("wc"), full("ns"), True, False)])
-        if OPT["gt"] == "v":
-            cp(full("gt"), IND(CN, A("l3", 0, 4)))
-        else:
-            lin(full("gt"), IND(CN, A("l3", 0, 4)), 1.0)
-        mm([(q, full("wt0"), A("eq2", 256, 320), False, False)] + counts(q, "eq2", False, False)
-           + [(q, full("wc"), full("gt"), False, True)])
-        lin(full("ht"), IND(MP[v], A("l3", 0, 4)), C(17), C(18))
-        ts(full("clo"), q, 16384.0 + 13, None, OP.is_ge)
-        ts(full("cl2"), q, 16384.0 + 13, 4096.0, OP.is_lt, OP.mult)
-        vt, vd = A("ps7", 192, 256), A("ps7", 256, 320)
-        mm([(vd, full("i32"), full("ht"), True, False), (vd, full("wx"), trained(v), False, False),
-            (vd, full("wh"), full("gt"), False, True),
-            (vt, full("wn"), full("ht"), True, False), (vt, full("wh"), full("gt"), False, True)])
-        dn = "d%d" % (v % 2)
-        scan(full(dn), full("clo"), full("zer"), C(27) if v == 0 else A("d%d" % (1 - v % 2), 63, 64), OP.add, OP.add)
-        tt(full("ncm"), full("cl2"), full("mof32"), OP.add)
-        tt(A("vv", 64, 128), full(dn), full("ncm"), OP.add)
-        tt(A("vv", 0, 64), full("nxm"), full("cl2"), OP.add)
-        tt(full("cd"), full("clo"), full(dn), OP.mult)
-        scan(full("k0"), full("cl"), full("vv"), 0.0, OP.max, OP.min)
-        tt(full("ee"), full("cd"), full("sel"), OP.mult)
-        cp(LT(v, 0, 8), A("k0", 15, 128, 16))
-        ts(VC(v, 0, 128), A("ps7", 192, 320), MAGIC, MAGIC, OP.add, OP.subtract)
-        tt(VC(v, 128, 192), full("gsm"), full("ee"), OP.max)
-        cp(IND(win("mp1", WD), LT(v, 4, 12)), VC(v, 64, 192))
-        tt(full("vn"), full("nxm"), full("cd"), OP.max)
-        scan(full("k2"), full("c0"), full("vn"), 0.0, OP.max, OP.min)
-        tail = A("sa", NA // 16 + 4 * v, NA // 16 + 4 * v + 4)
-        cp((tail, A("no", 8, 12), A("no", 16, 20), A("soh", 0, 4))[v], A("k2", 15, 64, 16))
-        cp(IND(win("cn", WD), LT(v, 0, 8)), VC(v, 0, 128))
+        xt = A("xb%d" % v, 0, 64)
+        vd, ee = A("ps6", 0, 64), A("ps6", 64, 128)
+        vt, ve, vo = A("ps7", 0, 64), A("ps7", 64, 192, 2), A("ps7", 65, 192, 2)
+        lin(full("inc"), full("sg2"), C(44), C(45))
+        tt(IND(win("cn", WD), LT(v, 8, 12)), full("gsc"), full("inc"), OP.add)
+        mm([(DF, IB, full("tw"), False, False)] + pairs("tw", False))
+        tt(full("ns"), PG, full("inc"), OP.mult)
+        tt(full("eq2"), A("ps4", 0, 320), full("tri2"), OP.is_equal)
+        mm([(Q, full("wng"), full("ng"), True, False), (Q, full("wc"), full("ns"), False, False)])
+        mm([(A("ps6", 0, 128), IB, full("ce"), True, False), (ee, full("dge"), full("sg2"), False, False)])
+        mm([(A("ps7", 0, 192), IB, full("cf"), True, False), (vt, IB, full("tw"), False, False),
+            (ve, full("ibn"), full("tw"), False, False)])
+        lin(full("gt"), IND(CN, L(v, 3)), 1.0)
+        lin(full("rct"), IND(MP[v], L(v, 3)), 1.0)
+        mm([(Q, full("wdf"), A("eq2", 256, 320), False, False)] + counts(Q, "eq2", False))
+        mm([(Q, full("wc"), full("gt"), False, True)])
+        act(full("csg"), Q, AF.Sign, 98291.5, -1.0)
+        mm([(P3(3), full("wav"), xt, True, False), (P3(3), full("wav"), full("rct"), False, True)])
+        lin(full("cb"), P3(3), 1.0, K["q25"])
+        mm([(P3(4), full("wtt"), full("rct"), True, False), (P3(4), full("wst"), full("cb"), False, True)])
+        lin(VC(v, 0, 64), P3(4), 1.0, K["ck"])
+        scan(full("dd"), full("csg"), full("one"), K["d0"] if v == 0 else K["keep"], OP.add, OP.add)
+        mm([(vd, full("i2n"), full("csg"), False, False), (ee, full("i2p"), full("csg"), False, False)])
+        mm([(vd, full("ihp"), full("dd"), False, False), (ee, full("ihp"), full("dd"), False, True)])
+        scan(full("kd"), A("cl", 0, 64), vd, 0.0, OP.max, OP.min)
+        cp(LT(v, 4, 8), A("kd", 15, 64, 16))
+        tt(VC(v, 64, 128), ee, full("gsm"), OP.max)
+        cp(IND(win("mp1", WD), LT(v, 4, 12)), VC(v, 0, 128))
+        mm([(vt, full("i2n"), full("csg"), False, False), (vo, full("i2n"), full("csg"), False, False),
+            (vo, full("ihn"), full("dd"), False, True)])
+        scan(full("kf"), A("cl", 64, 256), A("ps7", 0, 192), 0.0, OP.max, OP.min)
+        new = (A("sa", 4, 8), A("no", 8, 12), A("no", 16, 20), A("ks", 0, 4))[v]
         if v < 3:
-            send(A("dv", 128 * v, 128 * v + 128), VC(v, 64, 192), -(v + 1), [0, 1])
+            ts(new, A("kf", 95, 192, 32), -1.0, 2048.0, OP.mult, OP.add)
+            lin(K["keep"], A("dd", 63, 64), 1.0)
+        else:
+            lin(new, A("kf", 95, 192, 32), -1.0, 2048.0)
+        cp(LT(v, 0, 4), A("kf", 15, 64, 16))
+        lin(A("fn", 0, 64), full("gt"), 0.5 + 2.0 ** -15, MAGIC)
+        lin(A("fn", 64, 128), full("gt"), 0.5 - 2.0 ** -15, MAGIC)
+        lin(full("vcn"), full("fn"), 1.0, -MAGIC)
+        cp(IND(win("cn", WD), LT(v, 0, 8)), full("vcn"))
+        if v < 3:
+            send(A("dv", 128 * v, 128 * v + 128), VC(v, 0, 128), -(v + 1), [0, 1])
             send(A("dl", 8 * v, 8 * v + 8), LT(v, 4, 12), -(v + 1), [1])
-        if v > 0:
-            send(A("xa", NA + 64 * v, NA + 64 * v + 64), trained(v), -v, [0])
-        if v in (1, 2):
-            send(A("nl", 8 * v, 8 * v + 4), A("no", 8 * v, 8 * v + 4), -v, [1])
-            cp(tail, A("nl", 8 * v, 8 * v + 4))
-        if v == 3:
-            send(A("sfh", 0, 4), A("soh", 0, 4), -v, [1])
+        if v == 0:
+            lin(A("xa", 0, 64), xt, 1.0)
+        else:
+            send((A("xc", NM, NM + 64), A("xa", 448, 512), full("xh"))[v - 1], xt, -v, [0])
+            send((A("sc", 24, 28), A("sa", 32, 36), A("so", 12, 16))[v - 1], new, -v, [1])
 
     def base(v):
         n = (F + V0 + 64 * (v - 1)) // 2
@@ -420,58 +460,66 @@ def build():
     load[0] = 0
     dma("s", A("mp1", 0, F + W0), A("mp0", 0, F + W0))
     for v in range(4):
-        for step in range(3):
-            head_step(v, step)
-            if step == 1:
+        n = NB - 64 * v
+        for s in range(3):
+            S = lambda s: A("sb%d" % v, 16 * s, 16 * s + n // 16)
+            step("b", MP[v], 0, A("xb%d" % v, 0, n), S(s), [(S(s + 1), 0, n // 16)],
+                 (None, ("rc1", "sg1", "sw"), ("gsm", "sg2", "tw"))[s])
+            if s == 1:
                 stage1(v)
         if v < 3:
-            for step in range(3):
-                bulk_step("b", v, step)
-            n = NB - 64 - 64 * v
-            send(A("xb%d" % (v + 1), 0, n), A("xb%d" % v, 64, 64 + n), 1, [0, 1])
-            send(A("sb%d" % (v + 1), 0, n // 16), A("sb%d" % v, 4, 4 + n // 16), 1, [1])
+            send(A("xb%d" % (v + 1), 0, n - 64), A("xb%d" % v, 64, n), 1, [0, 1])
+            send(A("sb%d" % (v + 1), 0, n // 16 - 4), A("sb%d" % v, 52, 48 + n // 16), 1, [1])
         if v > 0:
             cp(IND(win("rp%d" % v, WD), A("dl", 8 * v - 8, 8 * v)), A("dv", 128 * v - 128, 128 * v))
         for c in "ca":
-            for step in range(3):
-                bulk_step(c, v, step)
+            home(c, v)
         train(v)
         if v < 2:
             base(v + 2)
+        if v == 2:
+            last = len(ops) - 1
+            load[0] = 0
+            for g in range(8):
+                dma("s", A("yp", 0, V0, 1, 16 * g, 16 * g + 12), A("tru", 0, V0, 1, 16 * g, 16 * g + 12))
+                ops[-1]["after"] = [last]
     load[0] = 0
+    lin(full("yc"), A("mp1", F + V0, F + W0), 1.0, K["cm240"])
+    for r in (12, 13):
+        dma("s", A("yp", 0, V0, 1, r, 128, 16), A("mp1", F, F + V0, 1, r, 128, 16))
     for g in range(8):
-        dma("s", A("yp", 0, W0, 1, 16 * g, 16 * g + 14), A("mp1", F, F + W0, 1, 16 * g, 16 * g + 14))
-    for g in range(8):
-        dma("s", A("yp", 0, W0, 1, 16 * g + 14, 16 * g + 16), A("cn", F, F + W0, 1, 16 * g + 14, 16 * g + 16))
+        dma("sa"[g % 2], A("yp", V0, W0, 1, 16 * g, 16 * g + 14), A("yc", 0, 256, 1, 16 * g, 16 * g + 14))
+    for r in (14, 15):
+        dma("s", A("yp", 0, W0, 1, r, 128, 16), A("cn", F, F + W0, 1, r, 128, 16))
     load[0] = 0
-    dma("s", A("yx", NB, NB + NC), A("xc", 0, NC))
-    dma("s", A("ys", NB // 16, (NB + NC) // 16), A("soc", 0, NC // 16))
+    for (o, n, i, j) in ((192, "xh", 0, 64), (256, "xc", 0, NM), (64, "xc", NM, NM + 64), (0, "xa", 0, 64),
+                         (640, "xa", 64, 448), (128, "xa", 448, 512)):
+        lin(A("xo", o, o + j - i), A(n, i, j), ST, K["cm240"])
+    dma("s", A("yx", 0, 1024), full("xo"))
     load[0] = 0
-    dma("s", A("yx", NB + NC, 1024), A("xa", 0, NA))
-    dma("a", A("yx", 0, 256), A("xa", NA, NA + 256))
-    dma("s", A("ys", (NB + NC) // 16, 64), A("soa", 0, NA // 16))
-    dma("a", A("ys", 0, 12), A("soa", NA // 16, NA // 16 + 12))
-    dma("a", A("ys", 12, 16), A("sfh", 0, 4))
+    dma("s", A("ys", 0, 64), full("so"))
 
     hist = {}
     for i, op in enumerate(ops):
         rd, wr = regions(op)
-        dep, land = set(), set()
+        dep, land = set(op["after"]), set()
         for lst, w in ((rd, False), (wr, True)):
             for r in lst:
                 if r[1] in IO:
                     continue
-                for (j, r2, w2) in hist.get(r[1], []):
+                lo, hi = span(r)
+                for (j, r2, w2, lo2, hi2) in hist.get(r[1], []):
                     if inps(r):
                         if ops[j]["q"] != op["q"] or op["q"] == "p":
                             dep.add(j)
-                    elif (w or w2) and r[5] < r2[6] and r2[5] < r[6] and r[2] < r2[3] and r2[2] < r[3]:
+                    elif (w or w2) and lo < hi2 and lo2 < hi and r[2][0] < r2[2][1] and r2[2][0] < r[2][1]:
                         dep.add(j)
                         if w2:
                             land.add(j)
         for lst, w in ((rd, False), (wr, True)):
             for r in lst:
-                hist.setdefault(r[1], []).append((i, r, w))
+                if r[1] not in IO:
+                    hist.setdefault(r[1], []).append((i, r, w) + span(r))
         op["dep"] = sorted(dep)
         op["left"] = set(j for j in dep if ops[j]["k"] == "send" and j not in land)
     return ops
@@ -582,8 +630,8 @@ def bits(engines):
 
 
 def piece(a, h, k):
-    n = (a[6] - a[5]) // k
-    return A(a[1], a[5] + h * n, a[5] + h * n + n)
+    n = (a[3][1] - a[3][0]) // k
+    return A(a[1], a[3][0] + h * n, a[3][0] + h * n + n)
 
 
 def rank_program(g, core, T, topo):
@@ -596,7 +644,7 @@ def rank_program(g, core, T, topo):
             return a
         if a[0] == "ind":
             return ap(a[1]).indirect(ap(a[2]))
-        return T[a[1]][slice(a[2], a[3]), slice(a[5], a[6], a[7] if a[7] != 1 else None)]
+        return T[a[1]][tuple(slice(d[0], d[1], d[2] if d[2] != 1 else None) if isinstance(d, tuple) else d for d in a[2:])]
 
     if rank is None:
         for r in range(nr):
@@ -639,8 +687,6 @@ def rank_program(g, core, T, topo):
                 continue
             s, val = gone[j] if j in op["left"] else token[j]
             need[s] = max(need.get(s, 0), val)
-        if k == "send":
-            need = {s: need[s] for s in need}
         if k in ("iota", "sel") and "cg" in count:
             need["cg"] = count["cg"]
         for s in need:

@@ -8,10 +8,11 @@ F = 8
 E = 240.0
 MAGIC = 12582912.0
 NM, NB = 384, 256
-OPT = {"pieces": 8, "iters": 4000, "seed": 1}
-MODEL = {"cyc": 0.95, "pe": 0.48, "g": 1.56, "s": 3.5, "h": 100.0, "hs": 100.0, "hop": 3500.0, "fix": 20.0, "bw": 80.0}
-MODELS = [MODEL, dict(MODEL, cyc=0.83, pe=0.42, h=80.0, hs=80.0, g=1.3, hop=3000.0, bw=100.0),
-          dict(MODEL, cyc=1.2, pe=0.6, h=130.0, hs=130.0, g=1.9, hop=5500.0, bw=50.0)]
+OPT = {"pieces": 8, "iters": 7000, "seed": 1, "sum_a": (), "eq_a": False, "snap": "a", "wide": "g", "zs": 2, "four": False,
+       "all16": False}
+MODEL = {"cyc": 0.9, "pe": 0.42, "g": 1.56, "s": 3.8, "h": 180.0, "hs": 150.0, "hop": 3200.0, "fix": 20.0, "bw": 80.0}
+MODELS = [MODEL, dict(MODEL, cyc=0.83, pe=0.36, h=70.0, hs=240.0, fix=55.0, hop=2500.0, bw=100.0),
+          dict(MODEL, cyc=1.2, pe=0.55, h=220.0, hs=200.0, g=1.9, s=5.0, fix=30.0, hop=5000.0, bw=50.0)]
 
 SCRATCH = {}
 
@@ -32,9 +33,13 @@ _buf("float32", 96, "rca rcb rcc pat")
 _buf("float32", 128, "i32n wc wuz fn vcn")
 _buf("float32", 192, "kf")
 _buf("float32", 256, "cl yc zb")
-_buf("float32", 384, "dv")
-_buf("float32", 512, "vc za zc")
-_buf("float32", 224, "wz")
+_buf("float16", 512, "vc dv")
+_buf("float16", F + V0 + 72, "w16 w17 l1 l2 l3")
+_buf("float32", 512, "za zc")
+_buf("uint16", 192, "ltd")
+_buf("uint16", 512, "dl")
+_buf("float32", 216, "wz")
+_buf("bfloat16", 36, "j36")
 _buf("bfloat16", 384, "wx")
 _buf("bfloat16", 64, "jm moff one sg7 ng cb xh")
 _buf("bfloat16", 128, "jd bd ib ibn ik ihp ihn i2p i2n wux wdt wtm wng wdf dge wav wst wtt ce")
@@ -47,7 +52,7 @@ _buf("bfloat16", [4, 128], "selb lc")
 _buf("float16", 64, "rc1 gsm rct sg1 sg2 zz sw tw csg dd")
 _buf("float16", [35, 4], "r4a r4c")
 _buf("float16", [71, 2], "r2b")
-_buf("uint16", 64, "sa sc sb0 sb1 sb2 sb3 ltd dl no")
+_buf("uint16", 64, "sa sc sb0 sb1 sb2 sb3 no")
 _buf("float32", 512, "ps0 ps1 ps2 ps3 ps4 ps5 ps6 ps7", "psum")
 
 SEMAPHORES = ["cv", "ca", "cp", "cg"] + [p + str(i) for p in "mt" for i in range(28)] + ["d%d" % i for i in range(48)]
@@ -88,6 +93,11 @@ def span(a):
     return ends[0][0] * w + ends[1][0], ends[0][1] * w + ends[1][1] + 1
 
 
+def cells(a):
+    axes = [range(*d) if isinstance(d, tuple) else [d] for d in a[3:]]
+    return set(axes[0]) if len(axes) == 1 else set((i, j) for i in axes[0] for j in axes[1])
+
+
 def isz(a):
     if a[0] == "ind":
         a = a[1]
@@ -109,8 +119,8 @@ def cost(op, m):
         return 150 + 2 * ncols(a[0]) * m["cyc"]
     if k == "dma":
         return 60.0
-    if k == "send":
-        return 700.0
+    if k in ("send", "fwd"):
+        return 700.0 if k == "send" else 0.0
     out, i0 = a[0], (a[1] if k != "ms" else a[0])
     n = ncols(out)
     if out[0] == "ind":
@@ -129,10 +139,9 @@ def latency(op, m):
     if op["k"] == "dma":
         return 1800 + op["load"] / 180.0
     if op["k"] == "send":
-        o = op["a"][0]
-        if op["load"]:
-            return m["hop"] + op["load"] / m["bw"]
-        return m["hop"] * (1.0 if op["a"][4] else 0.55) + 128 * ncols(o) * isz(o) / 100.0
+        return m["hop"] * (1.0 if op["a"][3] else 0.55) + op["load"] / m["bw"]
+    if op["k"] == "fwd":
+        return m["hop"] + op["load"] / m["bw"] + 900.0 * op["a"][3]
     return 0.0
 
 
@@ -151,6 +160,11 @@ def regions(op):
             add(out, wr)
             add(l, rd)
             add(r, rd)
+    elif k in ("send", "fwd"):
+        for (d, s, w) in a[0]:
+            add(d, wr)
+            if k == "send":
+                add(s, rd)
     else:
         add(a[0], wr)
         for x in a[1:]:
@@ -184,9 +198,17 @@ def build():
         load[0] += len(range(*out[2])) * ncols(out) * isz(out)
         ops[-1]["load"] = load[0]
 
-    def send(dst, src, step, ways):
-        put("g", "send", dst, src, nsend[0], step % 4, [] if step % 4 == 2 and ways != [2, 3] else ways)
+    def send(parts, step, via=None, wait=0):
+        put("g", "send", parts, nsend[0], step % 4, step % 4 != 2 if via is None else via)
+        ops[-1]["load"] = wait + sum(128 * ncols(d) * isz(d) for (d, s, w) in parts)
         nsend[0] += 1
+        return len(ops) - 1
+
+    def onward(first, places, step, nth):
+        put("r", "fwd", [(d, p[0], p[2]) for d, p in zip(places, ops[first]["a"][0])], nsend[0], step % 4, nth)
+        ops[-1]["load"], ops[-1]["after"] = ops[first]["load"], [first]
+        nsend[0] += 1
+    two = lambda d, s, ways: [(piece(d, h, 2), piece(s, h, 2), ways[h]) for h in range(2)]
 
     np_ = OPT["pieces"]
     hv = V0 // np_
@@ -203,6 +225,7 @@ def build():
     put("g", "iota", full("jd"), [[1, 8], [0, 16]], 0, 0)
     put("g", "iota", full("jm"), [[0, 4], [1, 16]], 0, 0)
     put("g", "sel", IB, zero(128), [[-1, 128]], OP.not_equal, 1.0, 0, 1)
+    put("g", "iota", full("j36"), [[0, 4], [1, 9]], 0, 0)
     put("g", "iota", full("j64"), [[1, 4], [0, 64]], 0, 0)
     put("g", "iota", full("j256"), [[0, 4], [1, 64]], 0, 0)
     ci = lambda k: A("coli", k, k + 1)
@@ -258,8 +281,8 @@ def build():
     ts(A("cl", 0, 128, 16), A("jd", 0, 128, 16), 16.0, K["spare"], OP.mult, OP.add)
     for n in ("r4a", "r4c", "r2b"):
         lin(A3(n, (0, SCRATCH[n][1][1], 1), (0, SCRATCH[n][1][2], 1)), zero(SCRATCH[n][1][1] * SCRATCH[n][1][2]), 1.0)
-    for k in range(4):
-        put("v", "ms", A("cn", 430 * k, 430 * k + 430), 0.0)
+    for n in ("wz", "wx"):
+        put("g", "iota", full(n), [[0, SCRATCH[n][1][1]]], 0, 0)
     bd8, BD = A("bd", 0, 128, 16), full("bd")
     lin(K["tpos"], R13, 1.0 / 4096)
     lin(K["tneg"], R12, -1.0 / 4096)
@@ -267,29 +290,20 @@ def build():
     def weights(v, sign):
         lin(C(48 + 2 * v), sign, -1.0, K["r14e"])
         lin(C(49 + 2 * v), sign, E, K["r12h"])
-        lin(A("wz", 56 * v + 4, 56 * v + 51, 6), bd8, C(48 + 2 * v))
+        lin(A("wz", 54 * v + 4, 54 * v + 51, 6), bd8, C(48 + 2 * v))
         lin(A("wx", 96 * v + 1, 96 * v + 48, 6), bd8, C(49 + 2 * v))
-    lin(full("wz"), zero(224), 1.0)
-    lin(full("wx"), zero(384), 1.0)
-    for v in range(4):
-        ts(A("wz", 56 * v + 3, 56 * v + 51, 6), bd8, K["tpos"], None, OP.mult)
-        ts(A("wz", 56 * v + 5, 56 * v + 51, 6), bd8, K["tneg"], None, OP.mult)
+    ts(A("wz", 3, 216, 6), full("j36"), C(2), K["tpos"], OP.is_equal, OP.mult)
+    ts(A("wz", 5, 216, 6), full("j36"), C(2), K["tneg"], OP.is_equal, OP.mult)
     weights(0, SG)
-    lin(full("wst"), IB, K["lt14"])
-    lin(A("wst", 14, 128, 16), bd8, SG)
-    lin(K["cuz"], C(48), -1.0)
-    lin(K["cux"], C(49), -1.0)
-    lin(K["dgc"], K["rd"], 2048.0)
-    lin(C(46), K["rd"], 0.5)
-    lin(C(47), K["rt"], 0.5)
-    lin(C(56), K["rc"], -1.0)
-    lin(C(57), ST, 0.5)
-    for n, c in (("wuz", K["cuz"]), ("wux", K["cux"]), ("wdt", C(46)), ("wtm", C(47)), ("wc", C(56)), ("wng", 8192.0),
-                 ("wdf", 2048.0)):
-        lin(full(n), BD, c)
-    for n, c in (("i32n", -1.0), ("ibn", -1.0), ("ik", 16384.0), ("ihp", 0.5), ("ihn", -0.5), ("i2p", 2048.0),
-                 ("i2n", -2048.0), ("dge", K["dgc"]), ("wav", C(57)), ("wtt", K["rt"])):
-        lin(full(n), IB, c)
+    ts(full("wst"), IB, K["lt14"], None, OP.mult)
+    ts(A("wst", 14, 128, 16), bd8, SG, None, OP.mult)
+    for n, i, c, f in (("wuz", BD, C(48), -1.0), ("wux", BD, C(49), -1.0), ("wdt", BD, K["rd"], 0.5),
+                       ("wtm", BD, K["rt"], 0.5), ("wc", BD, K["rc"], -1.0), ("dge", IB, K["rd"], 2048.0),
+                       ("wav", IB, ST, 0.5), ("wtt", IB, K["rt"], 1.0)):
+        ts(full(n), i, c, f, OP.mult, OP.mult)
+    for n, i, f in (("wng", BD, 8192.0), ("wdf", BD, 2048.0), ("i32n", IB, -1.0), ("ibn", IB, -1.0), ("ik", IB, 16384.0),
+                    ("ihp", IB, 0.5), ("ihn", IB, -0.5), ("i2p", IB, 2048.0), ("i2n", IB, -2048.0)):
+        lin(full(n), i, f)
     lin(A("ce", 0, 64), full("moff"), 1.0, 2048.0)
     lin(A("ce", 64, 128), zero(64), 1.0, K["cec"])
     lin(A("cf", 0, 64), full("moff"), 1.0, 2048.0)
@@ -301,8 +315,7 @@ def build():
     lin(K["ck"], A("ps3", 0, 1), C(58))
     lin(A("mp0", 0, F), zero(F), 1.0, SG)
     lin(A("mp0", F + V0, F + W0), zero(W0 - V0), 1.0, K["c240"])
-    for v in range(1, 4):
-        lin(A("rp%d" % v, F + V0 + 64 * (v - 1), F + W0), zero(W0 - V0 - 64 * (v - 1)), 1.0, K["c240"])
+    put("v", "ms", full("ltd"), 0)
     for k in range(np_):
         c0, c1 = hv * k, hv * k + hv
         o = A("ps%d" % (4 + k % 4), hv * (k // 4), hv * (k // 4) + hv)
@@ -310,10 +323,8 @@ def build():
         mm([(o, full("wst"), A("hf", c0, c1), True, True)])
         lin(A("mp0", F + c0, F + c1), o, 1.0, K["c240"])
     for k in range(4):
-        cp(A("tru", 332 * k, 332 * k + 332), A("raw", 332 * k, 332 * k + 332))
-    load[0] = 0
-    for r in (14, 15):
-        dma("s", A("cn", F, F + V0, 1, r, 128, 16), A("tru", 0, V0, 1, r, 128, 16))
+        cp(A("cn", F + 332 * k, F + 332 * k + 332), A("raw", 332 * k, 332 * k + 332))
+    lin(A("cn", F + V0, F + W0), zero(W0 - V0), 1.0)
     cp(A("sb0", 0, 16), A("sti", 0, 16))
     cp(A("sc", 0, 24), A("sti", 16, 40))
     cp(A("sa", 4 + 4, 32), A("sti", 40, 64))
@@ -342,12 +353,18 @@ def build():
         if side:
             mm([(P3(2), full("wuz"), A(z, 0, 64), False, True)])
             act(full(sgn), P3(2), AF.Sign, 0.0, 1.0)
-        mm([(A(bank, 48 * (k // 2), 48 * (k // 2) + 48, 1, 0, mp), A(z, k, n, kk),
-             A("wz", 56 * wk + 3 - 3 * (k % 2), 56 * wk + 51 - 3 * (k % 2)), False, k == kk - 1) for k in range(kk)])
+        zm = [(A(bank, 48 * (k // 2), 48 * (k // 2) + 48, 1, 0, mp), A(z, k, n, kk),
+               A("wz", 54 * wk + 3 - 3 * (k % 2), 54 * wk + 51 - 3 * (k % 2)), False, k == kk - 1) for k in range(kk)]
+        for k in range(0, kk, OPT["zs"]):
+            mm(zm[k:k + OPT["zs"]])
         lin(X, A(z, 0, n), K["xs"], K["xb"])
         if side:
             tt(full("zz"), P3(0), full(sgn), OP.mult)
-            tt(full(res), P3(1), full("zz"), OP.add)
+            if res in OPT["sum_a"]:
+                mm([(P3(5), full("wtm"), full(rec), True, False), (P3(5), IB, full("zz"), False, True)])
+                lin(full(res), P3(5), 1.0)
+            else:
+                tt(full(res), P3(1), full("zz"), OP.add)
         scan(A(rc, 0, 24 * kk, 1, 0, mp), A("pat", 0, 24 * kk, 1, 0, mp), A(bank, 0, 24 * kk, 1, 0, mp), 0.0,
              OP.mult, OP.max)
         for h in range(kk // 2):
@@ -374,6 +391,8 @@ def build():
 
     def pairs(w, start):
         lst = [(DF, full("ibn"), full(w), True, False)] if start else []
+        if start and OPT["eq_a"]:
+            lst = [(D, full("ik"), full("tri1"), True, False)]
         lst += [(half("ps4", h, 256), half(w, h), half("ra", h), False, False) for h in range(2)]
         return lst + [(A("ps4", 64 * k, 64 * k + 64), A3("selb", k, (0, 128, 1)), full(w), False, k == 3) for k in range(4)]
 
@@ -386,7 +405,11 @@ def build():
 
     def stage1(v):
         mm(pairs("sw", True))
-        tt(A("eq", 0, 256), D, full("tri1"), OP.is_equal)
+        if OPT["eq_a"]:
+            act(A("eq2", 0, 256), D, AF.Abs, 0.0, 1.0)
+            act(A("eq", 0, 256), A("eq2", 0, 256), AF.Relu, 1.0, -1.0)
+        else:
+            tt(A("eq", 0, 256), D, full("tri1"), OP.is_equal)
         mm([(SD, IB, full("moff"), True, False), (SD, IB, full("sw"), False, False)] + counts(SD, "eq", True))
         act(full("ng"), SD, AF.Sign, -2000.0, 1.0)
         mm([(DF, full("ibn"), full("sw"), True, False)]
@@ -440,23 +463,49 @@ def build():
         lin(A("fn", 64, 128), full("gt"), 0.5 - 2.0 ** -15, MAGIC)
         lin(full("vcn"), full("fn"), 1.0, -MAGIC)
         cp(IND(win("cn", WD), LT(v, 0, 8)), full("vcn"))
-        if v < 3:
-            send(A("dv", 128 * v, 128 * v + 128), VC(v, 0, 128), -(v + 1), [0, 1])
-            send(A("dl", 8 * v, 8 * v + 8), LT(v, 4, 12), -(v + 1), [1])
         if v == 0:
             lin(A("xa", 0, 64), xt, 1.0)
         else:
-            send((A("xc", NM, NM + 64), A("xa", 448, 512), full("xh"))[v - 1], xt, -v, [0])
-            send((A("sc", 24, 28), A("sa", 32, 36), A("so", 12, 16))[v - 1], new, -v, [1])
+            send([((A("xc", NM, NM + 64), A("xa", 448, 512), full("xh"))[v - 1], xt, 0)], -v)
+        if v < 3:
+            src = lambda w: [(DV(v, w), VC(v, 0, 128), 0), (DL(v, w), LT(v, 4, 132), 1)]
+            first = send(src(v + 1), -(v + 1))
+        if v > 0:
+            send([((A("sc", 24, 28), A("sa", 32, 36), A("so", 12, 16))[v - 1], new, 1)], -v)
+        if v == 1:
+            send(src(3), -3)
+        for w in ((1,), (2, 3), (3,), ())[v]:
+            cp(IND(win("rp%d" % w, WD), A("dl", DL(v, w)[3][0], DL(v, w)[3][0] + 8)), DV(v, w))
 
-    def base(v):
-        n = (F + V0 + 64 * (v - 1)) // 2
-        for h in range(2):
-            send(A("rp%d" % v, n * h, n * h + n), A("mp0" if v == 1 else "mp1", n * h, n * h + n), -v, [2, 3])
-            ops[-1]["load"] = 512 * n * (h + 1)
-        weights(v, A("rp%d" % v, 0, 1))
+    slot = lambda v, w: 128 * [(0, 1), (1, 2), (1, 3), (2, 3)].index((v, w))
+    DV = lambda v, w: A("dv", slot(v, w), slot(v, w) + 128)
+    DL = lambda v, w: A("dl", slot(v, w), slot(v, w) + 128)
 
-    base(1)
+    def cast(q, out, i):
+        for k in range(2):
+            if q == "g":
+                put("g", "sel", piece(out, k, 2), piece(i, k, 2), [[0, ncols(out) // 2]], OP.is_ge, 0.0, 0, 0)
+            else:
+                lin(piece(out, k, 2), piece(i, k, 2), 1.0)
+
+    def base(src, snap, n, visits):
+        n //= 2
+        first = []
+        for v in visits:
+            for h in range(2):
+                there = A("l%d" % v, n * h, n * h + n)
+                if v == visits[0]:
+                    cast(OPT["snap"], A(snap, n * h, n * h + n), A(src, n * h, n * h + n))
+                    ways = [0, 1] if v == 1 and h == 0 and OPT["four"] else [2, 3]
+                    first.append(send(two(there, A(snap, n * h, n * h + n), ways), -v, True,
+                                      256 * n * h * (v > 1 or not OPT["four"])))
+                else:
+                    onward(first[h], [piece(there, k, 2) for k in range(2)], -v, 6 + h)
+                cast(OPT["wide"], A("rp%d" % v, n * h, n * h + n), there)
+            lin(A("rp%d" % v, 2 * n, F + W0), zero(F + W0 - 2 * n), 1.0, K["c240"])
+            weights(v, A("rp%d" % v, 0, 1))
+
+    base("mp0", "w16", F + V0, [1])
     load[0] = 0
     dma("s", A("mp1", 0, F + W0), A("mp0", 0, F + W0))
     for v in range(4):
@@ -468,17 +517,17 @@ def build():
             if s == 1:
                 stage1(v)
         if v < 3:
-            send(A("xb%d" % (v + 1), 0, n - 64), A("xb%d" % v, 64, n), 1, [0, 1])
-            send(A("sb%d" % (v + 1), 0, n // 16 - 4), A("sb%d" % v, 52, 48 + n // 16), 1, [1])
-        if v > 0:
-            cp(IND(win("rp%d" % v, WD), A("dl", 8 * v - 8, 8 * v)), A("dv", 128 * v - 128, 128 * v))
+            send(two(A("xb%d" % (v + 1), 0, n - 64), A("xb%d" % v, 64, n), [0, 1]), 1)
+            last = send([(A("sb%d" % (v + 1), 0, n // 16 - 4), A("sb%d" % v, 52, 48 + n // 16), 1)], 1)
         for c in "ca":
             home(c, v)
         train(v)
-        if v < 2:
-            base(v + 2)
+        if v == 0:
+            base("mp1", "w17", F + V0 + 64 + 8, [2, 3])
         if v == 2:
-            last = len(ops) - 1
+            last = max(i for i, o in enumerate(ops) if o["k"] == "send")
+            for k in range(4):
+                lin(A("tru", 332 * k, 332 * k + 332), A("mp0", F + 332 * k, F + 332 * k + 332), 1.0, K["cm240"])
             load[0] = 0
             for g in range(8):
                 dma("s", A("yp", 0, V0, 1, 16 * g, 16 * g + 12), A("tru", 0, V0, 1, 16 * g, 16 * g + 12))
@@ -495,7 +544,9 @@ def build():
     for (o, n, i, j) in ((192, "xh", 0, 64), (256, "xc", 0, NM), (64, "xc", NM, NM + 64), (0, "xa", 0, 64),
                          (640, "xa", 64, 448), (128, "xa", 448, 512)):
         lin(A("xo", o, o + j - i), A(n, i, j), ST, K["cm240"])
-    dma("s", A("yx", 0, 1024), full("xo"))
+    for (i, j) in ((192, 640), (640, 1024), (0, 192)):
+        load[0] = 0
+        dma("s", A("yx", i, j), A("xo", i, j))
     load[0] = 0
     dma("s", A("ys", 0, 64), full("so"))
 
@@ -513,6 +564,8 @@ def build():
                         if ops[j]["q"] != op["q"] or op["q"] == "p":
                             dep.add(j)
                     elif (w or w2) and lo < hi2 and lo2 < hi and r[2][0] < r2[2][1] and r2[2][0] < r[2][1]:
+                        if op["q"] == ops[j]["q"] == "a" and op["k"] == ops[j]["k"] == "act" and not cells(r) & cells(r2):
+                            continue
                         dep.add(j)
                         if w2:
                             land.add(j)
@@ -522,17 +575,20 @@ def build():
                     hist.setdefault(r[1], []).append((i, r, w) + span(r))
         op["dep"] = sorted(dep)
         op["left"] = set(j for j in dep if ops[j]["k"] == "send" and j not in land)
+        op["free"] = set(j for j in dep if ops[j]["q"] == op["q"] == "p")
     return ops
 
 
 def gap(ops, j, i, m):
     a, b = ops[j], ops[i]
+    if b["k"] == "fwd":
+        return 0.0
     if j in b["left"]:
         return 2000 + a["load"] / 120.0
-    if a["k"] in ("dma", "send"):
+    if a["k"] in ("dma", "send", "fwd"):
         return latency(a, m) + m["h"]
     if a["q"] == b["q"]:
-        return 0.0 if a["q"] == "p" else m["hs"]
+        return 0.0 if j in b["free"] else m["hs"]
     return m["h"]
 
 
@@ -540,72 +596,86 @@ def schedule(ops, ms, iters, seed):
     n = len(ops)
     near = []
     for i in range(n):
-        far = set(k for j in ops[i]["dep"] for k in ops[j]["dep"] if ops[k]["k"] not in ("dma", "send"))
+        far = set(k for j in ops[i]["dep"] for k in ops[j]["dep"] if ops[k]["k"] not in ("dma", "send", "fwd"))
         near.append([j for j in ops[i]["dep"] if j not in far])
     tabs = []
     for m in ms:
         c = [cost(o, m) for o in ops]
         tabs.append((c, [latency(o, m) for o in ops], [[(j, c[j] + gap(ops, j, i, m)) for j in near[i]] for i in range(n)]))
+    c, lat, pre = tabs[0]
+    suc = [[] for i in range(n)]
+    for i in range(n):
+        for (j, d) in pre[i]:
+            suc[j].append((i, d - c[j] + c[i]))
+    qs = [o["q"] for o in ops]
     x = [seed]
 
     def rnd():
         x[0] = (x[0] * 1103515245 + 12345) % 2147483648
         return x[0] / 2147483648
 
-    def order_of(bump):
-        c, lat, dep = tabs[0]
-        rank = [c[i] + lat[i] for i in range(n)]
-        for i in range(n - 1, -1, -1):
-            rank[i] += bump[i]
-            for (j, d) in dep[i]:
-                if d + rank[i] > rank[j]:
-                    rank[j] = d + rank[i]
-        busy = {q: [] for q in "vapgs"}
+    def place(seq, dep, first):
+        busy = {q: [] for q in "vapgsr"}
         st = [0.0] * n
-        for i in sorted(range(n), key=lambda i: (-rank[i], i)):
-            t = 0.0
+        for i in seq:
+            t = first[i]
             for (j, d) in dep[i]:
                 if st[j] + d > t:
                     t = st[j] + d
-            b = busy[ops[i]["q"]]
+            b = busy[qs[i]]
             k = len(b)
             while k > 0 and b[k - 1][1] > t:
                 k -= 1
             while k < len(b) and t + c[i] > b[k][0]:
-                t = max(t, b[k][1])
+                if b[k][1] > t:
+                    t = b[k][1]
                 k += 1
             st[i] = t
             b.insert(k, (t, t + c[i]))
-        return sorted(range(n), key=lambda i: (st[i], i))
+        return st
 
-    def value(order):
+    def starts(key):
+        st = place(sorted(range(n), key=lambda i: (key[i], i)), pre, [0.0] * n)
+        back = place(sorted(range(n), key=lambda i: (-st[i] - c[i], -i)), suc, lat)
+        return place(sorted(range(n), key=lambda i: (-back[i] - c[i], i)), pre, [0.0] * n)
+
+    def value(st):
+        order = sorted(range(n), key=lambda i: (st[i], i))
         total = 0.0
         for (c, lat, dep) in tabs:
-            free = {q: 0.0 for q in "vapgs"}
+            free = {q: 0.0 for q in "vapgsr"}
             st = [0.0] * n
             end = 0.0
             for i in order:
-                t = free[ops[i]["q"]]
+                t = free[qs[i]]
                 for (j, d) in dep[i]:
                     if st[j] + d > t:
                         t = st[j] + d
                 st[i] = t
-                free[ops[i]["q"]] = t + c[i]
-                end = max(end, t + c[i] + lat[i])
+                free[qs[i]] = t + c[i]
+                if t + c[i] + lat[i] > end:
+                    end = t + c[i] + lat[i]
             total += end
         return total
-    bump = [0.0] * n
-    best = order_of(bump)
+    key = [-c[i] - lat[i] for i in range(n)]
+    for i in range(n - 1, -1, -1):
+        for (j, d) in pre[i]:
+            key[j] = min(key[j], key[i] - d)
+    best = starts(key)
     bv = value(best)
     for it in range(iters):
-        nb = list(bump)
-        for r in range(1 + int(rnd() * 4)):
-            nb[int(rnd() * n)] = rnd() * 5000.0 if rnd() < 0.8 else 0.0
-        o = order_of(nb)
-        val = value(o)
+        lo, amp = rnd() * max(best), rnd() * 1500.0
+        hi = lo + 1000.0 + rnd() * 8000.0
+        key = [t + rnd() * amp if lo < t < hi else t for t in best]
+        for i in range(n):
+            for (j, d) in pre[i]:
+                if key[j] >= key[i]:
+                    key[i] = key[j] + 0.001
+        st = starts(key)
+        val = value(st)
         if val <= bv:
-            bump, best, bv = nb, o, val
-    return best
+            best, bv = st, val
+    return sorted(range(n), key=lambda i: (best[i], i))
 
 
 PLAN = {}
@@ -646,24 +716,33 @@ def rank_program(g, core, T, topo):
             return ap(a[1]).indirect(ap(a[2]))
         return T[a[1]][tuple(slice(d[0], d[1], d[2] if d[2] != 1 else None) if isinstance(d, tuple) else d for d in a[2:])]
 
+    def write(parts, en, there, here):
+        n = len(en) // len(parts)
+        tr = []
+        for h, (d, s, to) in enumerate(parts):
+            rid, pid = topo.addr(to, core)
+            tr.append(RemoteDMATransfer(dst_ids=[DstId(rid=rid, pnc=pid)], remote_sem=T.sem[there],
+                                        dma_engine_mask=bits(en[h * n:h * n + n]), src=ap(s), dst=ap(d)))
+        g.remote_dma_fused(tr, local_sem=T.sem[here])
+
     if rank is None:
         for r in range(nr):
             rl = relays(T, topo, r)
             if core in rl:
                 me = rl.index(core)
-                half = len(topo.engines(T.cores[r], core)) // 2
+                whole = len(topo.engines(T.cores[r], core))
                 total = 0
                 for i in order:
                     op = ops[i]
-                    if op["k"] == "send" and me in op["a"][4]:
-                        (d, s, k, step, ways) = op["a"]
-                        dst = T.cores[(r + step) % nr]
-                        rid, pid = topo.addr(dst, core)
-                        en = topo.engines(core, dst)
-                        a = ap(piece(d, ways.index(me), len(ways)))
-                        g.wait_ge(T.sem["m%d" % k], half)
-                        g.remote_dma(a, a, T.sem["m%d" % k], T.sem.cg, pid, rid, bits(en))
-                        total += len(en)
+                    if op["k"] == "fwd" or op["k"] == "send" and op["a"][3]:
+                        (parts, k, step, via) = op["a"]
+                        mine = [(d, d if op["k"] == "send" else s) for (d, s, w) in parts if w == me]
+                        if mine:
+                            dst = T.cores[(r + step) % nr]
+                            if op["k"] == "send":
+                                g.wait_ge(T.sem["m%d" % k], whole // (len(parts) if OPT["all16"] else 2) * len(mine))
+                            write([(d, s, dst) for (d, s) in mine], topo.engines(core, dst), "m%d" % k, "cg")
+                            total += len(topo.engines(core, dst))
                 g.wait_ge(T.sem.cg, total)
         return
 
@@ -680,10 +759,16 @@ def rank_program(g, core, T, topo):
 
     for i in order:
         op = ops[i]
-        q, k, e = op["q"], op["k"], Q[op["q"]]
+        q, k = op["q"], op["k"]
+        if k == "fwd":
+            s = "m%d" % op["a"][1]
+            count[s] = arrive * len(set(w for (d, x, w) in op["a"][0]))
+            token[i] = (s, count[s])
+            continue
+        e = Q[q]
         need = {}
         for j in op["dep"]:
-            if q == "p" and ops[j]["q"] == "p":
+            if j in op["free"]:
                 continue
             s, val = gone[j] if j in op["left"] else token[j]
             need[s] = max(need.get(s, 0), val)
@@ -693,24 +778,14 @@ def rank_program(g, core, T, topo):
             wait(q, (s, need[s]))
         a = [ap(x) for x in op["a"]] if k != "mm" else None
         if k == "send":
-            (d, src, n, step, ways) = op["a"]
+            (parts, n, step, via) = op["a"]
             s, t = "m%d" % n, "t%d" % n
-            en = topo.engines(core, rl[0])
-            half = len(en) // 2
-            if len(ways) == 2:
-                tr = []
-                for h in range(2):
-                    rid, pid = topo.addr(rl[ways[h]], core)
-                    tr.append(RemoteDMATransfer(dst_ids=[DstId(rid=rid, pnc=pid)], remote_sem=T.sem[s],
-                                                dma_engine_mask=bits(en[h * half:h * half + half]),
-                                                src=ap(piece(src, h, 2)), dst=ap(piece(d, h, 2))))
-                g.remote_dma_fused(tr, local_sem=T.sem[t])
-            else:
-                to = rl[ways[0]] if ways else T.cores[(rank + step) % nr]
-                rid, pid = topo.addr(to, core)
-                g.remote_dma(a[0], a[1], T.sem[s], T.sem[t], pid, rid, bits(topo.engines(core, to)[:half]))
-            count[t] = max(1, len(ways)) * half
-            count[s] = max(1, len(ways)) * arrive
+            to = T.cores[(rank + step) % nr]
+            en = topo.engines(core, rl[0] if via else to)
+            en = en[len(en) // 2 * (2 - len(parts)):] if via and not OPT["all16"] else en
+            write([(d, x, rl[w] if via else to) for (d, x, w) in parts], en, s, t)
+            count[t] = len(en)
+            count[s] = arrive * (len(set(w for (d, x, w) in parts)) if via else 1)
             token[i], gone[i] = (s, count[s]), (t, count[t])
             continue
         if k == "dma":

@@ -8,11 +8,14 @@ F = 8
 E = 240.0
 MAGIC = 12582912.0
 NM, NB = 384, 256
-OPT = {"pieces": 8, "iters": 7000, "seed": 1, "sum_a": (), "eq_a": False, "snap": "a", "wide": "g", "zs": 2, "four": False,
-       "all16": False}
-MODEL = {"cyc": 0.9, "pe": 0.42, "g": 1.56, "s": 3.8, "h": 180.0, "hs": 150.0, "hop": 3200.0, "fix": 20.0, "bw": 80.0}
+OPT = {"pieces": 8, "iters": 8500, "seed": 1, "sum_a": (), "eq_a": False, "snap": "a", "wide": "g", "zs": 2, "four": False,
+       "all16": False, "cn": "v", "snap3": True, "cuts": (0, 3, 5, 7, 8), "endq": "ss", "xo": "v",
+       "so": "a", "ngv": False, "gs": False, "xs": False, "slack": 0.0}
+MODEL = {"cyc": 0.9, "pe": 0.42, "g": 1.56, "s": 3.8, "h": 180.0, "hs": 150.0, "hop": 3200.0, "fix": 20.0, "bw": 80.0,
+         "dma": 1300.0, "rate": 300.0}
 MODELS = [MODEL, dict(MODEL, cyc=0.83, pe=0.36, h=70.0, hs=240.0, fix=55.0, hop=2500.0, bw=100.0),
-          dict(MODEL, cyc=1.2, pe=0.55, h=220.0, hs=200.0, g=1.9, s=5.0, fix=30.0, hop=5000.0, bw=50.0)]
+          dict(MODEL, cyc=1.2, pe=0.55, h=220.0, hs=200.0, g=1.9, s=5.0, fix=30.0, hop=5000.0, bw=50.0, dma=1700.0,
+               rate=200.0)]
 
 SCRATCH = {}
 
@@ -28,13 +31,13 @@ _buf("int32", 8, "sgi coli")
 _buf("float32", V0, "tru")
 _buf("float16", V0, "hf")
 _buf("float32", F + WD, "mp0 mp1 rp1 rp2 rp3 cn")
-_buf("float32", 64, "so col gsc inc ns gt kd ks")
+_buf("float32", 64, "so col gsc inc ns gt kd ks tx")
 _buf("float32", 96, "rca rcb rcc pat")
 _buf("float32", 128, "i32n wc wuz fn vcn")
 _buf("float32", 192, "kf")
 _buf("float32", 256, "cl yc zb")
 _buf("float16", 512, "vc dv")
-_buf("float16", F + V0 + 72, "w16 w17 l1 l2 l3")
+_buf("float16", F + V0 + 136, "w16 w17 l1 l2 l3")
 _buf("float32", 512, "za zc")
 _buf("uint16", 192, "ltd")
 _buf("uint16", 512, "dl")
@@ -137,7 +140,7 @@ def cost(op, m):
 
 def latency(op, m):
     if op["k"] == "dma":
-        return 1800 + op["load"] / 180.0
+        return m["dma"] + op["load"] / m["rate"]
     if op["k"] == "send":
         return m["hop"] * (1.0 if op["a"][3] else 0.55) + op["load"] / m["bw"]
     if op["k"] == "fwd":
@@ -213,13 +216,19 @@ def build():
     np_ = OPT["pieces"]
     hv = V0 // np_
     dma("s", A("sgi", 0, 1), A("sg", 0, 1))
-    dma("a", full("sti"), A("st0", 0, 64))
-    for k in range(np_):
-        dma("sa"[k % 2], A("raw", hv * k, hv * k + hv), A("recs", hv * k, hv * k + hv))
-        if k == np_ // 2 - 1:
-            dma("s", A("xb0", 0, NB), A("cx0", 0, NB))
-    dma("a", A("xc", 0, NM), A("cx0", NB, NB + NM))
+    cuts = OPT["cuts"]
+    for k in range(len(cuts) - 1):
+        dma("as"[k % 2], A("raw", hv * cuts[k], hv * cuts[k + 1]), A("recs", hv * cuts[k], hv * cuts[k + 1]))
+    dma("a", A("xb0", 0, NB), A("cx0", 0, NB))
+    dma("s", full("sti"), A("st0", 0, 64))
+    load[0] = 0
+    dma("s", A("xc", 0, NM), A("cx0", NB, NB + NM))
     dma("s", A("xa", 64, 64 + NM), A("cx0", NB + NM, 1024))
+    for i, o in enumerate(ops):
+        o["after"] = [j for j in range(i) if ops[j]["q"] == o["q"]][-1:]
+    nload = len(ops) - 2
+    for o in ops[-2:]:
+        o["after"] = [2]
     put("v", "ms", full("zr"), 0.0)
     put("g", "iota", A("coli", 0, 1), [[0, 1]], 0, 1)
     put("g", "iota", full("jd"), [[1, 8], [0, 16]], 0, 0)
@@ -323,7 +332,11 @@ def build():
         mm([(o, full("wst"), A("hf", c0, c1), True, True)])
         lin(A("mp0", F + c0, F + c1), o, 1.0, K["c240"])
     for k in range(4):
-        cp(A("cn", F + 332 * k, F + 332 * k + 332), A("raw", 332 * k, 332 * k + 332))
+        if OPT["cn"] == "v":
+            cp(A("cn", F + 332 * k, F + 332 * k + 332), A("raw", 332 * k, 332 * k + 332))
+        else:
+            put("g", "sel", A("cn", F + 332 * k, F + 332 * k + 332), A("raw", 332 * k, 332 * k + 332), [[0, 332]], OP.is_ge,
+                0.0, 0, 0)
     lin(A("cn", F + V0, F + W0), zero(W0 - V0), 1.0)
     cp(A("sb0", 0, 16), A("sti", 0, 16))
     cp(A("sc", 0, 24), A("sti", 16, 40))
@@ -349,7 +362,9 @@ def build():
         mm([(A(bank, 0, 24 * kk, 1, 0, mp), xk(0), A("wx", 96 * wk, 96 * wk + 24 * kk), True, False)]
            + [(A(bank, at(k), at(k) + 43, 6, 0, mp), xk(k), A("wx", 96 * wk + 1, 96 * wk + 48, 6), False, False)
               for k in range(1, kk)])
-        tt(A(z, 0, n), IND(w, S), X, OP.mult)
+        cut = [0, n] if n <= 256 or not OPT["gs"] else [0, n // 64 * 32, n]
+        for (i, j) in zip(cut, cut[1:]):
+            tt(A(z, i, j), IND(w, A(S[1], S[3][0] + i // 16, S[3][0] + j // 16)), A(X[1], x0 + i, x0 + j), OP.mult)
         if side:
             mm([(P3(2), full("wuz"), A(z, 0, 64), False, True)])
             act(full(sgn), P3(2), AF.Sign, 0.0, 1.0)
@@ -357,7 +372,9 @@ def build():
                A("wz", 54 * wk + 3 - 3 * (k % 2), 54 * wk + 51 - 3 * (k % 2)), False, k == kk - 1) for k in range(kk)]
         for k in range(0, kk, OPT["zs"]):
             mm(zm[k:k + OPT["zs"]])
-        lin(X, A(z, 0, n), K["xs"], K["xb"])
+        cut = [0, n] if n <= 256 or not OPT["xs"] else [0, n // 64 * 32, n]
+        for (i, j) in zip(cut, cut[1:]):
+            lin(A(X[1], x0 + i, x0 + j), A(z, i, j), K["xs"], K["xb"])
         if side:
             tt(full("zz"), P3(0), full(sgn), OP.mult)
             if res in OPT["sum_a"]:
@@ -373,7 +390,7 @@ def build():
         mm([(A(bank, 128, 128 + m), A3(r, (aa - 1 - a, aa - 1 - a + 128 // kk, 1), (0, kk, 1), mp),
              A("ib", a, mp, aa, 0, mp), a == 0, a == aa - 1) for a in range(aa)])
         for (out, i, j) in outs:
-            (cp if isz(out) == 2 else lambda o, p: lin(o, p, 1.0))(out, A(bank, 128 + i, 128 + j))
+            (cp if isz(out) == 2 or OPT["so"] == "v" else lambda o, p: lin(o, p, 1.0))(out, A(bank, 128 + i, 128 + j))
 
     def home(c, v):
         lo, hi = {"a": (64 if v == 0 else 0, 448 + (64 if v == 3 else 0)), "c": (0, NM + (64 if v > 1 else 0))}[c]
@@ -412,8 +429,9 @@ def build():
             tt(A("eq", 0, 256), D, full("tri1"), OP.is_equal)
         mm([(SD, IB, full("moff"), True, False), (SD, IB, full("sw"), False, False)] + counts(SD, "eq", True))
         act(full("ng"), SD, AF.Sign, -2000.0, 1.0)
-        mm([(DF, full("ibn"), full("sw"), True, False)]
-           + [(half("ps4", h, 256), half("ng", h), half("ras", h), False, False) for h in range(2)])
+        if not OPT["ngv"]:
+            mm([(DF, full("ibn"), full("sw"), True, False)]
+               + [(half("ps4", h, 256), half("ng", h), half("ras", h), False, False) for h in range(2)])
         scan(full("ks"), A("cl", 64, 128), SD, 0.0, OP.max, OP.min)
         cp(LT(v, 8, 12), A("ks", 15, 64, 16))
         lin(full("gsc"), IND(CN, L(v, 2)), 1.0)
@@ -426,7 +444,14 @@ def build():
         vt, ve, vo = A("ps7", 0, 64), A("ps7", 64, 192, 2), A("ps7", 65, 192, 2)
         lin(full("inc"), full("sg2"), C(44), C(45))
         tt(IND(win("cn", WD), LT(v, 8, 12)), full("gsc"), full("inc"), OP.add)
-        mm([(DF, IB, full("tw"), False, False)] + pairs("tw", False))
+        if OPT["ngv"]:
+            mm([(P3(5), full("wdf"), full("ng"), True, False), (P3(5), full("wtm"), full("gsm"), False, True)])
+            tt(full("tx"), P3(5), full("zz"), OP.add)
+            mm([(DF, full("ibn"), full("sw"), True, False), (DF, IB, full("tw"), False, False)]
+               + [(A("ps4", 64 * k, 64 * k + 64), A3("selb", k, (0, 128, 1)), full("tw"), False, False) for k in range(4)])
+            mm([(half("ps4", h, 256), half("tx", h), half("ra", h), False, True) for h in range(2)])
+        else:
+            mm([(DF, IB, full("tw"), False, False)] + pairs("tw", False))
         tt(full("ns"), PG, full("inc"), OP.mult)
         tt(full("eq2"), A("ps4", 0, 320), full("tri2"), OP.is_equal)
         mm([(Q, full("wng"), full("ng"), True, False), (Q, full("wc"), full("ns"), False, False)])
@@ -472,9 +497,9 @@ def build():
             first = send(src(v + 1), -(v + 1))
         if v > 0:
             send([((A("sc", 24, 28), A("sa", 32, 36), A("so", 12, 16))[v - 1], new, 1)], -v)
-        if v == 1:
+        if v == 1 and not OPT["snap3"]:
             send(src(3), -3)
-        for w in ((1,), (2, 3), (3,), ())[v]:
+        for w in ((1,), (2,) if OPT["snap3"] else (2, 3), (3,), ())[v]:
             cp(IND(win("rp%d" % w, WD), A("dl", DL(v, w)[3][0], DL(v, w)[3][0] + 8)), DV(v, w))
 
     slot = lambda v, w: 128 * [(0, 1), (1, 2), (1, 3), (2, 3)].index((v, w))
@@ -523,7 +548,9 @@ def build():
             home(c, v)
         train(v)
         if v == 0:
-            base("mp1", "w17", F + V0 + 64 + 8, [2, 3])
+            base("mp1", "w17", F + V0 + 64 + 8, [2] if OPT["snap3"] else [2, 3])
+        if v == 1 and OPT["snap3"]:
+            base("mp1", "w16", F + V0 + 128 + 8, [3])
         if v == 2:
             last = max(i for i, o in enumerate(ops) if o["k"] == "send")
             for k in range(4):
@@ -537,13 +564,16 @@ def build():
     for r in (12, 13):
         dma("s", A("yp", 0, V0, 1, r, 128, 16), A("mp1", F, F + V0, 1, r, 128, 16))
     for g in range(8):
-        dma("sa"[g % 2], A("yp", V0, W0, 1, 16 * g, 16 * g + 14), A("yc", 0, 256, 1, 16 * g, 16 * g + 14))
+        dma(OPT["endq"][g % 2], A("yp", V0, W0, 1, 16 * g, 16 * g + 14), A("yc", 0, 256, 1, 16 * g, 16 * g + 14))
     for r in (14, 15):
         dma("s", A("yp", 0, W0, 1, r, 128, 16), A("cn", F, F + W0, 1, r, 128, 16))
     load[0] = 0
     for (o, n, i, j) in ((192, "xh", 0, 64), (256, "xc", 0, NM), (64, "xc", NM, NM + 64), (0, "xa", 0, 64),
                          (640, "xa", 64, 448), (128, "xa", 448, 512)):
-        lin(A("xo", o, o + j - i), A(n, i, j), ST, K["cm240"])
+        if OPT["xo"] == "v":
+            ts(A("xo", o, o + j - i), A(n, i, j), ST, K["cm240"], OP.mult, OP.add)
+        else:
+            lin(A("xo", o, o + j - i), A(n, i, j), ST, K["cm240"])
     for (i, j) in ((192, 640), (640, 1024), (0, 192)):
         load[0] = 0
         dma("s", A("yx", i, j), A("xo", i, j))
@@ -575,13 +605,13 @@ def build():
                     hist.setdefault(r[1], []).append((i, r, w) + span(r))
         op["dep"] = sorted(dep)
         op["left"] = set(j for j in dep if ops[j]["k"] == "send" and j not in land)
-        op["free"] = set(j for j in dep if ops[j]["q"] == op["q"] == "p")
+        op["free"] = set(j for j in dep if ops[j]["q"] == op["q"] == "p" or i < nload)
     return ops
 
 
 def gap(ops, j, i, m):
     a, b = ops[j], ops[i]
-    if b["k"] == "fwd":
+    if b["k"] == "fwd" or j in b["free"]:
         return 0.0
     if j in b["left"]:
         return 2000 + a["load"] / 120.0
@@ -661,19 +691,21 @@ def schedule(ops, ms, iters, seed):
     for i in range(n - 1, -1, -1):
         for (j, d) in pre[i]:
             key[j] = min(key[j], key[i] - d)
-    best = starts(key)
-    bv = value(best)
+    best = now = starts(key)
+    bv = nv = value(best)
     for it in range(iters):
-        lo, amp = rnd() * max(best), rnd() * 1500.0
-        hi = lo + 1000.0 + rnd() * 8000.0
-        key = [t + rnd() * amp if lo < t < hi else t for t in best]
+        lo, amp = rnd() * max(now), rnd() * 1500.0
+        hi = lo + 500.0 + rnd() * 6000.0
+        key = [t + rnd() * amp if lo < t < hi else t for t in now]
         for i in range(n):
             for (j, d) in pre[i]:
                 if key[j] >= key[i]:
                     key[i] = key[j] + 0.001
         st = starts(key)
         val = value(st)
-        if val <= bv:
+        if val <= nv + OPT["slack"] * (1 - it / iters) * rnd() ** 2:
+            now, nv = st, val
+        if val < bv:
             best, bv = st, val
     return sorted(range(n), key=lambda i: (best[i], i))
 

from concourse.bass import DstId, RemoteDMATransfer
from concourse.mybir import AluOpType, ActivationFunctionType

OP = AluOpType
AF = ActivationFunctionType
V0, W0, WD = 1328, 1584, 1712
F = 8
E = 240.0
MAGIC = 12582912.0
NM, NB = 384, 256
OPT = {"pieces": 8, "iters": 8500, "seed": 1, "sum_a": (), "eq_a": False, "snap": "a", "wide": "g", "zs": 2, "four": False,
       "all16": False, "cn": "v", "snap3": True, "cuts": (0, 3, 5, 7, 8), "endq": "ss", "xo": "v",
       "so": "a", "ngv": False, "gs": False, "xs": False, "slack": 0.0}
MODEL = {"cyc": 0.9, "pe": 0.42, "g": 1.56, "s": 3.8, "h": 180.0, "hs": 150.0, "hop": 3200.0, "fix": 20.0, "bw": 80.0,
         "dma": 1300.0, "rate": 300.0}
MODELS = [MODEL, dict(MODEL, cyc=0.83, pe=0.36, h=70.0, hs=240.0, fix=55.0, hop=2500.0, bw=100.0),
          dict(MODEL, cyc=1.2, pe=0.55, h=220.0, hs=200.0, g=1.9, s=5.0, fix=30.0, hop=5000.0, bw=50.0, dma=1700.0,
               rate=200.0)]

SCRATCH = {}


def _buf(dtype, shape, names, where="sbuf"):
    for n in names.split():
        SCRATCH[n] = (where, [128] + (shape if isinstance(shape, list) else [shape]), dtype)


_buf("int32", V0, "raw")
_buf("int32", 64, "sti")
_buf("int32", 8, "sgi coli")
_buf("float32", V0, "tru")
_buf("float16", V0, "hf")
_buf("float32", F + WD, "mp0 mp1 rp1 rp2 rp3 cn")
_buf("float32", 64, "so col gsc inc ns gt kd ks tx")
_buf("float32", 96, "rca rcb rcc pat")
_buf("float32", 128, "i32n wc wuz fn vcn")
_buf("float32", 192, "kf")
_buf("float32", 256, "cl yc zb")
_buf("float16", 512, "vc dv")
_buf("float16", F + V0 + 136, "w16 w17 l1 l2 l3")
_buf("float32", 512, "za zc")
_buf("uint16", 192, "ltd")
_buf("uint16", 512, "dl")
_buf("float32", 216, "wz")
_buf("bfloat16", 36, "j36")
_buf("bfloat16", 384, "wx")
_buf("bfloat16", 64, "jm moff one sg7 ng cb xh")
_buf("bfloat16", 128, "jd bd ib ibn ik ihp ihn i2p i2n wux wdt wtm wng wdf dge wav wst wtt ce")
_buf("bfloat16", 192, "cf")
_buf("bfloat16", 256, "j64 j256 ra ras tri1 xb0 xb1 xb2 xb3")
_buf("bfloat16", 320, "tri2 eq eq2")
_buf("bfloat16", 512, "zr xa xc")
_buf("bfloat16", 1024, "xo")
_buf("bfloat16", [4, 128], "selb lc")
_buf("float16", 64, "rc1 gsm rct sg1 sg2 zz sw tw csg dd")
_buf("float16", [35, 4], "r4a r4c")
_buf("float16", [71, 2], "r2b")
_buf("uint16", 64, "sa sc sb0 sb1 sb2 sb3 no")
_buf("float32", 512, "ps0 ps1 ps2 ps3 ps4 ps5 ps6 ps7", "psum")

SEMAPHORES = ["cv", "ca", "cp", "cg"] + [p + str(i) for p in "mt" for i in range(28)] + ["d%d" % i for i in range(48)]
BYTES = {"float32": 4, "int32": 4, "float16": 2, "bfloat16": 2, "uint16": 2}
IO = ("recs", "st0", "cx0", "sg", "yp", "ys", "yx")


def A(name, c0, c1, st=1, p0=0, p1=128, ps=1):
    return ("ap", name, (p0, p1, ps), (c0, c1, st))


def A3(name, i, j, p1=128):
    return ("ap", name, (0, p1, 1), i, j)


def C(k):
    return A("col", k, k + 1)


def IND(win, off):
    return ("ind", win, off)


def ncols(a):
    if a[0] == "ind":
        return 16 * ncols(a[2])
    n = 1
    for d in a[3:]:
        n *= len(range(*d)) if isinstance(d, tuple) else 1
    return n


def span(a):
    ends = [(d[0], range(*d)[-1]) if isinstance(d, tuple) else (d, d) for d in a[3:]]
    if len(ends) == 1:
        return ends[0][0], ends[0][1] + 1
    w = SCRATCH[a[1]][1][2]
    return ends[0][0] * w + ends[1][0], ends[0][1] * w + ends[1][1] + 1


def cells(a):
    axes = [range(*d) if isinstance(d, tuple) else [d] for d in a[3:]]
    return set(axes[0]) if len(axes) == 1 else set((i, j) for i in axes[0] for j in axes[1])


def isz(a):
    if a[0] == "ind":
        a = a[1]
    return (2 if a[1] in ("cx0", "yx") else 4) if a[1] in IO else BYTES[SCRATCH[a[1]][2]]


def inps(a):
    return a[0] == "ap" and a[1].startswith("ps")


def cost(op, m):
    k, a = op["k"], op["a"]
    if k == "mm":
        t = 0.0
        for (out, l, r, st, sp) in a:
            t += max(min(64, ncols(l)), ncols(r)) * (4 if isz(l) == 4 else 1) * m["pe"] + 5
        return t + m["fix"]
    if k in ("iota", "sel"):
        return 150 + 2 * ncols(a[0]) * m["cyc"]
    if k == "dma":
        return 60.0
    if k in ("send", "fwd"):
        return 700.0 if k == "send" else 0.0
    out, i0 = a[0], (a[1] if k != "ms" else a[0])
    n = ncols(out)
    if out[0] == "ind":
        return 50 + n * m["s"] * m["cyc"]
    if i0[0] == "ind":
        return 60 + n * m["g"] * m["cyc"]
    f = 1.0
    if k == "tt":
        f = 1.0 if (inps(a[1]) or inps(a[2])) else 2.0
    elif k in ("ts", "cp", "ms") and isz(out) == 2 and isz(i0) == 2:
        f = 0.5
    return max(64, n * f) * m["cyc"] + m["fix"]


def latency(op, m):
    if op["k"] == "dma":
        return m["dma"] + op["load"] / m["rate"]
    if op["k"] == "send":
        return m["hop"] * (1.0 if op["a"][3] else 0.55) + op["load"] / m["bw"]
    if op["k"] == "fwd":
        return m["hop"] + op["load"] / m["bw"] + 900.0 * op["a"][3]
    return 0.0


def regions(op):
    k, a = op["k"], op["a"]
    rd, wr = [], []

    def add(x, lst):
        if isinstance(x, tuple) and len(x) > 0 and x[0] == "ind":
            lst.append(x[1])
            rd.append(x[2])
        elif isinstance(x, tuple) and len(x) > 0 and x[0] == "ap":
            lst.append(x)
    if k == "mm":
        for (out, l, r, st, sp) in a:
            add(out, wr)
            add(l, rd)
            add(r, rd)
    elif k in ("send", "fwd"):
        for (d, s, w) in a[0]:
            add(d, wr)
            if k == "send":
                add(s, rd)
    else:
        add(a[0], wr)
        for x in a[1:]:
            add(x, rd)
    return rd, wr


def build():
    ops = []

    def put(q, k, *a):
        ops.append({"q": q, "k": k, "a": a, "load": 0, "after": []})
    ts = lambda out, i, s1, s2, o0, o1=None: put("v", "ts", out, i, s1, s2, o0, o1)
    tt = lambda out, i, j, o: put("v", "tt", out, i, j, o)
    cp = lambda out, i: put("v", "cp", out, i)
    scan = lambda out, d0, d1, init, o0, o1: put("v", "scan", out, d0, d1, init, o0, o1)
    act = lambda out, i, f, bias, scale: put("a", "act", out, i, f, bias, scale)
    lin = lambda out, i, scale, bias=0.0: act(out, i, AF.Identity, bias, scale)
    mm = lambda lst: put("p", "mm", *lst)
    full = lambda n: A(n, 0, SCRATCH[n][1][1])
    half = lambda n, h, c=None: A(n, 0, c or SCRATCH[n][1][1], 1, 64 * h, 64 * h + 64)
    zero = lambda n: A("zr", 0, n)
    win = lambda n, w=W0: A(n, F, F + w)
    MP = [win("mp0")] + [win("mp1")] * 3
    HOME = [win("mp0"), win("rp1"), win("rp2"), win("rp3")]
    CN, IB = win("cn"), full("ib")
    load, nsend = [0], [0]

    def dma(q, out, i):
        put(q, "dma", out, i)
        load[0] += len(range(*out[2])) * ncols(out) * isz(out)
        ops[-1]["load"] = load[0]

    def send(parts, step, via=None, wait=0):
        put("g", "send", parts, nsend[0], step % 4, step % 4 != 2 if via is None else via)
        ops[-1]["load"] = wait + sum(128 * ncols(d) * isz(d) for (d, s, w) in parts)
        nsend[0] += 1
        return len(ops) - 1

    def onward(first, places, step, nth):
        put("r", "fwd", [(d, p[0], p[2]) for d, p in zip(places, ops[first]["a"][0])], nsend[0], step % 4, nth)
        ops[-1]["load"], ops[-1]["after"] = ops[first]["load"], [first]
        nsend[0] += 1
    two = lambda d, s, ways: [(piece(d, h, 2), piece(s, h, 2), ways[h]) for h in range(2)]

    np_ = OPT["pieces"]
    hv = V0 // np_
    dma("s", A("sgi", 0, 1), A("sg", 0, 1))
    cuts = OPT["cuts"]
    for k in range(len(cuts) - 1):
        dma("as"[k % 2], A("raw", hv * cuts[k], hv * cuts[k + 1]), A("recs", hv * cuts[k], hv * cuts[k + 1]))
    dma("a", A("xb0", 0, NB), A("cx0", 0, NB))
    dma("s", full("sti"), A("st0", 0, 64))
    load[0] = 0
    dma("s", A("xc", 0, NM), A("cx0", NB, NB + NM))
    dma("s", A("xa", 64, 64 + NM), A("cx0", NB + NM, 1024))
    for i, o in enumerate(ops):
        o["after"] = [j for j in range(i) if ops[j]["q"] == o["q"]][-1:]
    nload = len(ops) - 2
    for o in ops[-2:]:
        o["after"] = [2]
    put("v", "ms", full("zr"), 0.0)
    put("g", "iota", A("coli", 0, 1), [[0, 1]], 0, 1)
    put("g", "iota", full("jd"), [[1, 8], [0, 16]], 0, 0)
    put("g", "iota", full("jm"), [[0, 4], [1, 16]], 0, 0)
    put("g", "sel", IB, zero(128), [[-1, 128]], OP.not_equal, 1.0, 0, 1)
    put("g", "iota", full("j36"), [[0, 4], [1, 9]], 0, 0)
    put("g", "iota", full("j64"), [[1, 4], [0, 64]], 0, 0)
    put("g", "iota", full("j256"), [[0, 4], [1, 64]], 0, 0)
    ci = lambda k: A("coli", k, k + 1)
    ts(ci(1), ci(0), 15, None, OP.bitwise_and)
    ts(ci(2), ci(0), 4, None, OP.arith_shift_right)
    ts(ci(3), ci(0), 63, None, OP.bitwise_and)
    ts(ci(4), ci(0), 4, 3, OP.arith_shift_right, OP.bitwise_and)
    cp(A("col", 0, 5), A("coli", 0, 5))
    SG, R12, R13, R14, R15, ST = C(5), C(6), C(7), C(8), C(9), C(10)
    cp(SG, A("sgi", 0, 1))
    ts(A("col", 6, 10), A("jm", 12, 16), C(1), None, OP.is_equal)
    ts(ST, C(1), 12.0, None, OP.is_lt)
    names = "xs xb xi c240 cm240 q25 lt14 rt rd rc ia r14e r12h cuz cux tneg tpos dgc cec spare d0 ck keep g4 h4".split()
    K = {n: C(11 + i) for i, n in enumerate(names)}
    lin(K["xs"], ST, 1.0 / 496)
    lin(K["xb"], ST, 122.742, 1.0)
    lin(K["xi"], ST, E - 1, 1.0)
    lin(K["c240"], ST, E)
    lin(K["cm240"], ST, -E)
    lin(K["q25"], ST, -0.25)
    lin(K["rt"], R12, 1.0, R13)
    lin(K["lt14"], ST, 1.0, K["rt"])
    lin(K["rd"], R12, -1.0, R13)
    lin(K["rc"], R14, 1.0, R15)
    lin(K["ia"], R14, -1.0, R15)
    lin(K["r14e"], R14, E)
    lin(K["r12h"], R12, 0.5)
    lin(K["cec"], K["rt"], 4096.0, -8192.0)
    lin(K["spare"], C(1), 1.0, float(W0))
    lin(K["d0"], C(1), 0.0, 2.0 * (V0 - 1))
    lin(K["g4"], C(2), 1.0, -4.0)
    ts(K["h4"], C(2), C(4), None, OP.subtract)
    ts(A("col", 40, 44), A("jm", 0, 4), K["h4"], None, OP.add)
    for (n, s) in (("ia", 0.5), ("rc", 0.5)):
        lin(C(44 if n == "ia" else 45), K[n], s)
    ts(full("bd"), full("jd"), C(2), None, OP.is_equal)
    ts(full("moff"), full("jm"), C(1), 4096.0, OP.not_equal, OP.mult)
    ts(full("ras"), full("j64"), C(4), 2048.0, OP.is_equal, OP.mult)
    ts(full("ra"), full("j64"), C(4), 1.0 / 16, OP.is_equal, OP.mult)
    for h in range(2):
        ts(A3("selb", (0, 4, 1), (64 * h, 64 * h + 64, 1)), full("j64"), K["g4"] if h else C(2), -1.0 / 16,
           OP.is_equal, OP.mult)
    for k in range(4):
        ts(A3("lc", k, (0, 128, 1)), full("jd"), C(40 + k), 32768.0, OP.is_equal, OP.mult)
    ts(full("tri1"), full("j256"), C(3), 0.5, OP.is_le, OP.mult)
    ts(A("tri2", 0, 256), full("tri1"), -57343.0, 28672.0, OP.mult, OP.add)
    put("v", "ms", A("tri2", 256, 320), 0.0)
    put("v", "ms", full("one"), 1.0)
    put("v", "ms", full("pat"), -1.0)
    put("v", "ms", A("pat", 0, 96, 3), 0.0)
    put("v", "ms", full("cl"), 0.0)
    put("v", "ms", A("cl", 128, 256, 32), 3000.0)
    ts(A("cl", 0, 128, 16), A("jd", 0, 128, 16), 16.0, K["spare"], OP.mult, OP.add)
    for n in ("r4a", "r4c", "r2b"):
        lin(A3(n, (0, SCRATCH[n][1][1], 1), (0, SCRATCH[n][1][2], 1)), zero(SCRATCH[n][1][1] * SCRATCH[n][1][2]), 1.0)
    for n in ("wz", "wx"):
        put("g", "iota", full(n), [[0, SCRATCH[n][1][1]]], 0, 0)
    bd8, BD = A("bd", 0, 128, 16), full("bd")
    lin(K["tpos"], R13, 1.0 / 4096)
    lin(K["tneg"], R12, -1.0 / 4096)

    def weights(v, sign):
        lin(C(48 + 2 * v), sign, -1.0, K["r14e"])
        lin(C(49 + 2 * v), sign, E, K["r12h"])
        lin(A("wz", 54 * v + 4, 54 * v + 51, 6), bd8, C(48 + 2 * v))
        lin(A("wx", 96 * v + 1, 96 * v + 48, 6), bd8, C(49 + 2 * v))
    ts(A("wz", 3, 216, 6), full("j36"), C(2), K["tpos"], OP.is_equal, OP.mult)
    ts(A("wz", 5, 216, 6), full("j36"), C(2), K["tneg"], OP.is_equal, OP.mult)
    weights(0, SG)
    ts(full("wst"), IB, K["lt14"], None, OP.mult)
    ts(A("wst", 14, 128, 16), bd8, SG, None, OP.mult)
    for n, i, c, f in (("wuz", BD, C(48), -1.0), ("wux", BD, C(49), -1.0), ("wdt", BD, K["rd"], 0.5),
                       ("wtm", BD, K["rt"], 0.5), ("wc", BD, K["rc"], -1.0), ("dge", IB, K["rd"], 2048.0),
                       ("wav", IB, ST, 0.5), ("wtt", IB, K["rt"], 1.0)):
        ts(full(n), i, c, f, OP.mult, OP.mult)
    for n, i, f in (("wng", BD, 8192.0), ("wdf", BD, 2048.0), ("i32n", IB, -1.0), ("ibn", IB, -1.0), ("ik", IB, 16384.0),
                    ("ihp", IB, 0.5), ("ihn", IB, -0.5), ("i2p", IB, 2048.0), ("i2n", IB, -2048.0)):
        lin(full(n), i, f)
    lin(A("ce", 0, 64), full("moff"), 1.0, 2048.0)
    lin(A("ce", 64, 128), zero(64), 1.0, K["cec"])
    lin(A("cf", 0, 64), full("moff"), 1.0, 2048.0)
    lin(A("cf", 64, 192, 2), full("moff"), 1.0, 2048.0)
    lin(A("cf", 65, 192, 2), full("moff"), 1.0, 4096.0)
    lin(full("cb"), zero(64), 1.0, K["c240"])
    mm([(A("ps3", 0, 8), full("wst"), A("cb", 0, 8), True, True)])
    lin(C(58), R14, -1.0)
    lin(K["ck"], A("ps3", 0, 1), C(58))
    lin(A("mp0", 0, F), zero(F), 1.0, SG)
    lin(A("mp0", F + V0, F + W0), zero(W0 - V0), 1.0, K["c240"])
    put("v", "ms", full("ltd"), 0)
    for k in range(np_):
        c0, c1 = hv * k, hv * k + hv
        o = A("ps%d" % (4 + k % 4), hv * (k // 4), hv * (k // 4) + hv)
        cp(A("hf", c0, c1), A("raw", c0, c1))
        mm([(o, full("wst"), A("hf", c0, c1), True, True)])
        lin(A("mp0", F + c0, F + c1), o, 1.0, K["c240"])
    for k in range(4):
        if OPT["cn"] == "v":
            cp(A("cn", F + 332 * k, F + 332 * k + 332), A("raw", 332 * k, 332 * k + 332))
        else:
            put("g", "sel", A("cn", F + 332 * k, F + 332 * k + 332), A("raw", 332 * k, 332 * k + 332), [[0, 332]], OP.is_ge,
                0.0, 0, 0)
    lin(A("cn", F + V0, F + W0), zero(W0 - V0), 1.0)
    cp(A("sb0", 0, 16), A("sti", 0, 16))
    cp(A("sc", 0, 24), A("sti", 16, 40))
    cp(A("sa", 4 + 4, 32), A("sti", 40, 64))
    for (n, i, j) in (("xb0", 0, NB), ("xc", 0, NM), ("xa", 64, 64 + NM)):
        lin(A(n, i, j), A(n, i, j), 1.0, K["xi"])

    P3 = lambda k: A("ps3", 64 * k, 64 * k + 64)

    def step(c, w, wk, X, S, outs, side=None):
        n = ncols(X)
        kk = 2 if n <= 256 else 4
        aa, mp, m = 16 // kk, n // kk, n // 16
        bank, z, rc, r = "ps" + str("acb".index(c)), "z" + c, "rc" + c, "r%d%s" % (kk, c)
        x0 = X[3][0]
        xk = lambda k: A(X[1], x0 + k, x0 + n, kk)
        if side:
            rec, sgn, res = side
            lin(full(rec), IND(w, A(S[1], S[3][0], S[3][0] + 4)), 1.0)
            mm([(P3(0), full("wdt"), full(rec), True, True), (P3(1), full("wtm"), full(rec), True, True),
                (P3(2), full("wux"), A(X[1], x0, x0 + 64), True, False)])
        at = lambda k: 48 * (k // 2) + 3 * (k % 2) + 1
        mm([(A(bank, 0, 24 * kk, 1, 0, mp), xk(0), A("wx", 96 * wk, 96 * wk + 24 * kk), True, False)]
           + [(A(bank, at(k), at(k) + 43, 6, 0, mp), xk(k), A("wx", 96 * wk + 1, 96 * wk + 48, 6), False, False)
              for k in range(1, kk)])
        cut = [0, n] if n <= 256 or not OPT["gs"] else [0, n // 64 * 32, n]
        for (i, j) in zip(cut, cut[1:]):
            tt(A(z, i, j), IND(w, A(S[1], S[3][0] + i // 16, S[3][0] + j // 16)), A(X[1], x0 + i, x0 + j), OP.mult)
        if side:
            mm([(P3(2), full("wuz"), A(z, 0, 64), False, True)])
            act(full(sgn), P3(2), AF.Sign, 0.0, 1.0)
        zm = [(A(bank, 48 * (k // 2), 48 * (k // 2) + 48, 1, 0, mp), A(z, k, n, kk),
               A("wz", 54 * wk + 3 - 3 * (k % 2), 54 * wk + 51 - 3 * (k % 2)), False, k == kk - 1) for k in range(kk)]
        for k in range(0, kk, OPT["zs"]):
            mm(zm[k:k + OPT["zs"]])
        cut = [0, n] if n <= 256 or not OPT["xs"] else [0, n // 64 * 32, n]
        for (i, j) in zip(cut, cut[1:]):
            lin(A(X[1], x0 + i, x0 + j), A(z, i, j), K["xs"], K["xb"])
        if side:
            tt(full("zz"), P3(0), full(sgn), OP.mult)
            if res in OPT["sum_a"]:
                mm([(P3(5), full("wtm"), full(rec), True, False), (P3(5), IB, full("zz"), False, True)])
                lin(full(res), P3(5), 1.0)
            else:
                tt(full(res), P3(1), full("zz"), OP.add)
        scan(A(rc, 0, 24 * kk, 1, 0, mp), A("pat", 0, 24 * kk, 1, 0, mp), A(bank, 0, 24 * kk, 1, 0, mp), 0.0,
             OP.mult, OP.max)
        for h in range(kk // 2):
            act(A3(r, (aa - 1, aa - 1 + 8 * aa, aa), (2 * h, 2 * h + 2, 1), mp), A(rc, 48 * h + 2, 48 * h + 48, 3, 0, mp),
                AF.Abs, 0.0, 4096.0)
        mm([(A(bank, 128, 128 + m), A3(r, (aa - 1 - a, aa - 1 - a + 128 // kk, 1), (0, kk, 1), mp),
             A("ib", a, mp, aa, 0, mp), a == 0, a == aa - 1) for a in range(aa)])
        for (out, i, j) in outs:
            (cp if isz(out) == 2 or OPT["so"] == "v" else lambda o, p: lin(o, p, 1.0))(out, A(bank, 128 + i, 128 + j))

    def home(c, v):
        lo, hi = {"a": (64 if v == 0 else 0, 448 + (64 if v == 3 else 0)), "c": (0, NM + (64 if v > 1 else 0))}[c]
        o = 4 if c == "a" else 0
        S = A("s" + c, o + lo // 16, o + hi // 16)
        for s in range(3):
            outs = [(S, 0, (hi - lo) // 16)]
            if v == 3 and s == 2:
                outs = {"a": [(A("so", 0, 4), 0, 4), (A("so", 40, 64), 4, 28), (A("so", 8, 12), 28, 32)],
                        "c": [(A("so", 16, 40), 0, 24), (A("so", 4, 8), 24, 28)]}[c]
            step(c, HOME[v], v, A("x" + c, lo, hi), S, outs)

    D, DF = A("ps4", 0, 256), A("ps4", 256, 320)
    Q, PG, SD = A("ps5", 0, 64), A("ps5", 64, 128), A("ps5", 128, 192)

    def pairs(w, start):
        lst = [(DF, full("ibn"), full(w), True, False)] if start else []
        if start and OPT["eq_a"]:
            lst = [(D, full("ik"), full("tri1"), True, False)]
        lst += [(half("ps4", h, 256), half(w, h), half("ra", h), False, False) for h in range(2)]
        return lst + [(A("ps4", 64 * k, 64 * k + 64), A3("selb", k, (0, 128, 1)), full(w), False, k == 3) for k in range(4)]

    def counts(out, e, stop):
        return [(out, A3("lc", k, (0, 128, 1)), A(e, 64 * k, 64 * k + 64), False, stop and k == 3) for k in range(4)]

    LT = lambda v, i, j: A("ltd", 16 * v + i, 16 * v + j)
    VC = lambda v, i, j: A("vc", 128 * v + i, 128 * v + j)
    L = lambda v, s: A("sb%d" % v, 16 * s, 16 * s + 4)

    def stage1(v):
        mm(pairs("sw", True))
        if OPT["eq_a"]:
            act(A("eq2", 0, 256), D, AF.Abs, 0.0, 1.0)
            act(A("eq", 0, 256), A("eq2", 0, 256), AF.Relu, 1.0, -1.0)
        else:
            tt(A("eq", 0, 256), D, full("tri1"), OP.is_equal)
        mm([(SD, IB, full("moff"), True, False), (SD, IB, full("sw"), False, False)] + counts(SD, "eq", True))
        act(full("ng"), SD, AF.Sign, -2000.0, 1.0)
        if not OPT["ngv"]:
            mm([(DF, full("ibn"), full("sw"), True, False)]
               + [(half("ps4", h, 256), half("ng", h), half("ras", h), False, False) for h in range(2)])
        scan(full("ks"), A("cl", 64, 128), SD, 0.0, OP.max, OP.min)
        cp(LT(v, 8, 12), A("ks", 15, 64, 16))
        lin(full("gsc"), IND(CN, L(v, 2)), 1.0)
        act(full("sg7"), full("gsc"), AF.Sign, -6.5, 1.0)
        mm([(PG, full("i32n"), full("gsc"), True, False), (PG, full("ik"), full("sg7"), False, True)])

    def train(v):
        xt = A("xb%d" % v, 0, 64)
        vd, ee = A("ps6", 0, 64), A("ps6", 64, 128)
        vt, ve, vo = A("ps7", 0, 64), A("ps7", 64, 192, 2), A("ps7", 65, 192, 2)
        lin(full("inc"), full("sg2"), C(44), C(45))
        tt(IND(win("cn", WD), LT(v, 8, 12)), full("gsc"), full("inc"), OP.add)
        if OPT["ngv"]:
            mm([(P3(5), full("wdf"), full("ng"), True, False), (P3(5), full("wtm"), full("gsm"), False, True)])
            tt(full("tx"), P3(5), full("zz"), OP.add)
            mm([(DF, full("ibn"), full("sw"), True, False), (DF, IB, full("tw"), False, False)]
               + [(A("ps4", 64 * k, 64 * k + 64), A3("selb", k, (0, 128, 1)), full("tw"), False, False) for k in range(4)])
            mm([(half("ps4", h, 256), half("tx", h), half("ra", h), False, True) for h in range(2)])
        else:
            mm([(DF, IB, full("tw"), False, False)] + pairs("tw", False))
        tt(full("ns"), PG, full("inc"), OP.mult)
        tt(full("eq2"), A("ps4", 0, 320), full("tri2"), OP.is_equal)
        mm([(Q, full("wng"), full("ng"), True, False), (Q, full("wc"), full("ns"), False, False)])
        mm([(A("ps6", 0, 128), IB, full("ce"), True, False), (ee, full("dge"), full("sg2"), False, False)])
        mm([(A("ps7", 0, 192), IB, full("cf"), True, False), (vt, IB, full("tw"), False, False),
            (ve, full("ibn"), full("tw"), False, False)])
        lin(full("gt"), IND(CN, L(v, 3)), 1.0)
        lin(full("rct"), IND(MP[v], L(v, 3)), 1.0)
        mm([(Q, full("wdf"), A("eq2", 256, 320), False, False)] + counts(Q, "eq2", False))
        mm([(Q, full("wc"), full("gt"), False, True)])
        act(full("csg"), Q, AF.Sign, 98291.5, -1.0)
        mm([(P3(3), full("wav"), xt, True, False), (P3(3), full("wav"), full("rct"), False, True)])
        lin(full("cb"), P3(3), 1.0, K["q25"])
        mm([(P3(4), full("wtt"), full("rct"), True, False), (P3(4), full("wst"), full("cb"), False, True)])
        lin(VC(v, 0, 64), P3(4), 1.0, K["ck"])
        scan(full("dd"), full("csg"), full("one"), K["d0"] if v == 0 else K["keep"], OP.add, OP.add)
        mm([(vd, full("i2n"), full("csg"), False, False), (ee, full("i2p"), full("csg"), False, False)])
        mm([(vd, full("ihp"), full("dd"), False, False), (ee, full("ihp"), full("dd"), False, True)])
        scan(full("kd"), A("cl", 0, 64), vd, 0.0, OP.max, OP.min)
        cp(LT(v, 4, 8), A("kd", 15, 64, 16))
        tt(VC(v, 64, 128), ee, full("gsm"), OP.max)
        cp(IND(win("mp1", WD), LT(v, 4, 12)), VC(v, 0, 128))
        mm([(vt, full("i2n"), full("csg"), False, False), (vo, full("i2n"), full("csg"), False, False),
            (vo, full("ihn"), full("dd"), False, True)])
        scan(full("kf"), A("cl", 64, 256), A("ps7", 0, 192), 0.0, OP.max, OP.min)
        new = (A("sa", 4, 8), A("no", 8, 12), A("no", 16, 20), A("ks", 0, 4))[v]
        if v < 3:
            ts(new, A("kf", 95, 192, 32), -1.0, 2048.0, OP.mult, OP.add)
            lin(K["keep"], A("dd", 63, 64), 1.0)
        else:
            lin(new, A("kf", 95, 192, 32), -1.0, 2048.0)
        cp(LT(v, 0, 4), A("kf", 15, 64, 16))
        lin(A("fn", 0, 64), full("gt"), 0.5 + 2.0 ** -15, MAGIC)
        lin(A("fn", 64, 128), full("gt"), 0.5 - 2.0 ** -15, MAGIC)
        lin(full("vcn"), full("fn"), 1.0, -MAGIC)
        cp(IND(win("cn", WD), LT(v, 0, 8)), full("vcn"))
        if v == 0:
            lin(A("xa", 0, 64), xt, 1.0)
        else:
            send([((A("xc", NM, NM + 64), A("xa", 448, 512), full("xh"))[v - 1], xt, 0)], -v)
        if v < 3:
            src = lambda w: [(DV(v, w), VC(v, 0, 128), 0), (DL(v, w), LT(v, 4, 132), 1)]
            first = send(src(v + 1), -(v + 1))
        if v > 0:
            send([((A("sc", 24, 28), A("sa", 32, 36), A("so", 12, 16))[v - 1], new, 1)], -v)
        if v == 1 and not OPT["snap3"]:
            send(src(3), -3)
        for w in ((1,), (2,) if OPT["snap3"] else (2, 3), (3,), ())[v]:
            cp(IND(win("rp%d" % w, WD), A("dl", DL(v, w)[3][0], DL(v, w)[3][0] + 8)), DV(v, w))

    slot = lambda v, w: 128 * [(0, 1), (1, 2), (1, 3), (2, 3)].index((v, w))
    DV = lambda v, w: A("dv", slot(v, w), slot(v, w) + 128)
    DL = lambda v, w: A("dl", slot(v, w), slot(v, w) + 128)

    def cast(q, out, i):
        for k in range(2):
            if q == "g":
                put("g", "sel", piece(out, k, 2), piece(i, k, 2), [[0, ncols(out) // 2]], OP.is_ge, 0.0, 0, 0)
            else:
                lin(piece(out, k, 2), piece(i, k, 2), 1.0)

    def base(src, snap, n, visits):
        n //= 2
        first = []
        for v in visits:
            for h in range(2):
                there = A("l%d" % v, n * h, n * h + n)
                if v == visits[0]:
                    cast(OPT["snap"], A(snap, n * h, n * h + n), A(src, n * h, n * h + n))
                    ways = [0, 1] if v == 1 and h == 0 and OPT["four"] else [2, 3]
                    first.append(send(two(there, A(snap, n * h, n * h + n), ways), -v, True,
                                      256 * n * h * (v > 1 or not OPT["four"])))
                else:
                    onward(first[h], [piece(there, k, 2) for k in range(2)], -v, 6 + h)
                cast(OPT["wide"], A("rp%d" % v, n * h, n * h + n), there)
            lin(A("rp%d" % v, 2 * n, F + W0), zero(F + W0 - 2 * n), 1.0, K["c240"])
            weights(v, A("rp%d" % v, 0, 1))

    base("mp0", "w16", F + V0, [1])
    load[0] = 0
    dma("s", A("mp1", 0, F + W0), A("mp0", 0, F + W0))
    for v in range(4):
        n = NB - 64 * v
        for s in range(3):
            S = lambda s: A("sb%d" % v, 16 * s, 16 * s + n // 16)
            step("b", MP[v], 0, A("xb%d" % v, 0, n), S(s), [(S(s + 1), 0, n // 16)],
                 (None, ("rc1", "sg1", "sw"), ("gsm", "sg2", "tw"))[s])
            if s == 1:
                stage1(v)
        if v < 3:
            send(two(A("xb%d" % (v + 1), 0, n - 64), A("xb%d" % v, 64, n), [0, 1]), 1)
            last = send([(A("sb%d" % (v + 1), 0, n // 16 - 4), A("sb%d" % v, 52, 48 + n // 16), 1)], 1)
        for c in "ca":
            home(c, v)
        train(v)
        if v == 0:
            base("mp1", "w17", F + V0 + 64 + 8, [2] if OPT["snap3"] else [2, 3])
        if v == 1 and OPT["snap3"]:
            base("mp1", "w16", F + V0 + 128 + 8, [3])
        if v == 2:
            last = max(i for i, o in enumerate(ops) if o["k"] == "send")
            for k in range(4):
                lin(A("tru", 332 * k, 332 * k + 332), A("mp0", F + 332 * k, F + 332 * k + 332), 1.0, K["cm240"])
            load[0] = 0
            for g in range(8):
                dma("s", A("yp", 0, V0, 1, 16 * g, 16 * g + 12), A("tru", 0, V0, 1, 16 * g, 16 * g + 12))
                ops[-1]["after"] = [last]
    load[0] = 0
    lin(full("yc"), A("mp1", F + V0, F + W0), 1.0, K["cm240"])
    for r in (12, 13):
        dma("s", A("yp", 0, V0, 1, r, 128, 16), A("mp1", F, F + V0, 1, r, 128, 16))
    for g in range(8):
        dma(OPT["endq"][g % 2], A("yp", V0, W0, 1, 16 * g, 16 * g + 14), A("yc", 0, 256, 1, 16 * g, 16 * g + 14))
    for r in (14, 15):
        dma("s", A("yp", 0, W0, 1, r, 128, 16), A("cn", F, F + W0, 1, r, 128, 16))
    load[0] = 0
    for (o, n, i, j) in ((192, "xh", 0, 64), (256, "xc", 0, NM), (64, "xc", NM, NM + 64), (0, "xa", 0, 64),
                         (640, "xa", 64, 448), (128, "xa", 448, 512)):
        if OPT["xo"] == "v":
            ts(A("xo", o, o + j - i), A(n, i, j), ST, K["cm240"], OP.mult, OP.add)
        else:
            lin(A("xo", o, o + j - i), A(n, i, j), ST, K["cm240"])
    for (i, j) in ((192, 640), (640, 1024), (0, 192)):
        load[0] = 0
        dma("s", A("yx", i, j), A("xo", i, j))
    load[0] = 0
    dma("s", A("ys", 0, 64), full("so"))

    hist = {}
    for i, op in enumerate(ops):
        rd, wr = regions(op)
        dep, land = set(op["after"]), set()
        for lst, w in ((rd, False), (wr, True)):
            for r in lst:
                if r[1] in IO:
                    continue
                lo, hi = span(r)
                for (j, r2, w2, lo2, hi2) in hist.get(r[1], []):
                    if inps(r):
                        if ops[j]["q"] != op["q"] or op["q"] == "p":
                            dep.add(j)
                    elif (w or w2) and lo < hi2 and lo2 < hi and r[2][0] < r2[2][1] and r2[2][0] < r[2][1]:
                        if op["q"] == ops[j]["q"] == "a" and op["k"] == ops[j]["k"] == "act" and not cells(r) & cells(r2):
                            continue
                        dep.add(j)
                        if w2:
                            land.add(j)
        for lst, w in ((rd, False), (wr, True)):
            for r in lst:
                if r[1] not in IO:
                    hist.setdefault(r[1], []).append((i, r, w) + span(r))
        op["dep"] = sorted(dep)
        op["left"] = set(j for j in dep if ops[j]["k"] == "send" and j not in land)
        op["free"] = set(j for j in dep if ops[j]["q"] == op["q"] == "p" or i < nload)
    return ops


def gap(ops, j, i, m):
    a, b = ops[j], ops[i]
    if b["k"] == "fwd" or j in b["free"]:
        return 0.0
    if j in b["left"]:
        return 2000 + a["load"] / 120.0
    if a["k"] in ("dma", "send", "fwd"):
        return latency(a, m) + m["h"]
    if a["q"] == b["q"]:
        return 0.0 if j in b["free"] else m["hs"]
    return m["h"]


def schedule(ops, ms, iters, seed):
    n = len(ops)
    near = []
    for i in range(n):
        far = set(k for j in ops[i]["dep"] for k in ops[j]["dep"] if ops[k]["k"] not in ("dma", "send", "fwd"))
        near.append([j for j in ops[i]["dep"] if j not in far])
    tabs = []
    for m in ms:
        c = [cost(o, m) for o in ops]
        tabs.append((c, [latency(o, m) for o in ops], [[(j, c[j] + gap(ops, j, i, m)) for j in near[i]] for i in range(n)]))
    c, lat, pre = tabs[0]
    suc = [[] for i in range(n)]
    for i in range(n):
        for (j, d) in pre[i]:
            suc[j].append((i, d - c[j] + c[i]))
    qs = [o["q"] for o in ops]
    x = [seed]

    def rnd():
        x[0] = (x[0] * 1103515245 + 12345) % 2147483648
        return x[0] / 2147483648

    def place(seq, dep, first):
        busy = {q: [] for q in "vapgsr"}
        st = [0.0] * n
        for i in seq:
            t = first[i]
            for (j, d) in dep[i]:
                if st[j] + d > t:
                    t = st[j] + d
            b = busy[qs[i]]
            k = len(b)
            while k > 0 and b[k - 1][1] > t:
                k -= 1
            while k < len(b) and t + c[i] > b[k][0]:
                if b[k][1] > t:
                    t = b[k][1]
                k += 1
            st[i] = t
            b.insert(k, (t, t + c[i]))
        return st

    def starts(key):
        st = place(sorted(range(n), key=lambda i: (key[i], i)), pre, [0.0] * n)
        back = place(sorted(range(n), key=lambda i: (-st[i] - c[i], -i)), suc, lat)
        return place(sorted(range(n), key=lambda i: (-back[i] - c[i], i)), pre, [0.0] * n)

    def value(st):
        order = sorted(range(n), key=lambda i: (st[i], i))
        total = 0.0
        for (c, lat, dep) in tabs:
            free = {q: 0.0 for q in "vapgsr"}
            st = [0.0] * n
            end = 0.0
            for i in order:
                t = free[qs[i]]
                for (j, d) in dep[i]:
                    if st[j] + d > t:
                        t = st[j] + d
                st[i] = t
                free[qs[i]] = t + c[i]
                if t + c[i] + lat[i] > end:
                    end = t + c[i] + lat[i]
            total += end
        return total
    key = [-c[i] - lat[i] for i in range(n)]
    for i in range(n - 1, -1, -1):
        for (j, d) in pre[i]:
            key[j] = min(key[j], key[i] - d)
    best = now = starts(key)
    bv = nv = value(best)
    for it in range(iters):
        lo, amp = rnd() * max(now), rnd() * 1500.0
        hi = lo + 500.0 + rnd() * 6000.0
        key = [t + rnd() * amp if lo < t < hi else t for t in now]
        for i in range(n):
            for (j, d) in pre[i]:
                if key[j] >= key[i]:
                    key[i] = key[j] + 0.001
        st = starts(key)
        val = value(st)
        if val <= nv + OPT["slack"] * (1 - it / iters) * rnd() ** 2:
            now, nv = st, val
        if val < bv:
            best, bv = st, val
    return sorted(range(n), key=lambda i: (best[i], i))


PLAN = {}


def plan():
    if not PLAN:
        PLAN["ops"] = build()
        PLAN["order"] = schedule(PLAN["ops"], MODELS, OPT["iters"], OPT["seed"])
    return PLAN["ops"], PLAN["order"]


def relays(T, topo, r):
    src = T.cores[r]
    ok = [c for c in topo.cores_of(src) if c != src and all(topo.may_write(c, d) for d in T.cores)]
    ok.sort(key=lambda c: topo.die(c) != topo.die(src))
    return ok


def bits(engines):
    return sum(1 << e for e in engines)


def piece(a, h, k):
    n = (a[3][1] - a[3][0]) // k
    return A(a[1], a[3][0] + h * n, a[3][0] + h * n + n)


def rank_program(g, core, T, topo):
    ops, order = plan()
    rank = T.rank_of(core)
    nr = len(T.cores)

    def ap(a):
        if not (isinstance(a, tuple) and len(a) > 0 and a[0] in ("ap", "ind")):
            return a
        if a[0] == "ind":
            return ap(a[1]).indirect(ap(a[2]))
        return T[a[1]][tuple(slice(d[0], d[1], d[2] if d[2] != 1 else None) if isinstance(d, tuple) else d for d in a[2:])]

    def write(parts, en, there, here):
        n = len(en) // len(parts)
        tr = []
        for h, (d, s, to) in enumerate(parts):
            rid, pid = topo.addr(to, core)
            tr.append(RemoteDMATransfer(dst_ids=[DstId(rid=rid, pnc=pid)], remote_sem=T.sem[there],
                                        dma_engine_mask=bits(en[h * n:h * n + n]), src=ap(s), dst=ap(d)))
        g.remote_dma_fused(tr, local_sem=T.sem[here])

    if rank is None:
        for r in range(nr):
            rl = relays(T, topo, r)
            if core in rl:
                me = rl.index(core)
                whole = len(topo.engines(T.cores[r], core))
                total = 0
                for i in order:
                    op = ops[i]
                    if op["k"] == "fwd" or op["k"] == "send" and op["a"][3]:
                        (parts, k, step, via) = op["a"]
                        mine = [(d, d if op["k"] == "send" else s) for (d, s, w) in parts if w == me]
                        if mine:
                            dst = T.cores[(r + step) % nr]
                            if op["k"] == "send":
                                g.wait_ge(T.sem["m%d" % k], whole // (len(parts) if OPT["all16"] else 2) * len(mine))
                            write([(d, s, dst) for (d, s) in mine], topo.engines(core, dst), "m%d" % k, "cg")
                            total += len(topo.engines(core, dst))
                g.wait_ge(T.sem.cg, total)
        return

    rl = relays(T, topo, rank)
    arrive = len(topo.engines(relays(T, topo, (rank - 1) % nr)[0], core))
    Q = {"v": g.vector, "a": g.scalar, "p": g.tensor, "g": g, "s": g.sync}
    token, gone, count, seen = {}, {}, {}, {q: {} for q in Q}
    nd = [0]

    def wait(q, tok):
        if seen[q].get(tok[0], 0) < tok[1]:
            Q[q].wait_ge(T.sem[tok[0]], tok[1])
            seen[q][tok[0]] = tok[1]

    for i in order:
        op = ops[i]
        q, k = op["q"], op["k"]
        if k == "fwd":
            s = "m%d" % op["a"][1]
            count[s] = arrive * len(set(w for (d, x, w) in op["a"][0]))
            token[i] = (s, count[s])
            continue
        e = Q[q]
        need = {}
        for j in op["dep"]:
            if j in op["free"]:
                continue
            s, val = gone[j] if j in op["left"] else token[j]
            need[s] = max(need.get(s, 0), val)
        if k in ("iota", "sel") and "cg" in count:
            need["cg"] = count["cg"]
        for s in need:
            wait(q, (s, need[s]))
        a = [ap(x) for x in op["a"]] if k != "mm" else None
        if k == "send":
            (parts, n, step, via) = op["a"]
            s, t = "m%d" % n, "t%d" % n
            to = T.cores[(rank + step) % nr]
            en = topo.engines(core, rl[0] if via else to)
            en = en[len(en) // 2 * (2 - len(parts)):] if via and not OPT["all16"] else en
            write([(d, x, rl[w] if via else to) for (d, x, w) in parts], en, s, t)
            count[t] = len(en)
            count[s] = arrive * (len(set(w for (d, x, w) in parts)) if via else 1)
            token[i], gone[i] = (s, count[s]), (t, count[t])
            continue
        if k == "dma":
            s = "d%d" % nd[0]
            nd[0] += 1
            e.dma_start(a[0], a[1]).then_inc(T.sem[s], 16)
            token[i] = (s, 16)
            count[s] = 16
            continue
        if k == "mm":
            for x in op["a"]:
                ins = e.matmul(ap(x[0]), ap(x[1]), ap(x[2]), x[3], x[4])
        elif k == "iota":
            if SCRATCH[op["a"][0][1]][2] == "int32":
                ins = e.iota(a[0], a[1], a[2], a[3])
            else:
                ins = e.iota(a[0], a[1], a[2], a[3], allow_small_or_imprecise_dtypes=True)
        elif k == "sel":
            ins = e.affine_select(*a)
        elif k == "ts":
            ins = e.tensor_scalar(*a[:5]) if a[5] is None else e.tensor_scalar(*a)
        elif k == "tt":
            ins = e.tensor_tensor(*a)
        elif k == "cp":
            ins = e.tensor_copy(*a)
        elif k == "ms":
            ins = e.memset(*a)
        elif k == "scan":
            ins = e.tensor_tensor_scan(*a)
        else:
            ins = e.activation(a[0], a[1], a[2], bias=a[3], scale=a[4])
        s = "c" + q
        count[s] = count.get(s, 0) + 1
        ins.then_inc(T.sem[s], 1)
        token[i] = (s, count[s])
    for s in count:
        wait("g", (s, count[s]))
